import numpy as np, ml_dtypes
CORES = [2,6,10,14,18,22,26,30]
N = 8
import mx_ref
BF = ml_dtypes.bfloat16
def gentries(a):
    return np.ascontiguousarray(a.reshape(8, 16, -1).transpose(0, 2, 1)).reshape(8, -1)
def gtable(e):
    e = np.asarray(e); return np.ascontiguousarray(e.reshape(8, -1, 16).transpose(0, 2, 1)).reshape(128, -1).astype(np.int32)
def gcols(t, e):
    v = np.concatenate([t.reshape(8, 16, -1, 4), np.zeros((8, 16, 1, 4), BF)], axis=2)
    return np.ascontiguousarray(np.stack([v[g][:, e[g]] for g in range(8)])).reshape(128, -1)
def cols(t, e):
    v = np.concatenate([t.reshape(128, -1, 4), np.zeros((128, 1, 4), BF)], axis=1)
    return np.ascontiguousarray(v[:, e]).reshape(128, -1)
def tile(rs):
    return np.stack(rs, axis=2).reshape(128, -1).astype(BF)
def pick(q, e):
    c = np.concatenate([q[0].reshape(128, -1, 4), np.zeros((128, 1, 4), np.uint8)], axis=1); s = np.concatenate([q[1], np.ones((16, 1), np.uint8)], axis=1)
    return (np.ascontiguousarray(c[:, e].reshape(128, -1)), np.ascontiguousarray(s[:, e]))
def join(*qs):
    return (np.concatenate([q[0] for q in qs], axis=1), np.concatenate([q[1] for q in qs], axis=1))
def put(q, e, v):
    c, s = q[0].reshape(128, -1, 4).copy(), q[1].copy(); c[:, e] = v[0].reshape(128, -1, 4); s[:, e] = v[1]
    return (c.reshape(128, -1), s)
def pk(c, s):
    return (np.ascontiguousarray(c), mx_ref.live(s))
def emit(q):
    return q[0], q[1]
def packed(v, rng):
    q = [mx_ref.quantize(np.ascontiguousarray(v[r])) for r in range(N)]
    return np.stack([a for a, b in q]), np.stack([mx_ref.plane(b, rng) for a, b in q])
def values_of_codes():
    e, c = np.zeros((128, 128, 4), np.float32), np.zeros((128, 2, 4), np.uint8)
    e[np.arange(128), np.arange(128), 0] = 1
    c[:127, :, 0] = np.arange(256).reshape(2, 128).T[:127]
    return mx_ref.matmul(mx_ref.quantize(e.reshape(128, 512).astype(BF)), (c.reshape(128, 8), np.full((16, 2), 127, np.uint8))).T.reshape(-1).astype(np.float64)
CODE_VALUE, SCALE_VALUE = values_of_codes(), 2.0 ** (np.arange(256) - 127.0)
def decode(q):
    return (CODE_VALUE[q[0]].reshape(16, 8, -1, 4) * SCALE_VALUE[q[1]][:, None, :, None] + 0.0).reshape(128, -1).astype(np.float32)
def f(rng, *shape):
    return mx_ref.flush((rng.standard_normal(shape, dtype=np.float32) * np.exp2(rng.integers(-2, 3, shape[:-1] + (1,)))).astype(BF))
def wide(rng, *shape, cols=0):
    v = rng.standard_normal(shape, dtype=np.float32) * np.exp2(rng.integers(-12, 13, shape)).astype(np.float32)
    if cols: v *= np.repeat(np.exp2(rng.integers(-cols, cols + 1, shape[:-2] + (1, shape[-1] // 4))) * (rng.random(shape[:-2] + (1, shape[-1] // 4)) > 0.0625), 4, axis=-1).astype(np.float32)
    return mx_ref.flush(v.astype(BF))
C, J, K, R = 320, 512, 128, 3
def big(v):
    v = v.astype(np.float32)
    v[np.abs(v) < np.float32(2.0 ** -16)] = 0
    return v.astype(BF)
def numbers_of(rng):
    return {"x": big(f(rng, N, 128, 4 * C)), "u": np.array(f(rng, N, 128, 512)), "v": np.array(f(rng, N, 128, 512))}
def paths(rng, n):
    a = np.zeros((8, J), np.int64)
    a[0] = rng.integers(0, C, J)
    for g in range(1, 8):
        a[g] = np.where(rng.random(J) < 0.5, a[g - 1], n[rng.integers(0, 8, J), a[g - 1]])
    return a
def lists(rng):
    n = rng.integers(0, C, (8, C))
    return {"nb": np.stack([gtable(n)] * N), "p": np.stack([gtable(paths(rng, n)) for r in range(N)])}
def weights(rng, kept=[]):
    w = (rng.random((N, 128, 512, 4), dtype=np.float32) * 2 - 1) * np.float32(2.0 ** -6)
    for i in range(2):
        k = rng.integers(0, 512, (N, 512))
        w[np.arange(N)[:, None], k >> 2, np.arange(512)[None], k & 3] = (3 + 6 * rng.random((N, 512))) * rng.choice([-1.0, 1.0], (N, 512))
    w = w.reshape(N, 128, 4, 128, 4)
    for i in kept:
        for h in range(i, 128, 16):
            w[:, :, :, h] = 0
            for b in range(4): w[:, h, b, h, b] = 32
    c, s = packed(w.reshape(N, 128, 2048).astype(BF), rng)
    return {"wc": c, "ws": s}
def setup_inputs(rng):
    return {**numbers_of(rng), **lists(rng), **weights(rng)}
def setup_inputs_ties(rng):
    d = numbers_of(rng)
    x = d["x"].reshape(N, 8, 16, C, 4)
    k = rng.integers(0, 3, (N, 8, C))
    k[:, rng.permutation(8)[:3]] = 1
    x[:, :, 0] = 0
    x[:, :, 0, :, 0] = k.astype(np.float32).astype(BF)
    z = (N, 8, 8, C, 4)
    odd = (1 + (2 * rng.integers(0, 64, z) + 1) * 2.0 ** -7) * np.exp2(-1.0 * rng.integers(8, 15, z)) * rng.choice([-1.0, 1.0], z)
    odd[:, :, 0, :, 0] = 1.96875
    o = rng.permutation(N)
    odd[o[2], :, 0, :, 1] = rng.integers(2, 32, (8, C)) * 2.0 ** -17
    x[:, :, 8:] = odd.astype(np.float32).astype(BF)
    u = d["u"].reshape(N, 128, 128, 4)
    u[:, :, ::16] = 0
    for r in range(N):
        for h in range(0, 128, 16):
            if r == o[2]: u[r, h + 8, h, 1] = 1.0
            else: u[r, h, h, 0] = 0.0 if r == o[0] else -1.0 if r == o[1] else 1.0
    l = lists(rng)
    t = np.array(gentries(l["p"][o[0]]))
    t[:, rng.permutation(J)[:J // 4]] = C - 32 + 4 * rng.integers(0, 8, (1, J // 4)) + np.arange(8)[:, None] % 2
    l["p"][o[0]] = gtable(t)
    return {"x": x.reshape(N, 128, 4 * C), "u": u.reshape(N, 128, 512), "v": d["v"], **l, **weights(rng, [0])}
def setup_inputs_near(rng):
    d = numbers_of(rng)
    x = d["x"].astype(np.float32).reshape(N, 8, 16, C, 4)
    x[:, :, :2] = 0
    x[:, :, 2:8] *= np.float32(0.25)
    x[:, :, 8:] = 0
    x[:, :, 0, :, 0] = 1
    x[:, :, 1, :, 0] = 2.0 ** -10
    s = rng.integers(0, 16, (N, 8, C))
    x[:, :, 8] = ((s[:, :, :, None] >> np.arange(4)) & 1) * np.exp2(np.arange(4) - 24.0)
    x[:, :, 10, :, 0] = (1 + 0.125 * rng.integers(0, 8, (N, 8, C))) * 2.0 ** -30
    x[:, :, 12] = x[:, :, 10]
    u = d["u"].reshape(N, 128, 128, 4)
    u[:, :, ::16] = 0
    o = rng.permutation(N) % 4
    for r in range(N):
        k = 2.0 ** -30 if o[r] in (1, 3) else 1.0
        sign = rng.permutation(8) % 2 * 2.0 - 1.0
        for g in range(8):
            h = 16 * g
            if o[r] == 3:
                u[r, h + 10, h, 0] = 1.125 * k * sign[g]
                u[r, h + 12, h, 0] = -k * sign[g]
            else:
                u[r, h, h, 0] = -k if o[r] == 2 else k
                u[r, h + 1, h, 0] = k
                u[r, h + 8, h] = 2 * k
    return {"x": x.reshape(N, 128, 4 * C).astype(BF), "u": u.reshape(N, 128, 512), "v": d["v"], **lists(rng), **weights(rng, [0, 1, 8, 9, 10, 11, 12, 13, 14, 15])}
def setup_inputs_huge(rng):
    d = numbers_of(rng)
    h = rng.permutation(8)
    x = -0.95 - 0.05 * rng.random((N, 8, 16, C, 4))
    x[:, h[4:]] = (0.75 + 0.1 * rng.random((N, 4, 16, C, 4))) * rng.choice([-1.0, 1.0], (N, 4, 1, C, 1))
    u = d["u"].reshape(N, 128, 128, 4)
    u[:, :, ::16] = 0
    for r in range(N):
        below = rng.permutation(8) < 4
        for g in range(8):
            a = 16 * int(rng.choice(h[:4] if below[g] else h[4:]))
            u[r, a:a + 16, 16 * g] = (2.0 ** 30 * (1 - 0.1 * rng.random((16, 4)))).astype(np.float32).astype(BF)
    return {"x": (2.0 ** 30 * x).astype(np.float32).reshape(N, 128, 4 * C).astype(BF), "u": u.reshape(N, 128, 512), "v": d["v"], **lists(rng), **weights(rng)}
def setup_inputs_ends(rng):
    d = numbers_of(rng)
    o = rng.permutation(N)
    sign = rng.integers(0, 2, (8, 16, 1, 4)) * 2.0 - 1.0
    x = np.zeros((N, 8, 16, C, 4))
    u = d["u"].reshape(N, 128, 128, 4)
    u[:, :, ::16] = 0
    v = np.zeros((N, 128, 512))
    n = rng.integers(0, C, (8, C))
    j = 1 + rng.permutation(C - 2)
    n[:, j[:C // 3]] = 0
    n[:, j[C // 3:2 * (C // 3)]] = C - 1
    t = np.stack([paths(rng, n) for r in range(N)])
    for i in range(N):
        r, k = o[i], 2.0 ** 30 if i % 2 == 0 else 2.0 ** -30
        if i % 2 == 0: x[r] = sign * k * (1 - 0.125 * rng.integers(0, 4, (8, 1, C, 1)))
        else: x[r] = sign * k * (1 + 0.125 * rng.integers(0, 8, (8, 1, C, 1)))
        none = 1 + rng.permutation(6)[:2]
        for g in range(8):
            if g in none: continue
            b = -1.0 if i == 0 else 1.0 if i == 2 else rng.choice([-1.0, 1.0])
            u[r, :, 16 * g] = (sign.reshape(128, 4) * (k * b)).astype(np.float32).astype(BF)
        v[r] = rng.choice([-1.0, 1.0], (128, 512)) * k
    t[o[0]] = C - 1
    t[o[1]] = 0
    t[o[2]] = np.where(np.arange(8) % 2 == 1, C - 1, 0)[:, None]
    return {"x": x.astype(np.float32).reshape(N, 128, 4 * C).astype(BF), "u": u.reshape(N, 128, 512), "v": v.astype(np.float32).astype(BF), "nb": np.stack([gtable(n)] * N), "p": np.stack([gtable(t[r]) for r in range(N)]), **weights(rng, range(16))}
def setup_inputs_spread(rng):
    d = setup_inputs(rng)
    d["x"] = big(wide(rng, N, 128, 4 * C, cols=6))
    return d
def check_inputs(d):
    b = []
    for k in ("x", "u", "v"):
        a = np.abs(d[k].astype(np.float32))
        if not (np.isfinite(a).all() and ((a == 0) | (a >= 2.0 ** -30) & (a <= 2.0 ** 30)).all()): b.append("a value of " + k)
    for k in ("nb", "p"):
        if not ((d[k] >= 0) & (d[k] < C)).all(): b.append("an entry of " + k)
    if (d["nb"] != d["nb"][:1]).any(): b.append("nb isn't the same on all ranks")
    none, least, most = [emit(mx_ref.quantize(np.full((128, 16), k, np.float32).astype(BF)))[1][0, 0] for k in (0.0, 2.0 ** -30, 2.0 ** 30)]
    tops = emit(mx_ref.quantize((np.ones((128, 1)) * np.repeat(1 + np.arange(128) * 2.0 ** -7, 4)).astype(np.float32).astype(BF)))[0] & 0x7F
    for r in range(N):
        if ((d["wc"][r] & 0x7F) == 0x7F).any(): b.append("wc: a code that is no number")
        s = mx_ref.live(d["ws"][r])
        if ((s != none) & ((s < least) | (s > most))).any(): b.append("ws: a scale out of range")
        elif not (np.sum(np.abs(decode(pk(d["wc"][r], d["ws"][r])).astype(np.float64)).reshape(128, 512, 4), axis=(0, 2)) <= 32).all(): b.append("the sizes in a column of W")
        a = np.max((d["wc"][r] & 0x7F).reshape(16, 8, 512, 4), axis=(1, 3))
        if not np.where(s == none, a == 0, (a >= np.min(tops)) & (a <= np.max(tops))).all(): b.append("wc: the codes of a block")
    return b
def hop(a, s, n):
    a = np.array(a)
    best = [n[np.argmax(s[e][n], axis=0), np.arange(C)] for e in (0, 7)]
    for h in range(4):
        for g in range(h % 2, 8, 2):
            if g == 0 or g == 7:
                m = a[1] if g == 0 else a[6]
                b = np.where(a[g] == m, best[0 if g == 0 else 1][m], m)
            else:
                low, high = a[g - 1] == a[g], a[g + 1] == a[g]
                b = np.where(low & ~high, a[g + 1], np.where(high & ~low, a[g - 1], a[g]))
            a[g] = np.where(s[g][b] > s[g][a[g]], b, a[g])
    return a
def reference(x, u, v, nb, p, wc, ws):
    qu = [mx_ref.quantize(u[r]) for r in range(N)]
    lay = [pk(wc[r], ws[r]) for r in range(N)]
    now = [x[r] for r in range(N)]
    at = [gentries(p[r]) for r in range(N)]
    for t in range(R):
        have, moved, z, first, gone = [], [], [], [], []
        for r in range(N):
            q = mx_ref.quantize(now[r])
            have.append(decode(q).astype(BF))
            s = mx_ref.matmul(qu[r], q)[::16] + np.float32(0.0)
            a = hop(at[r], s, gentries(nb[r]))
            bond = np.concatenate([a[1:], a[6:7]])
            z.append(((gcols(have[r], a).astype(np.float32) + gcols(have[r], bond).astype(np.float32)) * np.float32(0.5)).astype(BF))
            first.append(np.argsort(-np.sum(a[:-1] != a[1:], axis=0), kind="stable")[:K])
            gone.append(mx_ref.quantize(np.ascontiguousarray(cols(z[r], first[r]))))
            moved.append(a)
        for r in range(N):
            e = (r - 1) % N
            l = tile([mx_ref.matmul(pick(lay[r], np.arange(128 * b, 128 * b + 128)), gone[e]) * np.float32(0.03125) for b in range(4)])
            y = np.array(z[r]).reshape(128, J, 4)
            y[:, first[r]] = l.reshape(128, K, 4)
            at[r] = np.array(moved[r])
            at[r][:, first[r]] = moved[e][:, first[e]]
            low = np.stack([J + np.arange(C)] * 8)
            np.minimum.at(low, (np.arange(8)[:, None], at[r]), np.arange(J)[None])
            w = gcols(np.concatenate([y.reshape(128, 4 * J), have[r]], axis=1), low)
            now[r] = ((have[r].astype(np.float32) + w.astype(np.float32)) * np.float32(0.5)).astype(BF)
    y, ad = np.zeros((N, 128, C), np.float32), np.zeros((N, 8, J), np.float32)
    oc, osc = np.zeros((N, 128, 4 * C), np.uint8), np.zeros((N, 16, C), np.uint8)
    for r in range(N):
        q = mx_ref.quantize(now[r])
        y[r] = mx_ref.matmul(mx_ref.quantize(v[r]), q)
        ad[r] = at[r]
        oc[r], osc[r] = emit(q)
    return {"y": y, "ad": ad, "oc": oc, "osc": osc}

@@ -1,0 +1,544 @@
+from concourse.mybir import dt, AluOpType, AxisListType, ActivationFunctionType
+
+ROUNDS = 3
+FAR = 1e29
+BIAS = 8
+F32, BF, I32, U16, MXC, U8 = "float32", "bfloat16", "int32", "uint16", "float8_e4m3fn_x4", "uint8"
+SCRATCH, PART = {}, {}
+
+
+def _sb(dtype, **kw):
+    for k, n in kw.items():
+        SCRATCH[k] = ("sbuf", [128, n], dtype)
+        PART[k] = (k, 0, n)
+
+
+def _pack(buf, dtype, **kw):
+    at = 0
+    for k, n in kw.items():
+        PART[k] = (buf, at, n)
+        at += (n + 15) // 16 * 16
+    SCRATCH[buf] = ("sbuf", [128, at], dtype)
+
+
+_sb(BF, XT=1280, MT=1280, UT=512, VT=512, BY=512, ON=512, DT=512, HT=512, HG=512)
+_pack("CTB", BF, CT0=512, CT1=512, CT2=512, CT3=512)
+_pack("CBB", BF, CB0=512, CB7=512)
+_pack("YW", BF, YW0=960, YW1=960, YW2=960, YW3=960)
+_pack("FH", BF, FH0=320, FH1=320, FH2=320, FH3=320)
+_pack("FQ", BF, FQ0=320, FQ1=320, FQ2=320, FQ3=320)
+_pack("PF", BF, PF0=320, PF1=320, PF2=320, PF3=320)
+_pack("ZG", BF, ZG0=512, ZG1=512, ZG2=512, ZG3=512)
+_sb(MXC, uq=128, ur=1152, vq=128, dq=128, aq=128, wq=512, mq0=320, mq1=320, mq2=320, mq3=320, lq0=320, lq1=320, lq2=320)
+_sb(U8, us=128, urs=1152, vs=128, dsc=128, asc=128, wsc=512, ms0=320, ms1=320, ms2=320, ms3=320, ls0=320, ls1=320, ls2=320)
+_pack("eqc", MXC, eq0=128, eq1=128, eq2=128, eq3=128, bq0=128, bq7=128)
+_pack("esc", U8, es0=128, es1=128, es2=128, es3=128, bs0=128, bs7=128)
+_sb(F32, IOTA=4096, IO512=320, LOWC=672, PLC=512)
+_pack("KC", F32, MASK=512, KEEP=512, ONES=320, JK=4, CE=32, CIDX=20, PCF=4, JKN=32, HN=32)
+_sb(BF, KEEPB=512)
+_sb(I32, CI=512, CJ=32, PCI=4)
+_sb(F32, W07=320, ST=3200, NB8=2560, KT0=320, KT7=320, YO=320)
+_pack("BN", F32, GB=320, M1=160, M2=80, M3=40, NE8=320, SC8=320)
+_sb(I32, LBI=20, NBI=160, PI=32)
+_sb(U16, LB=20, NBL=160, ULU=72)
+SCRATCH["NBD"] = ("dram", [16, 160], I32)
+_pack("HB", F32, RB=32, E=16, O=16, SE=16, SO=16, DA=16, DB=20, SM=16, PR=16, NV=16, SYV=16, SG1=16, KK=16, E4=4, SYE=4, KD=4, GTB=4, G2=4, SG2=4, GT=16, GD=16, R=36, NE=28, D4=4, KR=32, NK=4, TA=96, PS=4, PP=32, PT=32, PF32=32, ISL=32, PD=32, PM=32, SELF=32, FC=32, LZ=32, OF=32, BI=40, GK=64, SK=64, GB2=64, SB=64, GS=256, SS=256, GI=512, SI=512, G8=128, S8=128)
+_sb(F32, TR=32, RK=512, SG=512, FW=640, DP=512, SRT=512, SELX=512, FM=512, SCN=512, FX=512, LOWA=672, LOWB=672, LO1=640, LO2=320, REVF=32, XE=320, XS=320, FXR=512)
+_sb(BF, CMP=512, EQB=512, CNT=512)
+_pack("HI", I32, P8=8, P8A=8, P8B=8, XI=20, XJ=20)
+_pack("HU", U16, OFFI=32, KOU=4, KU=16, KU2=4, TU=96, PU=32, SEL=32, EL=20, OFF=32, REV=32, BIU=40)
+_sb(U16, AL=96, PA=32, SL0=16, SL1=16, SL2=16, AR0=16, AR1=16, AR2=16)
+for _t in range(8):
+    SCRATCH["ps%d" % _t] = ("psum", [128, 512], F32)
+
+SEMAPHORES = ["sv", "st", "ss", "sg", "dx", "du", "dv", "dw", "dp", "dlb", "dnb", "dnl", "rsend", "dad", "doc", "dy"]
+for _t in range(3):
+    SEMAPHORES += ["da%d" % _t, "db%d" % _t, "dc%d" % _t, "rq%d" % _t, "rl%d" % _t]
+
+
+def rank_program(g, core, T, topo):
+    rank = T.rank_of(core)
+    if rank is None:
+        return
+    A, ACT = AluOpType, ActivationFunctionType
+    add, sub, mul, mx_, mn_, eq, ne, gt, lt = A.add, A.subtract, A.mult, A.max, A.min, A.is_equal, A.not_equal, A.is_gt, A.is_lt
+    bw, shr = A.bitwise_and, A.arith_shift_right
+    queue = {"v": g.vector, "t": g.tensor, "s": g.scalar, "y": g.sync, "g": g}
+    own = {"v": "sv", "t": "st", "s": "ss", "g": "sg"}
+    count = {k: 0 for k in own}
+    know = {k: {} for k in queue}
+    hist, serial, totals = {}, [0], {}
+
+    def W(name, a, b, st=1, p0=0, p1=128, ps=1):
+        buf, at, _n = PART.get(name, (name, 0, 0))
+        return (buf, a + at, b + at, st, p0, p1, ps)
+
+    def N(v):
+        return W(v, 0, PART[v][2]) if isinstance(v, str) else v
+
+    def I(win, off):
+        return ("I", N(win), N(off))
+
+    def ap(v):
+        v = N(v)
+        if v[0] == "I":
+            return ap(v[1]).indirect(ap(v[2]))
+        n, a, b, st, p0, p1, ps = v
+        rows = slice(p0, p1, ps) if ps != 1 else slice(p0, p1)
+        cs = slice(a, b, st) if st != 1 else slice(a, b)
+        return T[n][rows, cs]
+
+    def meet(a, b, s, c, d, u):
+        if b <= c or d <= a:
+            return False
+        return not (s == u and s > 1 and (a - c) % s)
+
+    def overlap(x, y):
+        return meet(x[1], x[2], x[3], y[1], y[2], y[3]) and meet(x[4], x[5], x[6], y[4], y[5], y[6])
+
+    def covers(x, y):
+        return x[3] == 1 and x[6] == 1 and x[1] <= y[1] and x[2] >= y[2] and x[4] <= y[4] and x[5] >= y[5]
+
+    def sync_for(q, reads, writes):
+        todo = {}
+        for v, w in [(v, False) for v in reads] + [(v, True) for v in writes]:
+            bank = v[0].startswith("ps")
+            for h in hist.get(v[0], ()):
+                if not (w or h["w"] or (bank and h["q"] != q)):
+                    continue
+                if not bank and not overlap(v, h["v"]):
+                    continue
+                if know[q].get(h["sem"], 0) < h["val"]:
+                    if h["sem"] not in todo or todo[h["sem"]]["val"] < h["val"]:
+                        todo[h["sem"]] = h
+        for h in sorted(todo.values(), key=lambda h: -h["n"]):
+            if know[q].get(h["sem"], 0) >= h["val"]:
+                continue
+            queue[q].wait_ge(T.sem[h["sem"]], h["val"])
+            for s, x in h["snap"].items():
+                know[q][s] = max(know[q].get(s, 0), x)
+            know[q][h["sem"]] = h["val"]
+
+    def note(q, reads, writes, sem, val, late, snap=None):
+        serial[0] += 1
+        snap = dict(know[q]) if snap is None else snap
+        for v, w in [(v, False) for v in reads] + [(v, True) for v in writes]:
+            old = hist.setdefault(v[0], [])
+            if w:
+                old[:] = [h for h in old if not covers(v, h["v"])]
+            else:
+                old[:] = [h for h in old if not (not h["w"] and h["q"] == q and not late and not h["late"] and h["v"] == v)]
+            old.append({"v": v, "w": w, "q": q, "late": late, "sem": sem, "val": val, "snap": snap, "n": serial[0]})
+
+    def op(q, call, reads, writes):
+        rd, wr = [], []
+        for v in map(N, reads):
+            rd += [v[1], v[2]] if v[0] == "I" else [v]
+        for v in map(N, writes):
+            wr.append(v[1] if v[0] == "I" else v)
+            rd += [v[2]] if v[0] == "I" else []
+        sync_for(q, rd, wr)
+        if q == "g" and know[q].get("sg", 0) < count[q]:
+            g.wait_ge(T.sem["sg"], count[q])
+            know[q]["sg"] = count[q]
+        count[q] += 1
+        call().then_inc(T.sem[own[q]], 1)
+        note(q, rd, wr, own[q], count[q], False)
+
+    def cp(out, a):
+        op("v", lambda: g.vector.tensor_copy(ap(out), ap(a)), [a], [out])
+
+    def tt(out, a, b, o):
+        op("v", lambda: g.vector.tensor_tensor(ap(out), ap(a), ap(b), o), [a, b], [out])
+
+    def ts(out, a, s1, o0, s2=None, o1=None):
+        x1, x2 = [ap(s) if isinstance(s, tuple) else s for s in (s1, s2)]
+        more = () if o1 is None else (o1,)
+        op("v", lambda: g.vector.tensor_scalar(ap(out), ap(a), x1, x2, o0, *more), [a] + [s for s in (s1, s2) if isinstance(s, tuple)], [out])
+
+    def scan(out, d0, d1):
+        op("v", lambda: g.vector.tensor_tensor_scan(ap(out), ap(d0), ap(d1), 0.0, mul, add), [d0, d1], [out])
+
+    def red(out, a):
+        op("v", lambda: g.vector.tensor_reduce(ap(out), ap(a), AxisListType.X, add), [a], [out])
+
+    def fill(out, c):
+        op("v", lambda: g.vector.memset(ap(out), c), [], [out])
+
+    def tr(out, a):
+        op("v", lambda: g.vector.transpose(ap(out), ap(a)), [a], [out])
+
+    def quant(q, s, a):
+        op("v", lambda: g.vector.quantize_mx(ap(q), ap(s), ap(a)), [a], [q, s])
+
+    def act(out, a, scale=1.0):
+        more = {} if scale == 1.0 else {"scale": scale}
+        op("s", lambda: g.scalar.activation(ap(out), ap(a), ACT.Copy, **more), [a], [out])
+
+    def iota(out, pattern, base, mult):
+        more = {"allow_small_or_imprecise_dtypes": True} if SCRATCH[N(out)[0]][2] == F32 else {}
+        op("g", lambda: g.iota(ap(out), pattern, base, mult, **more), [], [out])
+
+    def select(out, a, pattern, base, mult):
+        op("g", lambda: g.affine_select(ap(out), ap(a), pattern, eq, 0.0, base, mult), [a], [out])
+
+    def mm(bank, lq, ls, l0, rq, rs):
+        a, b, o = W(lq, l0, l0 + 128), W(ls, l0, l0 + 128), W("ps%d" % bank, 0, PART[rq][2])
+        op("t", lambda: g.tensor.matmul_mx(ap(o), ap(a), ap(b), ap(rq), ap(rs), True, True), [a, b, rq, rs], [o])
+
+    def dmas(sem, items):
+        done, total = [], 16 * len(items)
+        totals[sem] = total
+
+        def side(v):
+            if isinstance(v, tuple) and v[0] == "C":
+                return ap(v[1]).bitcast(dt.uint8), [N(v[1])]
+            return (ap(v), [N(v)]) if isinstance(v, (tuple, str)) else (v, [])
+        for q, out, a in items:
+            (o, ow), (i, ir) = side(out), side(a)
+            sync_for(q, ir, ow)
+            queue[q].dma_start(o, i).then_inc(T.sem[sem], 16)
+            done.append((q, ir, ow, dict(know[q])))
+        for q, ir, ow, snap in done:
+            note(q, ir, ow, sem, total, True, snap)
+
+    nxt, prv = T.cores[(rank + 1) % len(T.cores)], T.cores[(rank - 1) % len(T.cores)]
+    a_nxt, m_nxt = topo.addr(nxt), topo.mask(core, nxt)
+    e_out, e_in = len(topo.engines(core, nxt)), len(topo.engines(prv, core))
+    sent = [0]
+
+    def send(out, src, rsem, code=False):
+        sync_for("g", [N(src)], [])
+        o, i = ap(out), ap(src)
+        if code:
+            o, i = o.bitcast(dt.uint8), i.bitcast(dt.uint8)
+        g.remote_dma(o, i, T.sem[rsem], T.sem["rsend"], a_nxt[1], a_nxt[0], m_nxt)
+        sent[0] += e_out
+
+    def arrival(names, sem, n):
+        totals[sem] = n
+        note("r", [], [N(v) for v in names], sem, n, True, {})
+
+    dmas("dx", [("y", "XT", T.x[:, :])])
+    dmas("du", [("s", "UT", T.u[:, :])])
+    dmas("dlb", [("ys"[t % 2], W("LBI", 0, 20, 1, 8 * y + 7 - t, 128, 16), T.nb[16 * t + 8 * y:16 * t + 8 * y + 8, :]) for y in range(2) for t in range(8)])
+    dmas("dp", [("ys"[(b + Q) % 2], W("PI", 0, 32, 1, 32 * Q + b, 32 * Q + 32, 4), T.p[15 - 4 * b - Q:128:16, :]) for Q in range(4) for b in range(4)])
+    dmas("dnb", [("ys"[k % 2], W("NBD", 20 * k, 20 * k + 20, 1, 8 * y, 8 * y + 8), T.nb[2 * k + y:128:16, :]) for k in range(8) for y in range(2)])
+    dmas("dnl", [("y", W("NBI", 0, 160, 1, 16 * k, 16 * k + 16), W("NBD", 0, 160, 1, 0, 16)) for k in range(8)])
+    dmas("dw", [("y", ("C", "wq"), T.wc[:, :]), ("y", "wsc", T.ws[:, :])])
+    dmas("dv", [("y", "VT", T.v[:, :])])
+
+    fill("BY", 0.0)
+    for k in range(8):
+        for y in range(2):
+            fill(W("BY", 64 * k + 33 * y, 64 * k + 32 * y + 32, 4), 1.0)
+    fill("ULU", 0)
+    fill("DT", 0.0)
+    iota(W("PCI", 0, 1), [[0, 1]], 0, 1)
+    iota(W("IOTA", 0, 320), [[1, 320]], 0, 0)
+    for e in (0, 7):
+        select("CB%d" % e, "BY", [[0, 16], [-16, 8], [0, 4]], 0 if e == 0 else -8, 1)
+    iota("CI", [[0, 32], [-1, 16]], 16, 1)
+    iota("CIDX", [[16, 20]], -1, 0)
+    for Q in range(4):
+        iota(W("JK", 0, 4, 1, 32 * Q, 32 * Q + 32), [[-4, 4]], 7 * 512 + 15 - Q, 16)
+    iota("CE", [[16, 32]], 128, 0)
+    iota("CJ", [[16, 32]], 15, 0)
+
+    def later_constants():
+        for b in range(4):
+            select("CT%d" % b, "ON", [[1, 512]], -b, -4)
+        iota(W("LOWC", 0, 336), [[1, 336]], 512 * 1024 + 640, 0)
+        iota(W("LOWC", 336, 672), [[1, 336]], 512 * 1024 + 640, 0)
+        iota("PLC", [[16384, 32], [-1024, 16]], 15 * 1024, 0)
+        iota("IO512", [[512, 320]], 0, 0)
+        iota(W("IOTA", 320, 4096), [[1, 3776]], 320, 0)
+
+    pc, pf = (lambda i: W("PCI", i, i + 1)), (lambda i: W("PCF", i, i + 1))
+    ts(pc(1), pc(0), 15, bw)
+    ts(pc(2), pc(0), 3, shr, 1, bw)
+    cp(pf(0), pc(1))
+    cp(pf(1), pc(2))
+    ts(W("ULU", 0, 8), W("ULU", 8, 16), pf(1), add, 112.0, mul)
+    for k in range(1, 8):
+        fill(W("ULU", 8 + 8 * k, 16 + 8 * k), 16 * k)
+    quant("uq", "us", "UT")
+
+    def pick_u(a, b):
+        ul, o = W("ULU", a // 16, b // 16), W("ur", a, b)
+        op("v", lambda: g.vector.tensor_copy(ap(o).bitcast(dt.uint32), ap("uq").bitcast(dt.uint32).indirect(ap(ul))), ["uq", ul], [o])
+        act(W("urs", a, b), I("us", ul))
+    pick_u(0, 128)
+    quant("mq0", "ms0", "XT")
+    pick_u(128, 1152)
+    for e in (0, 7):
+        quant("bq%d" % e, "bs%d" % e, "CB%d" % e)
+    fill("ONES", 1.0)
+    fill("ON", 1.0)
+    cp("LB", "LBI")
+    ts("TR", "PI", float(BIAS), add)
+    CELLS, CELLS8 = W("IOTA", 0, 320), W("IOTA", BIAS, BIAS + 320)
+
+    def more_constants():
+        cp("NBL", "NBI")
+        act(W("NB8", 0, 1600), I(CELLS, W("NBL", 0, 100)))
+        for k in ("KEEP", "KEEPB"):
+            fill(k, 1.0)
+        ts("CI", "CI", 15, bw)
+        for k in ("KEEP", "KEEPB"):
+            fill(W(k, 0, 512, 16), 0.0)
+        ts("MASK", "CI", 0.0, eq)
+        ts("CE", "CE", pf(0), add)
+        ts(pc(2), pc(1), 1, shr)
+        ts(pc(3), pc(1), 1, bw)
+        fill("DB", 0.0)
+        ts(pf(2), pc(2), 320.0, mul)
+        ts(pf(3), pc(3), 8.0, mul)
+        for k in (0, 2880):
+            fill(W("ST", k, k + 320), 0.0)
+        ts("CIDX", "CIDX", pf(2), add, pf(3), add)
+        ts(pf(0), pf(0), 320.0 + BIAS, add)
+        cp(W("NB8", 1600, 2560), I(CELLS, W("NBL", 100, 160)))
+
+    def last_constants():
+        for b in range(4):
+            quant("eq%d" % b, "es%d" % b, "CT%d" % b)
+        for k in range(8):
+            ts(W("JKN", 4 * k, 4 * k + 4), "JK", -1.0 / 512, mul)
+        fill("HN", -511.0)
+        fill(W("HN", 3, 32, 4), 0.0)
+
+    def end_constants():
+        quant("vq", "vs", "VT")
+        ts("REVF", "CJ", pf(0), sub, 320.0 + BIAS, add)
+        cp("REV", "REVF")
+
+    MASK, KEEP = (lambda n: W("MASK", 0, n)), (lambda n: W("KEEP", 0, n))
+
+    def halfstep(par, last, fillers):
+        Y, S, oth = ("E", "SE", "O") if par == 0 else ("O", "SO", "E")
+        eb, i0, ge, kt = (0, 4, 0, "KT0") if par == 0 else (12, 0, 7, "KT7")
+        e = lambda n: W(n, eb, eb + 4)
+        m, dbv, off = e(oth), (W("DB", 0, 16) if par == 0 else W("DB", 4, 20)), 320.0 * (ge + 1)
+        cp("KOU", m)
+        ts(e("KU"), m, off, add)
+        if par == 0:
+            tt(W("KK", 4, 16), W("O", 4, 16), W("DB", 4, 16), sub)
+        else:
+            tt(W("KK", 0, 12), W("E", 4, 16), W("DA", 0, 12), sub)
+        tt("PR", "DA", dbv, mul)
+        ts("E4", e("DA"), 0.0, ne, FAR, mul)
+        tt("GK", I(kt, "KOU"), MASK(64), mul)
+        for i in range(i0 // 4, i0 // 4 + 3):
+            ts(W("KU", 4 * i, 4 * i + 4), W("KK", 4 * i, 4 * i + 4), 320.0 * (2 * i + par + 1), add)
+        ts("NV", "PR", 0.0, ne, FAR, mul)
+        tt("SYE", e(S), "E4", add)
+        scan("SK", KEEP(64), "GK")
+        tt("GS", I("ST", "KU"), MASK(256), mul)
+        tt("SM", *(("DA", dbv) if par == 0 else (dbv, "DA")), sub)
+        tt("SYV", S, "NV", add)
+        for f in fillers:
+            f()
+        k0, sk, sb = W("SK", 15, 64, 16), W("SS", 15, 256, 16), W("SB", 15, 64, 16)
+        ts("KU2", k0, off, add)
+        scan("SS", KEEP(256), "GS")
+        tt("KD", k0, m, sub)
+        tt("GB2", I("ST", "KU2"), MASK(64), mul)
+        tt("GT", sk, "SYV", gt)
+        scan("SB", KEEP(64), "GB2")
+        tt("GD", "GT", "SM", mul)
+        tt("GTB", sb, "SYE", gt)
+        if last and par == 1:
+            for i in (3, 0, 1, 2):
+                tt(W("R", 8 * i + 4, 8 * i + 8), W("O", 4 * i, 4 * i + 4), W("GD", 4 * i, 4 * i + 4), add)
+        else:
+            tt(Y, Y, "GD", add)
+            tt("DA", "DA", "GD", sub if par == 0 else add)
+            if par == 0:
+                tt(W("DB", 4, 16), W("DB", 4, 16), W("GD", 4, 16), add)
+            else:
+                tt(W("DB", 4, 16), W("DB", 4, 16), W("GD", 0, 12), sub)
+        tt("G2", "GTB", "KD", mul)
+        if not last:
+            tt("SG1", sk, "NV", sub)
+            tt("SG2", sb, "E4", sub)
+            tt(S, S, "SG1", mx_)
+        if last and par == 1:
+            tt(W("R", 28, 32), W("R", 28, 32), "G2", add)
+        else:
+            tt(e("DA"), e("DA"), "G2", sub if par == 0 else add)
+            tt(e(Y), e(Y), "G2", add)
+        if not last:
+            tt(e(S), e(S), "SG2", mx_)
+
+    for rd in range(ROUNDS):
+        mq, ms, lq, ls, sl, ar = "mq%d" % rd, "ms%d" % rd, "lq%d" % rd, "ls%d" % rd, "SL%d" % rd, "AR%d" % rd
+        send(lq, mq, "rq%d" % rd, True)
+        send(ls, ms, "rq%d" % rd)
+        arrival([lq, ls], "rq%d" % rd, 2 * e_in)
+        if rd == 0:
+            later_constants()
+        mm(0, "ur", "urs", 0, mq, ms)
+        for k in range(8):
+            mm((k + 1) % 8, "ur", "urs", 128 + 128 * k, mq, ms)
+            if k == 0:
+                act("W07", W("ps0", 0, 320))
+            act(W("ST", 320 * k + 320, 320 * k + 640), W("ps%d" % ((k + 1) % 8), 0, 320))
+        tr("RB", "TR")
+        for i in range(4):
+            for par in range(2):
+                src = W("RB", 8 * i + 4 * par, 8 * i + 4 * par + 4)
+                ts(W("OFFI", 16 * par + 4 * i, 16 * par + 4 * i + 4), src, 320.0 * (2 * i + par + 1) - BIAS, add)
+                ts(W("EO"[par], 4 * i, 4 * i + 4), src, -float(BIAS), add)
+        cp("GB", I("W07", "LB"))
+        tt("M1", W("GB", 0, 320, 2), W("GB", 1, 320, 2), mx_)
+        tt("M2", W("M1", 0, 160, 2), W("M1", 1, 160, 2), mx_)
+        tt("M3", W("M2", 0, 80, 2), W("M2", 1, 80, 2), mx_)
+        for t in range(8):
+            tt(W("NE8", t, 320, 8), W("GB", t, 320, 8), "M3", ne)
+        scan("SC8", "NE8", "ONES")
+        cp(W("DT", 0, 80, 4), W("SC8", 7, 320, 16))
+        cp(W("DT", 1, 80, 4), W("SC8", 15, 320, 16))
+        quant("dq", "dsc", "DT")
+        mm(1, "bq0", "bs0", 0, "dq", "dsc")
+        mm(2, "bq7", "bs7", 0, "dq", "dsc")
+        if rd == 0:
+            more_constants()
+        tt("GI", I("ST", "OFFI"), "MASK", mul)
+        tt(W("BI", 0, 20), W("ps1", 0, 20), "CIDX", add)
+        tt(W("BI", 20, 40), W("ps2", 0, 20), "CIDX", add)
+        cp("BIU", "BI")
+        act("KT0", I("NB8", W("BIU", 0, 20)))
+        act("KT7", I("NB8", W("BIU", 20, 40)))
+        scan("SI", "KEEP", "GI")
+        tt("DA", "O", "E", sub)
+        tt(W("DB", 4, 16), W("E", 4, 16), W("O", 0, 12), sub)
+        cp("SE", W("SI", 15, 256, 16))
+        cp("SO", W("SI", 271, 512, 16))
+        halfstep(0, False, [])
+        if rd == 0:
+            last_constants()
+        for t in range(4):
+            f = W("ps%d" % (3 + t), 0, 320)
+            mm(3 + t, "eq%d" % t, "es%d" % t, 0, mq, ms)
+            act("FQ%d" % t, f, 0.25)
+            act("FH%d" % t, f, 0.5)
+            act(W("YW%d" % t, 640, 960), f, 0.5)
+        act("LOWA", "LOWC")
+        act("LOWB", "LOWC")
+        for t in range(4):
+            k = (7, 0, 1, 2)[t]
+            mm(k, "eq%d" % t, "es%d" % t, 0, lq, ls)
+            act("PF%d" % t, W("ps%d" % k, 0, 320), 0.5)
+        halfstep(1, False, [])
+        halfstep(0, True, [])
+        halfstep(1, True, [lambda i=i: cp(W("R", 8 * i, 8 * i + 4), W("E", 4 * i, 4 * i + 4)) for i in range(4)] + [lambda: cp(W("R", 32, 36), W("E", 12, 16))])
+        tt("NE", W("R", 0, 28), W("R", 4, 32), ne)
+        tr(W("TA", 0, 32), W("R", 0, 32))
+        tr(W("TA", 32, 64), W("R", 4, 36))
+        for b in range(4):
+            red(W("D4", b, b + 1), W("NE", b, 28, 4))
+        for b in range(4):
+            ts(W("KR", b, 32, 4), W("JKN", b, 32, 4), W("D4", b, b + 1), add, -512.0, mul)
+        tr(W("TA", 64, 96), "KR")
+        ts("NK", W("KR", 0, 4), -1.0, mul)
+        cp("TU", "TA")
+        dmas("da%d" % rd, [("ys"[Q % 2], W("AL", 0, 96, 1, Q, 128, 4), W("TU", 0, 96, 1, 32 * Q, 32 * Q + 32)) for Q in range(4)])
+        if rd == 0:
+            end_constants()
+        al, bl, kl = W("AL", 0, 32), W("AL", 32, 64), W("AL", 64, 96)
+        cp("RK", I("IOTA", kl))
+        for b in range(3):
+            bi, ac = W("NK", b, b + 1), W("PS", b, b + 1)
+            op("s", lambda: g.scalar.activation(ap("SG"), ap("RK"), ACT.Sign, bias=ap(bi), accum_out=ap(ac)), ["RK", bi], ["SG", ac])
+        act(W("FW", 128, 640), I(CELLS8, al))
+        ts("CMP", "RK", W("KR", 3, 4), lt, -2.0, mul)
+        red(W("PS", 3, 4), "CMP")
+        for b in range(4):
+            ts(W("PP", b, 32, 4), W("HN", b, 32, 4), W("PS", b, b + 1), add, -0.5, mul)
+        tr("PT", "PP")
+        cp("PU", "PT")
+        dmas("db%d" % rd, [("y", W("PA", 0, 32, 1, Q, 128, 4), W("PU", 0, 32, 1, 32 * Q, 32 * Q + 32)) for Q in range(4)])
+        tt("DP", I("IO512", bl), W("FW", 128, 640), add)
+        for t in range(4):
+            act("ZG%d" % t, I("FQ%d" % t, al))
+
+        def bonds(t):
+            tt(W("YW%d" % t, 128, 640), I("FQ%d" % t, bl), "ZG%d" % t, add)
+        bonds(0)
+        bonds(1)
+        cp(I("SRT", "PA"), "DP")
+        cp("PF32", "PA")
+        tt("G8", W("SRT", 0, 128), MASK(128), mul)
+        ts("ISL", "PF32", 128.0, lt)
+        scan("S8", KEEP(128), "G8")
+        tt("PD", "PF32", "CE", sub)
+        cp("P8", W("S8", 15, 128, 16))
+        tt("PM", "PD", "ISL", mul)
+        ts("P8A", "P8", 511, bw)
+        ts("P8B", "P8", 9, shr)
+        tt("SELF", "PM", "CE", add)
+        ts(W(sl, 0, 8), "P8A", -float(BIAS), add)
+        cp(W(sl, 8, 16), "P8B")
+        cp("SEL", "SELF")
+        send(ar, sl, "rl%d" % rd)
+        arrival([ar], "rl%d" % rd, e_in)
+        tt("SELX", I("IOTA", "SEL"), "PLC", add)
+        bonds(2)
+        bonds(3)
+        aa, ab = W(ar, 0, 8), W(ar, 8, 16)
+        cp(W("FW", 0, 128), I(CELLS8, aa))
+        for t in range(4):
+            act(W("HG", 128 * t, 128 * t + 128), I("PF%d" % t, aa))
+        act("FX", I("FW", "SEL"))
+        tt("FM", I("FW", "SEL"), "MASK", mul)
+
+        def arrived(t):
+            tt(W("HT", t, 512, 4), I("PF%d" % t, ab), W("HG", 128 * t, 128 * t + 128), add)
+        arrived(0)
+        scan("SCN", "KEEP", "FM")
+        arrived(1)
+        tt("EQB", "FX", "SCN", eq)
+        cp("FC", W("SCN", 15, 512, 16))
+        if rd + 1 < ROUNDS:
+            dmas("dc%d" % rd, [("y", W("TR", 0, 32, 1, 32 * Q, 32 * Q + 32), W("FC", 0, 32, 1, Q, 128, 4)) for Q in range(4)])
+        arrived(2)
+        scan("CNT", "KEEPB", "EQB")
+        arrived(3)
+        ts("LZ", W("CNT", 15, 512, 16), 1.5, gt, pf(0), mul)
+        quant("aq", "asc", "HT")
+        tt("OF", "FC", "LZ", mx_)
+        for b in range(4):
+            mm(3 + b, "wq", "wsc", 128 * b, "aq", "asc")
+            act(W("YW%d" % b, 0, 128), W("ps%d" % (3 + b), 0, 128), 2.0 ** -6)
+        if rd + 1 == ROUNDS:
+            fr = I("FX", "REV")
+            op("s", lambda: g.scalar.activation(ap("FXR"), ap(fr), ACT.Identity, bias=-float(BIAS)), [fr], ["FXR"])
+            dmas("dad", [("y", T.ad[:, :], W("FXR", 0, 512, 1, 0, 128, 16))])
+        ts(W("OFF", 0, 32, 2), W("OF", 0, 32, 2), -float(BIAS), add)
+        ts(W("OFF", 1, 32, 2), W("OF", 1, 32, 2), 336.0 - BIAS, add)
+        for k in range(15, -1, -1):
+            cp(I("LOWA" if k % 2 else "LOWB", W("OFF", 2 * k, 2 * k + 2)), W("SELX", 32 * k, 32 * k + 32))
+        for i in range(2):
+            tt(W("LO1", 320 * i, 320 * i + 320), W("LOWA", 336 * i, 336 * i + 320), W("LOWB", 336 * i, 336 * i + 320), mn_)
+        tt("LO2", W("LO1", 0, 320), W("LO1", 320, 640), mn_)
+        tt("XE", "LO2", MASK(320), mul)
+        scan("XS", KEEP(320), "XE")
+        cp("XI", W("XS", 15, 320, 16))
+        ts("XJ", "XI", 1023, bw)
+        cp("EL", "XJ")
+        for t in range(4):
+            tt(W("MT", t, 1280, 4), I("YW%d" % t, "EL"), "FH%d" % t, add)
+        quant("mq%d" % (rd + 1), "ms%d" % (rd + 1), "MT")
+
+    mq, ms = "mq%d" % ROUNDS, "ms%d" % ROUNDS
+    mm(0, "vq", "vs", 0, mq, ms)
+    act("YO", W("ps0", 0, 320))
+    dmas("doc", [("y", T.oc[:, :], ("C", mq))] + [("y", T.osc[4 * k:4 * k + 4, :], W(ms, 0, 320, 1, 32 * k, 32 * k + 4)) for k in range(4)])
+    dmas("dy", [("s", T.y[:, :], "YO")])
+
+    g.wait_ge(T.sem["rsend"], sent[0])
+    for q in own:
+        g.wait_ge(T.sem[own[q]], count[q])
+    for s in sorted(totals):
+        g.wait_ge(T.sem[s], totals[s])

@@ -2,7 +2,8 @@ from concourse.mybir import dt, AluOpType, AxisListType, ActivationFunctionType
 
 ROUNDS = 3
 FAR = 1e29
-BIAS = 8
+MID = 160
+ROUND = 12582912.0
 F32, BF, I32, U16, MXC, U8 = "float32", "bfloat16", "int32", "uint16", "float8_e4m3fn_x4", "uint8"
 SCRATCH, PART = {}, {}
 
@@ -21,39 +22,41 @@ def _pack(buf, dtype, **kw):
     SCRATCH[buf] = ("sbuf", [128, at], dtype)
 
 
-_sb(BF, XT=1280, MT=1280, UT=512, VT=512, BY=512, ON=512, DT=512, HT=512, HG=512)
+_sb(BF, XT=1280, MT=1280, UT=512, VT=512, BY=128, ON=512, DT=512, ZT=512, HT=512, CB=512)
 _pack("CTB", BF, CT0=512, CT1=512, CT2=512, CT3=512)
-_pack("CBB", BF, CB0=512, CB7=512)
 _pack("YW", BF, YW0=960, YW1=960, YW2=960, YW3=960)
 _pack("FH", BF, FH0=320, FH1=320, FH2=320, FH3=320)
 _pack("FQ", BF, FQ0=320, FQ1=320, FQ2=320, FQ3=320)
-_pack("PF", BF, PF0=320, PF1=320, PF2=320, PF3=320)
 _pack("ZG", BF, ZG0=512, ZG1=512, ZG2=512, ZG3=512)
-_sb(MXC, uq=128, ur=1152, vq=128, dq=128, aq=128, wq=512, mq0=320, mq1=320, mq2=320, mq3=320, lq0=320, lq1=320, lq2=320)
-_sb(U8, us=128, urs=1152, vs=128, dsc=128, asc=128, wsc=512, ms0=320, ms1=320, ms2=320, ms3=320, ls0=320, ls1=320, ls2=320)
-_pack("eqc", MXC, eq0=128, eq1=128, eq2=128, eq3=128, bq0=128, bq7=128)
-_pack("esc", U8, es0=128, es1=128, es2=128, es3=128, bs0=128, bs7=128)
-_sb(F32, IOTA=4096, IO512=320, LOWC=672, PLC=512)
-_pack("KC", F32, MASK=512, KEEP=512, ONES=320, JK=4, CE=32, CIDX=20, PCF=4, JKN=32, HN=32)
-_sb(BF, KEEPB=512)
-_sb(I32, CI=512, CJ=32, PCI=4)
-_sb(F32, W07=320, ST=3200, NB8=2560, KT0=320, KT7=320, YO=320)
-_pack("BN", F32, GB=320, M1=160, M2=80, M3=40, NE8=320, SC8=320)
-_sb(I32, LBI=20, NBI=160, PI=32)
-_sb(U16, LB=20, NBL=160, ULU=72)
-SCRATCH["NBD"] = ("dram", [16, 160], I32)
-_pack("HB", F32, RB=32, E=16, O=16, SE=16, SO=16, DA=16, DB=20, SM=16, PR=16, NV=16, SYV=16, SG1=16, KK=16, E4=4, SYE=4, KD=4, GTB=4, G2=4, SG2=4, GT=16, GD=16, R=36, NE=28, D4=4, KR=32, NK=4, TA=96, PS=4, PP=32, PT=32, PF32=32, ISL=32, PD=32, PM=32, SELF=32, FC=32, LZ=32, OF=32, BI=40, GK=64, SK=64, GB2=64, SB=64, GS=256, SS=256, GI=512, SI=512, G8=128, S8=128)
-_sb(F32, TR=32, RK=512, SG=512, FW=640, DP=512, SRT=512, SELX=512, FM=512, SCN=512, FX=512, LOWA=672, LOWB=672, LO1=640, LO2=320, REVF=32, XE=320, XS=320, FXR=512)
-_sb(BF, CMP=512, EQB=512, CNT=512)
-_pack("HI", I32, P8=8, P8A=8, P8B=8, XI=20, XJ=20)
-_pack("HU", U16, OFFI=32, KOU=4, KU=16, KU2=4, TU=96, PU=32, SEL=32, EL=20, OFF=32, REV=32, BIU=40)
-_sb(U16, AL=96, PA=32, SL0=16, SL1=16, SL2=16, AR0=16, AR1=16, AR2=16)
+_sb(F32, W07=320, GB=320, RM=320, K8=320)
+_sb(MXC, uq=128, ur=384, vq=128, dq=256, bq=128, wq=512, mq0=320, mq1=320, mq2=320, mq3=320)
+_sb(U8, us=128, urs=384, vs=128, dsc=256, bs=128, wsc=512, ms0=320, ms1=320, ms2=320, ms3=320)
+_sb(MXC, aq0=128, aq1=128, aq2=128, lq0=128, lq1=128, lq2=128)
+_sb(U8, as0=128, as1=128, as2=128, ls0=128, ls1=128, ls2=128)
+_pack("eqc", MXC, eq0=128, eq1=128, eq2=128, eq3=128)
+_pack("esc", U8, es0=128, es1=128, es2=128, es3=128)
+_sb(F32, IOTA=4096, LOWC=640, ENT=512)
+_sb(BF, MASK=512, KEEP=512, I16=512, KP=256)
+_pack("KC", F32, PCF=16, CE=32, CIDX=20, ULF=24, RHO=16, E256=16, NF=16, TF=16, T2=16, T3=16, DUMP=32, REVF=32, LEF=2)
+_sb(I32, PCI=8, LBI=20, NBI=160, PI=32)
+_pack("KU16", U16, ULU=24, LB=20, NBL=160, LI=16, LJ=16, LE=2, REV=32)
+_sb(F32, ST=960, NB8=2560, KT=640, YO=320)
+_pack("HB", F32, R=64, S30=16, NS=16, NZ=16, BL=16, DE=64, DO=64, DL=64, D0=64, D0L=64, OUT0=64, OUT1=64, OUT2=64, OUT3=64, ZZ=32, KK0=32, KK1=32,
+      KK2=32, KK3=32, DC=16, PR=16, NV=16, SYV=16, SG1=16, BA=16, BC=16, BI=20, GS=256, SS=256, GK=256, SK0=256, SK1=256, GI=512, SI=512)
+_pack("OB", F32, NN=64, S1=64, S2=64, KD=32, KR=32, NK=4, PS=4, PP=32, PT=32, TA=64, PF=32, T1=32, TM=32, SELF=32, VT_=32, G8=128, S8=128,
+      E1=8, E2=8, FCF=32, PP_=32, LZD=32, OF=32, OT=32, M1=40)
+_sb(F32, RK=512, DP=512, SRT=512, SELX=512, LA=672, LBW=672, TLA=640, TLB=640, FX=512, FXR=512)
+_sb(BF, SG0=512, SG1B=512, SG2=512, CMP=514, FM=512, SCN=512, PA_=256, PB_=256, EQ=256, EQS=256, MSG0=128, MSG1=128, MSG2=128, FW0=640, FW1=640, FW2=640)
+_pack("HI", I32, FCI=32, FA=32, M2=20, M3=20)
+_pack("HU", U16, OFFI=32, KU=16, BKU=16, BIU=20, AL=64, KL=32, PA=32, SEL=32, VL=32, EL2=8, OFF=32, EL=20)
 for _t in range(8):
     SCRATCH["ps%d" % _t] = ("psum", [128, 512], F32)
 
-SEMAPHORES = ["sv", "st", "ss", "sg", "dx", "du", "dv", "dw", "dp", "dlb", "dnb", "dnl", "rsend", "dad", "doc", "dy"]
+SEMAPHORES = ["sv", "st", "ss", "sg", "dx", "du", "dv", "dw", "dp0", "dp1", "dl0", "dl1", "dn", "rsend", "dad", "doc", "dy"]
 for _t in range(3):
-    SEMAPHORES += ["da%d" % _t, "db%d" % _t, "dc%d" % _t, "rq%d" % _t, "rl%d" % _t]
+    SEMAPHORES += ["rq%d" % _t, "rl%d" % _t]
+
+WAKE, LOCAL, REMOTE = 130.0, 1900.0, 2800.0
 
 
 def rank_program(g, core, T, topo):
@@ -61,13 +64,10 @@ def rank_program(g, core, T, topo):
     if rank is None:
         return
     A, ACT = AluOpType, ActivationFunctionType
-    add, sub, mul, mx_, mn_, eq, ne, gt, lt = A.add, A.subtract, A.mult, A.max, A.min, A.is_equal, A.not_equal, A.is_gt, A.is_lt
+    add, sub, mul, mx_, mn_, eq, ne, gt, lt, ge, le = A.add, A.subtract, A.mult, A.max, A.min, A.is_equal, A.not_equal, A.is_gt, A.is_lt, A.is_ge, A.is_le
     bw, shr = A.bitwise_and, A.arith_shift_right
     queue = {"v": g.vector, "t": g.tensor, "s": g.scalar, "y": g.sync, "g": g}
     own = {"v": "sv", "t": "st", "s": "ss", "g": "sg"}
-    count = {k: 0 for k in own}
-    know = {k: {} for k in queue}
-    hist, serial, totals = {}, [0], {}
 
     def W(name, a, b, st=1, p0=0, p1=128, ps=1):
         buf, at, _n = PART.get(name, (name, 0, 0))
@@ -75,6 +75,9 @@ def rank_program(g, core, T, topo):
 
     def N(v):
         return W(v, 0, PART[v][2]) if isinstance(v, str) else v
+
+    def Q(v, q, n=1):
+        return N(v)[:4] + (32 * q, 32 * (q + n), 1)
 
     def I(win, off):
         return ("I", N(win), N(off))
@@ -97,447 +100,507 @@ def rank_program(g, core, T, topo):
         return meet(x[1], x[2], x[3], y[1], y[2], y[3]) and meet(x[4], x[5], x[6], y[4], y[5], y[6])
 
     def covers(x, y):
-        return x[3] == 1 and x[6] == 1 and x[1] <= y[1] and x[2] >= y[2] and x[4] <= y[4] and x[5] >= y[5]
+        return (x[3] == 1 or x[1:4] == y[1:4]) and x[6] == 1 and x[1] <= y[1] and x[2] >= y[2] and x[4] <= y[4] and x[5] >= y[5]
 
-    def sync_for(q, reads, writes):
-        todo = {}
-        for v, w in [(v, False) for v in reads] + [(v, True) for v in writes]:
-            bank = v[0].startswith("ps")
-            for h in hist.get(v[0], ()):
-                if not (w or h["w"] or (bank and h["q"] != q)):
-                    continue
-                if not bank and not overlap(v, h["v"]):
-                    continue
-                if know[q].get(h["sem"], 0) < h["val"]:
-                    if h["sem"] not in todo or todo[h["sem"]]["val"] < h["val"]:
-                        todo[h["sem"]] = h
-        for h in sorted(todo.values(), key=lambda h: -h["n"]):
-            if know[q].get(h["sem"], 0) >= h["val"]:
-                continue
-            queue[q].wait_ge(T.sem[h["sem"]], h["val"])
-            for s, x in h["snap"].items():
-                know[q][s] = max(know[q].get(s, 0), x)
-            know[q][h["sem"]] = h["val"]
+    def clash(v, w, q, h):
+        bank = v[0].startswith("ps")
+        return (w or h["w"] or (bank and h["q"] != q)) and (bank or overlap(v, h["v"]))
 
-    def note(q, reads, writes, sem, val, late, snap=None):
-        serial[0] += 1
-        snap = dict(know[q]) if snap is None else snap
-        for v, w in [(v, False) for v in reads] + [(v, True) for v in writes]:
-            old = hist.setdefault(v[0], [])
-            if w:
-                old[:] = [h for h in old if not covers(v, h["v"])]
-            else:
-                old[:] = [h for h in old if not (not h["w"] and h["q"] == q and not late and not h["late"] and h["v"] == v)]
-            old.append({"v": v, "w": w, "q": q, "late": late, "sem": sem, "val": val, "snap": snap, "n": serial[0]})
+    nodes = []
 
-    def op(q, call, reads, writes):
+    def width(v):
+        v = N(v)
+        return 16 * width(v[2]) if v[0] == "I" else len(range(v[1], v[2], v[3]))
+
+    def cost(out, ins, per=1.0):
+        sides = [N(v) for v in [out] + ins]
+        if sides[0][0] == "I":
+            return 50 + 2.5 * width(out)
+        if any(v[0] == "I" for v in sides):
+            return 55 + 1.25 * width(out)
+        if all(SCRATCH[v[0]][2] in (BF, U16) for v in sides):
+            per *= 0.5
+        return max(64.0, per * width(ins[0] if ins else out))
+
+    def node(q, call, reads, writes, busy, kind="op", after=0.0, **more):
         rd, wr = [], []
         for v in map(N, reads):
             rd += [v[1], v[2]] if v[0] == "I" else [v]
         for v in map(N, writes):
             wr.append(v[1] if v[0] == "I" else v)
             rd += [v[2]] if v[0] == "I" else []
-        sync_for(q, rd, wr)
-        if q == "g" and know[q].get("sg", 0) < count[q]:
-            g.wait_ge(T.sem["sg"], count[q])
-            know[q]["sg"] = count[q]
-        count[q] += 1
-        call().then_inc(T.sem[own[q]], 1)
-        note(q, rd, wr, own[q], count[q], False)
+        nodes.append(dict(q=q, call=call, rd=rd, wr=wr, busy=busy, kind=kind, after=after, **more))
 
     def cp(out, a):
-        op("v", lambda: g.vector.tensor_copy(ap(out), ap(a)), [a], [out])
+        node("v", lambda: g.vector.tensor_copy(ap(out), ap(a)), [a], [out], cost(out, [a]))
 
     def tt(out, a, b, o):
-        op("v", lambda: g.vector.tensor_tensor(ap(out), ap(a), ap(b), o), [a, b], [out])
+        per = 1.0 if N(a)[0].startswith("ps") else 2.0
+        node("v", lambda: g.vector.tensor_tensor(ap(out), ap(a), ap(b), o), [a, b], [out], cost(out, [a, b], per),
+             drain=N(a)[0] != "I" and N(a)[4] != N(b)[4])
 
     def ts(out, a, s1, o0, s2=None, o1=None):
         x1, x2 = [ap(s) if isinstance(s, tuple) else s for s in (s1, s2)]
         more = () if o1 is None else (o1,)
-        op("v", lambda: g.vector.tensor_scalar(ap(out), ap(a), x1, x2, o0, *more), [a] + [s for s in (s1, s2) if isinstance(s, tuple)], [out])
+        node("v", lambda: g.vector.tensor_scalar(ap(out), ap(a), x1, x2, o0, *more), [a] + [s for s in (s1, s2) if isinstance(s, tuple)], [out], cost(out, [a]))
 
-    def scan(out, d0, d1):
-        op("v", lambda: g.vector.tensor_tensor_scan(ap(out), ap(d0), ap(d1), 0.0, mul, add), [d0, d1], [out])
+    def scan(out, d0, d1, o0=mul, o1=add, first=0.0):
+        node("v", lambda: g.vector.tensor_tensor_scan(ap(out), ap(d0), ap(d1), first, o0, o1), [d0, d1], [out], cost(out, [d0, d1]))
 
     def red(out, a):
-        op("v", lambda: g.vector.tensor_reduce(ap(out), ap(a), AxisListType.X, add), [a], [out])
+        node("v", lambda: g.vector.tensor_reduce(ap(out), ap(a), AxisListType.X, add), [a], [out], float(width(a)))
 
     def fill(out, c):
-        op("v", lambda: g.vector.memset(ap(out), c), [], [out])
+        node("v", lambda: g.vector.memset(ap(out), c), [], [out], cost(out, []))
 
     def tr(out, a):
-        op("v", lambda: g.vector.transpose(ap(out), ap(a)), [a], [out])
+        node("v", lambda: g.vector.transpose(ap(out), ap(a)), [a], [out], cost(out, [a]))
 
     def quant(q, s, a):
-        op("v", lambda: g.vector.quantize_mx(ap(q), ap(s), ap(a)), [a], [q, s])
+        node("v", lambda: g.vector.quantize_mx(ap(q), ap(s), ap(a)), [a], [q, s], 12 + 0.26 * width(a))
 
-    def act(out, a, scale=1.0):
+    def act(out, a, scale=1.0, bias=None, func=None, acc=None):
         more = {} if scale == 1.0 else {"scale": scale}
-        op("s", lambda: g.scalar.activation(ap(out), ap(a), ACT.Copy, **more), [a], [out])
+        if bias is not None:
+            more["bias"] = ap(bias) if isinstance(bias, tuple) else bias
+        if acc is not None:
+            more["accum_out"] = ap(acc)
+        f = func or (ACT.Copy if bias is None else ACT.Identity)
+        busy = cost(out, [a]) if N(a)[0] == "I" else max(64.0, width(a))
+        node("s", lambda: g.scalar.activation(ap(out), ap(a), f, **more), [a] + ([bias] if isinstance(bias, tuple) else []), [out] + ([acc] if acc else []), busy + 20)
 
     def iota(out, pattern, base, mult):
-        more = {"allow_small_or_imprecise_dtypes": True} if SCRATCH[N(out)[0]][2] == F32 else {}
-        op("g", lambda: g.iota(ap(out), pattern, base, mult, **more), [], [out])
+        more = {} if SCRATCH[N(out)[0]][2] == I32 else {"allow_small_or_imprecise_dtypes": True}
+        node("g", lambda: g.iota(ap(out), pattern, base, mult, **more), [], [out], 130 + WAKE + 2.0 * width(out))
 
     def select(out, a, pattern, base, mult):
-        op("g", lambda: g.affine_select(ap(out), ap(a), pattern, eq, 0.0, base, mult), [a], [out])
+        node("g", lambda: g.affine_select(ap(out), ap(a), pattern, eq, 0.0, base, mult), [a], [out], 170 + WAKE + 2.0 * width(out))
 
-    def mm(bank, lq, ls, l0, rq, rs):
-        a, b, o = W(lq, l0, l0 + 128), W(ls, l0, l0 + 128), W("ps%d" % bank, 0, PART[rq][2])
-        op("t", lambda: g.tensor.matmul_mx(ap(o), ap(a), ap(b), ap(rq), ap(rs), True, True), [a, b, rq, rs], [o])
+    def mm(bank, lq, ls, rq, rs, start=True, stop=True):
+        o = W("ps%d" % bank, 0, width(rq))
+        node("t", lambda: g.tensor.matmul_mx(ap(o), ap(lq), ap(ls), ap(rq), ap(rs), start, stop), [lq, ls, rq, rs], [o], 60 + 0.63 * (width(rq) + 16), chain=not start)
 
-    def dmas(sem, items):
-        done, total = [], 16 * len(items)
-        totals[sem] = total
-
+    def dmas(q, sem, items):
         def side(v):
             if isinstance(v, tuple) and v[0] == "C":
-                return ap(v[1]).bitcast(dt.uint8), [N(v[1])]
-            return (ap(v), [N(v)]) if isinstance(v, (tuple, str)) else (v, [])
-        for q, out, a in items:
-            (o, ow), (i, ir) = side(out), side(a)
-            sync_for(q, ir, ow)
-            queue[q].dma_start(o, i).then_inc(T.sem[sem], 16)
-            done.append((q, ir, ow, dict(know[q])))
-        for q, ir, ow, snap in done:
-            note(q, ir, ow, sem, total, True, snap)
+                return ap(v[1]).bitcast(dt.uint8), [v[1]]
+            return (ap(v), [v]) if isinstance(v, (tuple, str)) else (v, [])
+        sides = [(side(o), side(a)) for o, a in items]
+
+        def call():
+            for (o, _w), (a, _r) in sides:
+                queue[q].dma_start(o, a).then_inc(T.sem[sem], 16)
+        node(q, call, [v for _o, a in sides for v in a[1]], [v for o, _a in sides for v in o[1]], 60.0 * len(items), "dma", LOCAL, sem=sem, total=16 * len(items))
 
     nxt, prv = T.cores[(rank + 1) % len(T.cores)], T.cores[(rank - 1) % len(T.cores)]
     a_nxt, m_nxt = topo.addr(nxt), topo.mask(core, nxt)
     e_out, e_in = len(topo.engines(core, nxt)), len(topo.engines(prv, core))
-    sent = [0]
 
-    def send(out, src, rsem, code=False):
-        sync_for("g", [N(src)], [])
-        o, i = ap(out), ap(src)
-        if code:
-            o, i = o.bitcast(dt.uint8), i.bitcast(dt.uint8)
-        g.remote_dma(o, i, T.sem[rsem], T.sem["rsend"], a_nxt[1], a_nxt[0], m_nxt)
-        sent[0] += e_out
+    def send(sem, items):
+        def call():
+            for out, src, code in items:
+                o, i = ap(out), ap(src)
+                if code:
+                    o, i = o.bitcast(dt.uint8), i.bitcast(dt.uint8)
+                g.remote_dma(o, i, T.sem[sem], T.sem["rsend"], a_nxt[1], a_nxt[0], m_nxt)
+        node("g", call, [src for _o, src, _c in items], [out for out, _s, _c in items], 400.0 * len(items), "send", REMOTE, sem=sem, total=e_in * len(items), left=e_out * len(items))
 
-    def arrival(names, sem, n):
-        totals[sem] = n
-        note("r", [], [N(v) for v in names], sem, n, True, {})
-
-    dmas("dx", [("y", "XT", T.x[:, :])])
-    dmas("du", [("s", "UT", T.u[:, :])])
-    dmas("dlb", [("ys"[t % 2], W("LBI", 0, 20, 1, 8 * y + 7 - t, 128, 16), T.nb[16 * t + 8 * y:16 * t + 8 * y + 8, :]) for y in range(2) for t in range(8)])
-    dmas("dp", [("ys"[(b + Q) % 2], W("PI", 0, 32, 1, 32 * Q + b, 32 * Q + 32, 4), T.p[15 - 4 * b - Q:128:16, :]) for Q in range(4) for b in range(4)])
-    dmas("dnb", [("ys"[k % 2], W("NBD", 20 * k, 20 * k + 20, 1, 8 * y, 8 * y + 8), T.nb[2 * k + y:128:16, :]) for k in range(8) for y in range(2)])
-    dmas("dnl", [("y", W("NBI", 0, 160, 1, 16 * k, 16 * k + 16), W("NBD", 0, 160, 1, 0, 16)) for k in range(8)])
-    dmas("dw", [("y", ("C", "wq"), T.wc[:, :]), ("y", "wsc", T.ws[:, :])])
-    dmas("dv", [("y", "VT", T.v[:, :])])
-
-    fill("BY", 0.0)
-    for k in range(8):
-        for y in range(2):
-            fill(W("BY", 64 * k + 33 * y, 64 * k + 32 * y + 32, 4), 1.0)
-    fill("ULU", 0)
-    fill("DT", 0.0)
-    iota(W("PCI", 0, 1), [[0, 1]], 0, 1)
-    iota(W("IOTA", 0, 320), [[1, 320]], 0, 0)
-    for e in (0, 7):
-        select("CB%d" % e, "BY", [[0, 16], [-16, 8], [0, 4]], 0 if e == 0 else -8, 1)
-    iota("CI", [[0, 32], [-1, 16]], 16, 1)
-    iota("CIDX", [[16, 20]], -1, 0)
-    for Q in range(4):
-        iota(W("JK", 0, 4, 1, 32 * Q, 32 * Q + 32), [[-4, 4]], 7 * 512 + 15 - Q, 16)
-    iota("CE", [[16, 32]], 128, 0)
-    iota("CJ", [[16, 32]], 15, 0)
-
-    def later_constants():
-        for b in range(4):
-            select("CT%d" % b, "ON", [[1, 512]], -b, -4)
-        iota(W("LOWC", 0, 336), [[1, 336]], 512 * 1024 + 640, 0)
-        iota(W("LOWC", 336, 672), [[1, 336]], 512 * 1024 + 640, 0)
-        iota("PLC", [[16384, 32], [-1024, 16]], 15 * 1024, 0)
-        iota("IO512", [[512, 320]], 0, 0)
-        iota(W("IOTA", 320, 4096), [[1, 3776]], 320, 0)
+    dmas("y", "dx", [("XT", T.x[:, :])])
+    dmas("s", "du", [("UT", T.u[:, :])])
+    for y in range(2):
+        dmas("ys"[y], "dl%d" % y, [(W("LBI", 0, 20, 1, 8 * y + t, 128, 16), T.nb[16 * t + y:16 * t + 16:2, :]) for t in range(8)])
+    dmas("y", "dn", [(W("NBI", 0, 160, 1, 16 * k, 16 * k + 16), T.nb[:, :]) for k in (0, 1, 6, 7)])
+    for e in range(2):
+        dmas("ys"[e], "dp%d" % e, [(W("PI", 16 * par, 16 * par + 16, 1, 32 * a + 16 * e, 32 * a + 16 * e + 16),
+                                    T.p[32 * a + 16 * par:32 * a + 16 * par + 16, 16 * e:16 * e + 16]) for a in range(4) for par in range(2)])
+    dmas("y", "dw", [(("C", "wq"), T.wc[:, :]), ("wsc", T.ws[:, :])])
+    dmas("y", "dv", [("VT", T.v[:, :])])
 
     pc, pf = (lambda i: W("PCI", i, i + 1)), (lambda i: W("PCF", i, i + 1))
+    iota(pc(0), [[0, 1]], 0, 1)
     ts(pc(1), pc(0), 15, bw)
     ts(pc(2), pc(0), 3, shr, 1, bw)
-    cp(pf(0), pc(1))
-    cp(pf(1), pc(2))
-    ts(W("ULU", 0, 8), W("ULU", 8, 16), pf(1), add, 112.0, mul)
-    for k in range(1, 8):
-        fill(W("ULU", 8 + 8 * k, 16 + 8 * k), 16 * k)
+    ts(pc(3), pc(0), 4, shr, 1, bw)
+    ts(pc(4), pc(0), 7, bw)
+    cp(W("PCF", 0, 5), W("PCI", 0, 5))
+    cq, ch, ce, c7 = pf(1), pf(2), pf(3), pf(4)
+    iota(W("ULF", 0, 8), [[0, 8]], 112, 0)
+    iota(W("ULF", 8, 24), [[16, 2], [32, 4], [0, 2]], 0, 0)
+    ts(W("ULU", 0, 8), W("ULF", 0, 8), ch, mul)
+    cp(W("ULU", 8, 24), W("ULF", 8, 24))
     quant("uq", "us", "UT")
-
-    def pick_u(a, b):
-        ul, o = W("ULU", a // 16, b // 16), W("ur", a, b)
-        op("v", lambda: g.vector.tensor_copy(ap(o).bitcast(dt.uint32), ap("uq").bitcast(dt.uint32).indirect(ap(ul))), ["uq", ul], [o])
-        act(W("urs", a, b), I("us", ul))
-    pick_u(0, 128)
+    node("v", lambda: g.vector.tensor_copy(ap("ur").bitcast(dt.uint32), ap("uq").bitcast(dt.uint32).indirect(ap("ULU"))), ["uq", "ULU"], ["ur"], 530.0)
+    act("urs", I("us", "ULU"))
     quant("mq0", "ms0", "XT")
-    pick_u(128, 1152)
-    for e in (0, 7):
-        quant("bq%d" % e, "bs%d" % e, "CB%d" % e)
-    fill("ONES", 1.0)
-    fill("ON", 1.0)
+    ZERO = 2048
+    iota(W("IOTA", 1888, 2688), [[1, 800]], 1888 - ZERO, 0)
+    iota(W("IOTA", 0, 1888), [[1, 1888]], -ZERO, 0)
+    iota(W("IOTA", 2688, 4096), [[1, 1408]], 2688 - ZERO, 0)
+    CELLS, CELLM, COLS = W("IOTA", ZERO, ZERO + 320), W("IOTA", ZERO - MID, ZERO - MID + 320), W("IOTA", ZERO, ZERO + 640)
+    fill("BY", 0.0)
+    for k in (0, 1, 6, 7):
+        fill(W("BY", k, 128, 8), 2.0)
+    fill(W("CB", 128, 384), 0.0)
+    for e in range(2):
+        select(W("CB", 384 * e, 384 * e + 128), "BY", [[0, 2], [-16, 8], [0, 8]], -8 * e, 1)
+    quant("bq", "bs", "CB")
+    fill("DT", 0.0)
+    fill("ZT", 0.0)
+    quant(W("dq", 128, 256), W("dsc", 128, 256), "ZT")
+    fill("K8", 0.0)
+    fill(W("K8", 0, 320, 8), -FAR)
     cp("LB", "LBI")
-    ts("TR", "PI", float(BIAS), add)
-    CELLS, CELLS8 = W("IOTA", 0, 320), W("IOTA", BIAS, BIAS + 320)
-
-    def more_constants():
-        cp("NBL", "NBI")
-        act(W("NB8", 0, 1600), I(CELLS, W("NBL", 0, 100)))
-        for k in ("KEEP", "KEEPB"):
-            fill(k, 1.0)
-        ts("CI", "CI", 15, bw)
-        for k in ("KEEP", "KEEPB"):
-            fill(W(k, 0, 512, 16), 0.0)
-        ts("MASK", "CI", 0.0, eq)
-        ts("CE", "CE", pf(0), add)
-        ts(pc(2), pc(1), 1, shr)
-        ts(pc(3), pc(1), 1, bw)
-        fill("DB", 0.0)
-        ts(pf(2), pc(2), 320.0, mul)
-        ts(pf(3), pc(3), 8.0, mul)
-        for k in (0, 2880):
-            fill(W("ST", k, k + 320), 0.0)
-        ts("CIDX", "CIDX", pf(2), add, pf(3), add)
-        ts(pf(0), pf(0), 320.0 + BIAS, add)
-        cp(W("NB8", 1600, 2560), I(CELLS, W("NBL", 100, 160)))
-
-    def last_constants():
-        for b in range(4):
-            quant("eq%d" % b, "es%d" % b, "CT%d" % b)
-        for k in range(8):
-            ts(W("JKN", 4 * k, 4 * k + 4), "JK", -1.0 / 512, mul)
-        fill("HN", -511.0)
-        fill(W("HN", 3, 32, 4), 0.0)
-
-    def end_constants():
-        quant("vq", "vs", "VT")
-        ts("REVF", "CJ", pf(0), sub, 320.0 + BIAS, add)
-        cp("REV", "REVF")
+    for k in (1, 2):
+        fill(Q("NBI", k), 0)
+    cp("NBL", "NBI")
+    act(W("NB8", 0, 1280), I(CELLS, W("NBL", 0, 80)))
+    for k in range(4):
+        cp(W("NB8", 1280 + 320 * k, 1600 + 320 * k), I(CELLS, W("NBL", 80 + 20 * k, 100 + 20 * k)))
+    iota("CIDX", [[16, 20]], 0, 0)
+    ts(pf(5), c7, 320.0, mul, ch, add)
+    ts("CIDX", "CIDX", pf(5), add)
+    act(W("KT", 320, 640), CELLS)
+    iota("I16", [[0, 32], [1, 16]], 0, 0)
+    ts("MASK", "I16", cq, eq)
+    fill("KEEP", 1.0)
+    fill(W("KEEP", 0, 512, 16), 0.0)
+    fill(W("ST", 640, 960), 0.0)
+    for k in ("DE", "DO", "DL", "D0", "D0L", "ZZ", "NN"):
+        fill(k, 0.0)
+    fill("BKU", 0)
+    fill(W("D0", 3, 64, 4), -1.0)
+    fill(W("D0L", 2, 64, 4), -1.0)
+    fill(W("D0L", 3, 64, 4), 1.0)
+    ts(W("R", 0, 32), "PI", 0.0, add)
+    fill("ON", 1.0)
+    for b in range(4):
+        select("CT%d" % b, "ON", [[1, 512]], -b, -4)
+        quant("eq%d" % b, "es%d" % b, "CT%d" % b)
+    iota(Q(W("KR", 0, 16), 3), [[16, 16]], -ZERO, 1)
+    ts(pf(6), ce, 240.0, mul)
+    ts(Q(W("NN", 3, 64, 4), 3), Q(W("KR", 0, 16), 3), Q(pf(6), 3), add)
+    fill(W("CMP", 512, 513), -256.0)
+    fill(W("CMP", 513, 514), -255.0)
+    iota("CE", [[16, 32]], 128, 0)
+    ts("CE", "CE", cq, add)
+    act("ENT", W("IOTA", ZERO, ZERO + 512), 1.0 / 2048)
+    iota("RHO", [[0, 2], [1, 8]], 1, 0)
+    iota("E256", [[256, 2], [0, 8]], 15, 0)
+    ts("NF", "RHO", cq, le)
+    tt("TF", "NF", "RHO", mul)
+    ts("T2", "TF", cq, sub, -16.0, mul)
+    tt("T2", "T2", "E256", add)
+    cp("LI", "T2")
+    ts("T3", "TF", -2.0, mul)
+    tt("T3", "T3", "RHO", add)
+    ts("NF", "NF", 16.0, mul)
+    tt("T3", "T3", "NF", add)
+    ts("T3", "T3", 16.0, mul)
+    tt("T3", "T3", "E256", add)
+    cp("LJ", "T3")
+    fill("KP", 1.0)
+    fill(W("KP", 0, 256, 16), 0.0)
+    for e in range(2):
+        fill(W("KP", 128 * e + 1, 128 * e + 128, 17), 0.0)
+    ts(pf(7), cq, 17.0, mul, -17.0, add)
+    ts(pf(8), cq, -16.0, mul, 255.0, add)
+    ts(pf(9), pf(7), pf(8), mn_)
+    ts(W("LE", 0, 1), pf(9), 0.0, add)
+    ts(W("LE", 1, 2), pf(9), 128.0, add)
+    iota("DUMP", [[0, 2], [1, 16]], 640, 0)
+    fill(W("DUMP", 0, 32, 16), 0.0)
+    iota("LOWC", [[16, 20], [0, 2], [1, 16]], 3 * 1024 + 640, 0)
+    ts(pf(10), ce, 2048.0, mul)
+    ts(pf(11), ce, 2048.0, mul, 1024.0, add)
+    ts(pf(12), ce, -8192.0, mul, 8192.0, add)
+    iota("REVF", [[256, 2], [1, 16]], 0, 0)
+    ts(pf(13), cq, 16.0, mul)
+    ts("REV", "REVF", pf(13), add)
+    quant("vq", "vs", "VT")
 
     MASK, KEEP = (lambda n: W("MASK", 0, n)), (lambda n: W("KEEP", 0, n))
+    slot = lambda name, k: W(name, k, 64, 4)
+    ends = lambda name, n=256: W(name, 15, n, 16)
+    E, O = W("R", 0, 16), W("R", 16, 32)
 
-    def halfstep(par, last, fillers):
-        Y, S, oth = ("E", "SE", "O") if par == 0 else ("O", "SO", "E")
-        eb, i0, ge, kt = (0, 4, 0, "KT0") if par == 0 else (12, 0, 7, "KT7")
-        e = lambda n: W(n, eb, eb + 4)
-        m, dbv, off = e(oth), (W("DB", 0, 16) if par == 0 else W("DB", 4, 20)), 320.0 * (ge + 1)
-        cp("KOU", m)
-        ts(e("KU"), m, off, add)
-        if par == 0:
-            tt(W("KK", 4, 16), W("O", 4, 16), W("DB", 4, 16), sub)
+    def lookup(g_, s_, win, off):
+        tt(g_, I(win, off), MASK(16 * width(off)), mul)
+        scan(s_, KEEP(16 * width(off)), g_)
+
+    def other(kk, n, s3, even, ns):
+        for q in range(3):
+            cp(Q(ns, q + 1 if even else q), Q(n, q if even else q + 1))
+        for q, k in ((1, 1), (2, 2)) if even else ((0, 3),):
+            tt(Q(kk, q, k), Q(ns, q, k), Q(s3, q, k), sub)
+
+    def halfstep(h):
+        even = h % 2 == 0
+        kk, out, d1 = W("KK%d" % h, 1, 32, 2), "OUT%d" % h, ("DE", "DO", "DE", "DL")[h]
+        S = W("SI", 15, 256, 16) if even else W("SI", 271, 512, 16)
+        if h == 0:
+            y, n, s3 = E, O, "S30"
         else:
-            tt(W("KK", 0, 12), W("E", 4, 16), W("DA", 0, 12), sub)
-        tt("PR", "DA", dbv, mul)
-        ts("E4", e("DA"), 0.0, ne, FAR, mul)
-        tt("GK", I(kt, "KOU"), MASK(64), mul)
-        for i in range(i0 // 4, i0 // 4 + 3):
-            ts(W("KU", 4 * i, 4 * i + 4), W("KK", 4 * i, 4 * i + 4), 320.0 * (2 * i + par + 1), add)
+            before = "OUT%d" % (h - 1)
+            y, n, s3 = slot(("DE", "DO", "DE")[h - 1], 3), slot(before, 2), slot(before, 3)
+            end = 0 if even else 3
+            other(kk, n, s3, even, W("R", 48, 64) if h == 3 else "NS")
+            ts(Q(W("ZZ", 1, 32, 2), end), Q(s3, end), 0.0, eq)
+            scan(Q("KK%d" % h, end), Q("ZZ", end), Q(W(before, 0, 64, 2), end))
+            cp("KU", kk)
+        tt("GS", I(W("ST", 0, 640) if even else W("ST", 320, 960), "KU"), MASK(256), mul)
+        sm, sy, sn = (slot(d1, 1), slot(d1, 2), slot(d1, 3)) if h < 3 else (slot(d1, 0), slot(d1, 1), slot(d1, 2))
+        tt("DC", kk, n, sub)
+        tt("PR", "DC", s3, mul)
         ts("NV", "PR", 0.0, ne, FAR, mul)
-        tt("SYE", e(S), "E4", add)
-        scan("SK", KEEP(64), "GK")
-        tt("GS", I("ST", "KU"), MASK(256), mul)
-        tt("SM", *(("DA", dbv) if par == 0 else (dbv, "DA")), sub)
         tt("SYV", S, "NV", add)
-        for f in fillers:
-            f()
-        k0, sk, sb = W("SK", 15, 64, 16), W("SS", 15, 256, 16), W("SB", 15, 64, 16)
-        ts("KU2", k0, off, add)
+        tt(sm, kk, y, sub)
+        cp(sy, y)
+        cp(sn, n)
+        if h == 1:
+            ts(Q("BKU", 0), Q(n, 0), 0.0, add)
+            ts(Q("BKU", 3), Q(kk, 3), 0.0, add)
+            lookup("GK", "SK1", "KT", "BKU")
+            tt(Q(slot("DO", 0), 0), Q(ends("SK1"), 0), Q(n, 0), sub)
+            tt(Q("BA", 3), Q(ends("SK1"), 3), Q(ends("SK0"), 3), sub)
+        if h == 3:
+            cp(E, n)
+            tt(Q(slot("DL", 3), 0, 3), Q(W("R", 48, 64), 0, 3), Q(n, 0, 3), sub)
+            cp(Q(W("R", 48, 64), 3), Q(n, 3))
         scan("SS", KEEP(256), "GS")
-        tt("KD", k0, m, sub)
-        tt("GB2", I("ST", "KU2"), MASK(64), mul)
-        tt("GT", sk, "SYV", gt)
-        scan("SB", KEEP(64), "GB2")
-        tt("GD", "GT", "SM", mul)
-        tt("GTB", sb, "SYE", gt)
-        if last and par == 1:
-            for i in (3, 0, 1, 2):
-                tt(W("R", 8 * i + 4, 8 * i + 8), W("O", 4 * i, 4 * i + 4), W("GD", 4 * i, 4 * i + 4), add)
-        else:
-            tt(Y, Y, "GD", add)
-            tt("DA", "DA", "GD", sub if par == 0 else add)
-            if par == 0:
-                tt(W("DB", 4, 16), W("DB", 4, 16), W("GD", 4, 16), add)
-            else:
-                tt(W("DB", 4, 16), W("DB", 4, 16), W("GD", 0, 12), sub)
-        tt("G2", "GTB", "KD", mul)
-        if not last:
-            tt("SG1", sk, "NV", sub)
-            tt("SG2", sb, "E4", sub)
+        d0 = slot("D0", 2) if h < 3 else slot("D0L", 1)
+        tt(d0, ends("SS"), "SYV", gt)
+        scan(out, "D0" if h < 3 else "D0L", d1)
+        if h < 2:
+            tt("SG1", ends("SS"), "NV", sub)
             tt(S, S, "SG1", mx_)
-        if last and par == 1:
-            tt(W("R", 28, 32), W("R", 28, 32), "G2", add)
-        else:
-            tt(e("DA"), e("DA"), "G2", sub if par == 0 else add)
-            tt(e(Y), e(Y), "G2", add)
-        if not last:
-            tt(e(S), e(S), "SG2", mx_)
+        if h == 1:
+            tt(Q("BC", 3), Q("BA", 3), Q(d0, 3), mul)
+            tt(Q("BC", 3), Q("BC", 3), Q(ends("SK0"), 3), add)
+            tt(Q(slot("DE", 0), 3), Q("BC", 3), Q(slot(out, 2), 3), sub)
 
     for rd in range(ROUNDS):
-        mq, ms, lq, ls, sl, ar = "mq%d" % rd, "ms%d" % rd, "lq%d" % rd, "ls%d" % rd, "SL%d" % rd, "AR%d" % rd
-        send(lq, mq, "rq%d" % rd, True)
-        send(ls, ms, "rq%d" % rd)
-        arrival([lq, ls], "rq%d" % rd, 2 * e_in)
-        if rd == 0:
-            later_constants()
-        mm(0, "ur", "urs", 0, mq, ms)
-        for k in range(8):
-            mm((k + 1) % 8, "ur", "urs", 128 + 128 * k, mq, ms)
-            if k == 0:
-                act("W07", W("ps0", 0, 320))
-            act(W("ST", 320 * k + 320, 320 * k + 640), W("ps%d" % ((k + 1) % 8), 0, 320))
-        tr("RB", "TR")
-        for i in range(4):
-            for par in range(2):
-                src = W("RB", 8 * i + 4 * par, 8 * i + 4 * par + 4)
-                ts(W("OFFI", 16 * par + 4 * i, 16 * par + 4 * i + 4), src, 320.0 * (2 * i + par + 1) - BIAS, add)
-                ts(W("EO"[par], 4 * i, 4 * i + 4), src, -float(BIAS), add)
+        mq, ms, fw, msg = "mq%d" % rd, "ms%d" % rd, "FW%d" % rd, "MSG%d" % rd
+        ts(W("OFFI", 0, 16), E, 0.0, add)
+        ts(W("OFFI", 16, 32), O, 320.0, add)
+        tt("S30", E, O, sub)
+        kk0 = W("KK0", 1, 32, 2)
+        other(kk0, O, "S30", True, "NS")
+        cp(Q("KU", 1), Q(kk0, 1))
+        cp(Q("KU", 2, 2), Q(kk0, 2, 2))
+        ts(Q("NZ", 0), Q("S30", 0), 0.0, ne, 320.0, mul)
+        tt(Q("BL", 0), Q("NZ", 0), Q(O, 0), add)
+        cp(Q("BKU", 0), Q("BL", 0))
+        cp(Q("BKU", 3), Q(O, 3))
+        for k in range(3):
+            mm(k, W("ur", 128 * k, 128 * k + 128), W("urs", 128 * k, 128 * k + 128), mq, ms)
+        act("W07", W("ps0", 0, 320))
+        cp(W("ST", 0, 320), W("ps1", 0, 320))
+        act(W("ST", 320, 640), W("ps2", 0, 320))
         cp("GB", I("W07", "LB"))
-        tt("M1", W("GB", 0, 320, 2), W("GB", 1, 320, 2), mx_)
-        tt("M2", W("M1", 0, 160, 2), W("M1", 1, 160, 2), mx_)
-        tt("M3", W("M2", 0, 80, 2), W("M2", 1, 80, 2), mx_)
-        for t in range(8):
-            tt(W("NE8", t, 320, 8), W("GB", t, 320, 8), "M3", ne)
-        scan("SC8", "NE8", "ONES")
-        cp(W("DT", 0, 80, 4), W("SC8", 7, 320, 16))
-        cp(W("DT", 1, 80, 4), W("SC8", 15, 320, 16))
-        quant("dq", "dsc", "DT")
-        mm(1, "bq0", "bs0", 0, "dq", "dsc")
-        mm(2, "bq7", "bs7", 0, "dq", "dsc")
-        if rd == 0:
-            more_constants()
-        tt("GI", I("ST", "OFFI"), "MASK", mul)
-        tt(W("BI", 0, 20), W("ps1", 0, 20), "CIDX", add)
-        tt(W("BI", 20, 40), W("ps2", 0, 20), "CIDX", add)
+        scan("RM", "K8", "GB", add, mx_)
+        for t in range(7):
+            at = 80 * (t // 2) + t % 2
+            tt(W("DT", at, at + 79, 2), W("RM", t, 320, 8), W("RM", 7, 320, 8), ne)
+        quant(W("dq", 0, 128), W("dsc", 0, 128), "DT")
+        for k in range(4):
+            mm(3, "bq", "bs", W("dq", 20 * k, 20 * k + 128), W("dsc", 20 * k, 20 * k + 128), k == 0, k == 3)
+        tt("BI", W("ps3", 0, 20), "CIDX", add)
         cp("BIU", "BI")
-        act("KT0", I("NB8", W("BIU", 0, 20)))
-        act("KT7", I("NB8", W("BIU", 20, 40)))
-        scan("SI", "KEEP", "GI")
-        tt("DA", "O", "E", sub)
-        tt(W("DB", 4, 16), W("E", 4, 16), W("O", 0, 12), sub)
-        cp("SE", W("SI", 15, 256, 16))
-        cp("SO", W("SI", 271, 512, 16))
-        halfstep(0, False, [])
-        if rd == 0:
-            last_constants()
+        act(W("KT", 0, 320), I("NB8", "BIU"))
+        lookup("GK", "SK0", "KT", "BKU")
+        cp(Q("KU", 0), Q(ends("SK0"), 0))
+        cp(Q(kk0, 0), Q(ends("SK0"), 0))
+        tt(Q(slot("DE", 0), 3), Q(ends("SK0"), 3), Q(O, 3), sub)
+        lookup("GI", "SI", W("ST", 0, 640), "OFFI")
         for t in range(4):
-            f = W("ps%d" % (3 + t), 0, 320)
-            mm(3 + t, "eq%d" % t, "es%d" % t, 0, mq, ms)
+            f = W("ps%d" % (4 + t), 0, 320)
+            mm(4 + t, "eq%d" % t, "es%d" % t, mq, ms)
             act("FQ%d" % t, f, 0.25)
             act("FH%d" % t, f, 0.5)
             act(W("YW%d" % t, 640, 960), f, 0.5)
-        act("LOWA", "LOWC")
-        act("LOWB", "LOWC")
-        for t in range(4):
-            k = (7, 0, 1, 2)[t]
-            mm(k, "eq%d" % t, "es%d" % t, 0, lq, ls)
-            act("PF%d" % t, W("ps%d" % k, 0, 320), 0.5)
-        halfstep(1, False, [])
-        halfstep(0, True, [])
-        halfstep(1, True, [lambda i=i: cp(W("R", 8 * i, 8 * i + 4), W("E", 4 * i, 4 * i + 4)) for i in range(4)] + [lambda: cp(W("R", 32, 36), W("E", 12, 16))])
-        tt("NE", W("R", 0, 28), W("R", 4, 32), ne)
-        tr(W("TA", 0, 32), W("R", 0, 32))
-        tr(W("TA", 32, 64), W("R", 4, 36))
-        for b in range(4):
-            red(W("D4", b, b + 1), W("NE", b, 28, 4))
-        for b in range(4):
-            ts(W("KR", b, 32, 4), W("JKN", b, 32, 4), W("D4", b, b + 1), add, -512.0, mul)
-        tr(W("TA", 64, 96), "KR")
-        ts("NK", W("KR", 0, 4), -1.0, mul)
-        cp("TU", "TA")
-        dmas("da%d" % rd, [("ys"[Q % 2], W("AL", 0, 96, 1, Q, 128, 4), W("TU", 0, 96, 1, 32 * Q, 32 * Q + 32)) for Q in range(4)])
-        if rd == 0:
-            end_constants()
-        al, bl, kl = W("AL", 0, 32), W("AL", 32, 64), W("AL", 64, 96)
-        cp("RK", I("IOTA", kl))
+        act(W("LA", 0, 640), "LOWC", bias=pf(12))
+        act(W("LBW", 0, 640), "LOWC", bias=8192.0)
+        for h in range(4):
+            halfstep(h)
+        cp(O, slot("OUT3", 1))
+        cp(W("R", 32, 48), slot("OUT3", 1))
+        tr("TA", "R")
+        cp("AL", "TA")
+        al, bl = W("AL", 0, 32), W("AL", 32, 64)
+        ts(Q("NN", 0, 3), Q("OUT3", 0, 3), 0.0, eq, 512.0, mul)
+        ts(Q(slot("NN", 2), 3), Q(slot("OUT3", 2), 3), 0.0, eq, 512.0, mul)
+        tt(Q("S1", 0, 2), Q("NN", 0, 2), Q("NN", 2, 2), add)
+        tt(Q("S2", 0), Q("S1", 0), Q("S1", 1), add)
+        for k in range(2):
+            tt(Q(W("KD", 16 * k, 16 * k + 16), 0), Q(slot("S2", 2), 0), Q(slot("S2", 3), 0), add)
+        tr(Q("KR", 0), Q("KD", 0))
+        for q in range(4):
+            ts(Q("KL", q), Q("KR", 0), float(ZERO), add)
+            act(Q("NK", q), Q(W("KD", 4 * q, 4 * q + 4), 0))
+        act("RK", I("IOTA", "KL"))
         for b in range(3):
-            bi, ac = W("NK", b, b + 1), W("PS", b, b + 1)
-            op("s", lambda: g.scalar.activation(ap("SG"), ap("RK"), ACT.Sign, bias=ap(bi), accum_out=ap(ac)), ["RK", bi], ["SG", ac])
-        act(W("FW", 128, 640), I(CELLS8, al))
-        ts("CMP", "RK", W("KR", 3, 4), lt, -2.0, mul)
+            act(("SG0", "SG1B", "SG2")[b], "RK", -1.0, W("NK", b, b + 1), ACT.Sign, W("PS", b, b + 1))
+        ts(W("CMP", 0, 512), "RK", W("NK", 3, 4), lt, 2.0, mul)
         red(W("PS", 3, 4), "CMP")
-        for b in range(4):
-            ts(W("PP", b, 32, 4), W("HN", b, 32, 4), W("PS", b, b + 1), add, -0.5, mul)
-        tr("PT", "PP")
-        cp("PU", "PT")
-        dmas("db%d" % rd, [("y", W("PA", 0, 32, 1, Q, 128, 4), W("PU", 0, 32, 1, 32 * Q, 32 * Q + 32)) for Q in range(4)])
-        tt("DP", I("IO512", bl), W("FW", 128, 640), add)
+        for q in range(4):
+            ts(Q(W("PP", 4 * q, 4 * q + 4), 0), Q("PS", q), 511.0, add, 0.5, mul)
+            act(Q(W("PP", 16 + 4 * q, 20 + 4 * q), 0), Q("PS", q), 0.5, 255.5)
+        tr(Q("PT", 0), Q("PP", 0))
+        for q in range(4):
+            cp(Q("PA", q), Q("PT", 0))
+        tt("DP", I(CELLM, al), "ENT", add)
+        cp(I("SRT", "PA"), "DP")
+        ts(msg, W("SRT", 0, 128), ROUND, add, ROUND, sub)
+        send("rl%d" % rd, [(W(fw, 0, 128), msg, False)])
+        act(W(fw, 128, 640), I(CELLM, al))
         for t in range(4):
             act("ZG%d" % t, I("FQ%d" % t, al))
-
-        def bonds(t):
             tt(W("YW%d" % t, 128, 640), I("FQ%d" % t, bl), "ZG%d" % t, add)
-        bonds(0)
-        bonds(1)
-        cp(I("SRT", "PA"), "DP")
-        cp("PF32", "PA")
         tt("G8", W("SRT", 0, 128), MASK(128), mul)
-        ts("ISL", "PF32", 128.0, lt)
         scan("S8", KEEP(128), "G8")
-        tt("PD", "PF32", "CE", sub)
-        cp("P8", W("S8", 15, 128, 16))
-        tt("PM", "PD", "ISL", mul)
-        ts("P8A", "P8", 511, bw)
-        ts("P8B", "P8", 9, shr)
-        tt("SELF", "PM", "CE", add)
-        ts(W(sl, 0, 8), "P8A", -float(BIAS), add)
-        cp(W(sl, 8, 16), "P8B")
-        cp("SEL", "SELF")
-        send(ar, sl, "rl%d" % rd)
-        arrival([ar], "rl%d" % rd, e_in)
-        tt("SELX", I("IOTA", "SEL"), "PLC", add)
-        bonds(2)
-        bonds(3)
-        aa, ab = W(ar, 0, 8), W(ar, 8, 16)
-        cp(W("FW", 0, 128), I(CELLS8, aa))
+        ts("E1", ends("S8", 128), ROUND, add, ROUND, sub)
+        tt("E2", ends("S8", 128), "E1", sub)
+        ts("EL2", "E2", 2048.0, mul)
         for t in range(4):
-            act(W("HG", 128 * t, 128 * t + 128), I("PF%d" % t, aa))
-        act("FX", I("FW", "SEL"))
-        tt("FM", I("FW", "SEL"), "MASK", mul)
-
-        def arrived(t):
-            tt(W("HT", t, 512, 4), I("PF%d" % t, ab), W("HG", 128 * t, 128 * t + 128), add)
-        arrived(0)
-        scan("SCN", "KEEP", "FM")
-        arrived(1)
-        tt("EQB", "FX", "SCN", eq)
-        cp("FC", W("SCN", 15, 512, 16))
-        if rd + 1 < ROUNDS:
-            dmas("dc%d" % rd, [("y", W("TR", 0, 32, 1, 32 * Q, 32 * Q + 32), W("FC", 0, 32, 1, Q, 128, 4)) for Q in range(4)])
-        arrived(2)
-        scan("CNT", "KEEPB", "EQB")
-        arrived(3)
-        ts("LZ", W("CNT", 15, 512, 16), 1.5, gt, pf(0), mul)
-        quant("aq", "asc", "HT")
-        tt("OF", "FC", "LZ", mx_)
+            act(W("HT", t, 512, 4), I(W("YW%d" % t, 128, 640), "EL2"), 2.0)
+        aq, asc, lq, ls = "aq%d" % rd, "as%d" % rd, "lq%d" % rd, "ls%d" % rd
+        quant(aq, asc, "HT")
+        send("rq%d" % rd, [(lq, aq, True), (ls, asc, False)])
         for b in range(4):
-            mm(3 + b, "wq", "wsc", 128 * b, "aq", "asc")
-            act(W("YW%d" % b, 0, 128), W("ps%d" % (3 + b), 0, 128), 2.0 ** -6)
-        if rd + 1 == ROUNDS:
-            fr = I("FX", "REV")
-            op("s", lambda: g.scalar.activation(ap("FXR"), ap(fr), ACT.Identity, bias=-float(BIAS)), [fr], ["FXR"])
-            dmas("dad", [("y", T.ad[:, :], W("FXR", 0, 512, 1, 0, 128, 16))])
-        ts(W("OFF", 0, 32, 2), W("OF", 0, 32, 2), -float(BIAS), add)
-        ts(W("OFF", 1, 32, 2), W("OF", 1, 32, 2), 336.0 - BIAS, add)
-        for k in range(15, -1, -1):
-            cp(I("LOWA" if k % 2 else "LOWB", W("OFF", 2 * k, 2 * k + 2)), W("SELX", 32 * k, 32 * k + 32))
-        for i in range(2):
-            tt(W("LO1", 320 * i, 320 * i + 320), W("LOWA", 336 * i, 336 * i + 320), W("LOWB", 336 * i, 336 * i + 320), mn_)
-        tt("LO2", W("LO1", 0, 320), W("LO1", 320, 640), mn_)
-        tt("XE", "LO2", MASK(320), mul)
-        scan("XS", KEEP(320), "XE")
-        cp("XI", W("XS", 15, 320, 16))
-        ts("XJ", "XI", 1023, bw)
-        cp("EL", "XJ")
+            mm(4 + b, W("wq", 128 * b, 128 * b + 128), W("wsc", 128 * b, 128 * b + 128), lq, ls)
+            act(W("YW%d" % b, 0, 128), W("ps%d" % (4 + b), 0, 128), 2.0 ** -6)
+        cp("PF", "PA")
+        ts("T1", "PA", 128.0, ge, 1024.0, mul)
+        tt("TM", "T1", "PF", mx_)
+        tt("SELF", "TM", "CE", mn_)
+        cp("SEL", "SELF")
+        tr("VT_", "SELF")
+        for par in range(2):
+            cp(W("VL", par, 32, 2), W("VT_", 16 * par, 16 * par + 16))
+        for w in range(2):
+            act(W("SELX", 256 * w, 256 * w + 256), I(COLS, W("VL", 16 * w, 16 * w + 16)), bias=pf(10 + w))
+        tt("FM", I(fw, "SEL"), "MASK", mul)
+        scan("SCN", "KEEP", "FM")
+        cp("PA_", I("SCN", "LI"))
+        act("PB_", I("SCN", "LJ"))
+        tt("EQ", "PA_", "PB_", eq)
+        scan("EQS", "KP", "EQ", mul, mx_)
+        tt("LZD", I("EQS", "LE"), "DUMP", mul)
+        ts("FCI", ends("SCN", 512), float(MID), add)
+        ts("FA", "FCI", 496, bw)
+        tt("PP_", "FA", "FCI", add)
+        tt("OF", "PP_", "LZD", mx_)
+        tr("OT", "OF")
+        for par in range(2):
+            ts(W("OFF", par, 32, 2), W("OT", 16 * par, 16 * par + 16), 16.0 * par, add)
+        if rd + 1 < ROUNDS:
+            ts("FCF", ends("SCN", 512), float(MID), add)
+            tr(W("R", 0, 32), "FCF")
+        else:
+            act("FX", I(fw, "SEL"), bias=float(MID))
+            act("FXR", I("FX", "REV"))
+            dmas("y", "dad", [(T.ad[:, :], W("FXR", 0, 512, 1, 0, 128, 16))])
+        for y in range(7, -1, -1):
+            for w in (1, 0):
+                k = 8 * w + y
+                cp(I("LA" if w else "LBW", W("OFF", 2 * k, 2 * k + 2)), W("SELX", 32 * k, 32 * k + 32))
+        tr("TLA", W("LA", 0, 640))
+        tr("TLB", W("LBW", 0, 640))
+        tt("M1", W("TLA", 0, 640, 16), W("TLB", 0, 640, 16), mn_)
+        tt("M2", W("M1", 0, 40, 2), W("M1", 1, 40, 2), mn_)
+        ts("M3", "M2", 1023, bw)
+        cp("EL", "M3")
         for t in range(4):
             tt(W("MT", t, 1280, 4), I("YW%d" % t, "EL"), "FH%d" % t, add)
         quant("mq%d" % (rd + 1), "ms%d" % (rd + 1), "MT")
 
     mq, ms = "mq%d" % ROUNDS, "ms%d" % ROUNDS
-    mm(0, "vq", "vs", 0, mq, ms)
+    mm(0, "vq", "vs", mq, ms)
     act("YO", W("ps0", 0, 320))
-    dmas("doc", [("y", T.oc[:, :], ("C", mq))] + [("y", T.osc[4 * k:4 * k + 4, :], W(ms, 0, 320, 1, 32 * k, 32 * k + 4)) for k in range(4)])
-    dmas("dy", [("s", T.y[:, :], "YO")])
+    dmas("y", "doc", [(T.oc[:, :], ("C", mq))] + [(T.osc[4 * k:4 * k + 4, :], W(ms, 0, 320, 1, 32 * k, 32 * k + 4)) for k in range(4)])
+    dmas("s", "dy", [(T.y[:, :], "YO")])
 
-    g.wait_ge(T.sem["rsend"], sent[0])
+    seen = {}
+    for i, n in enumerate(nodes):
+        n["pre"], n["post"] = set(), []
+        for v, w in [(v, False) for v in n["rd"]] + [(v, True) for v in n["wr"]]:
+            n["pre"].update(h["i"] for h in seen.get(v[0], ()) if clash(v, w, n["q"], h))
+        for v, w in [(v, False) for v in n["rd"]] + [(v, True) for v in n["wr"]]:
+            old = seen.setdefault(v[0], [])
+            if w:
+                old[:] = [h for h in old if not covers(v, h["v"])]
+            old.append({"v": v, "w": w, "q": n["q"], "i": i})
+        n["pre"].discard(i)
+        for j in n["pre"]:
+            nodes[j]["post"].append(i)
+    for n in reversed(nodes):
+        n["way"] = n["busy"] + n["after"] + max([WAKE + nodes[j]["way"] for j in n["post"]] or [0.0])
+    free = {q: 0.0 for q in queue}
+    left = [len(n["pre"]) for n in nodes]
+    ready = {i: 0.0 for i, n in enumerate(nodes) if not n["pre"]}
+    order = []
+    while ready:
+        picks = []
+        for q in queue:
+            mine = [i for i in ready if nodes[i]["q"] == q]
+            if not mine:
+                continue
+            best = max(mine, key=lambda i: (nodes[i]["way"], -i))
+            start = max(free[q], ready[best])
+            for i in sorted(mine, key=lambda i: (-nodes[i]["way"], i)):
+                at = max(free[q], ready[i])
+                first = max(max(start, at + nodes[i]["busy"]) + nodes[best]["way"], at + nodes[i]["way"])
+                second = max(start + nodes[best]["way"], start + nodes[best]["busy"] + nodes[i]["way"])
+                if i != best and at < start and first <= second:
+                    best, start = i, at
+                    break
+            picks.append((start, best))
+        start, i = min(picks)
+        n = nodes[i]
+        del ready[i]
+        order.append(i)
+        free[n["q"]] = start + n["busy"] + (WAKE if n.get("drain") else 0.0)
+        n["done"] = start + n["busy"] + n["after"]
+        for j in n["post"]:
+            left[j] -= 1
+            if left[j] == 0:
+                ready[j] = max(nodes[k]["done"] + (0.0 if nodes[j].get("chain") and nodes[k]["q"] == "t" else WAKE) for k in nodes[j]["pre"])
+
+    count, know, totals, sent = {k: 0 for k in own}, {k: {} for k in queue}, {}, 0
+    drain = False
+    for i in order:
+        n = nodes[i]
+        q = n["q"]
+        todo = {}
+        for j in n["pre"]:
+            m = nodes[j]
+            if n.get("chain") and m["q"] == "t":
+                continue
+            if know[q].get(m["sig"], 0) < m["val"] and todo.get(m["sig"], {"val": 0})["val"] < m["val"]:
+                todo[m["sig"]] = m
+        for m in sorted(todo.values(), key=lambda m: -m["at"]):
+            if know[q].get(m["sig"], 0) < m["val"]:
+                queue[q].wait_ge(T.sem[m["sig"]], m["val"])
+                for s, x in m["snap"].items():
+                    know[q][s] = max(know[q].get(s, 0), x)
+                know[q][m["sig"]] = m["val"]
+        if n["kind"] == "op":
+            if (q == "g" or (q == "v" and drain)) and know[q].get(own[q], 0) < count[q]:
+                queue[q].wait_ge(T.sem[own[q]], count[q])
+                know[q][own[q]] = count[q]
+            if q == "v":
+                drain = n.get("drain")
+            count[q] += 1
+            n["call"]().then_inc(T.sem[own[q]], 1)
+            n["sig"], n["val"], n["snap"] = own[q], count[q], dict(know[q])
+        else:
+            n["call"]()
+            totals[n["sem"]] = n["total"]
+            sent += n.get("left", 0)
+            n["sig"], n["val"], n["snap"] = n["sem"], n["total"], dict(know[q]) if n["kind"] == "dma" else {}
+        n["at"] = len(totals) + sum(count.values())
+
+    g.wait_ge(T.sem["rsend"], sent)
     for q in own:
         g.wait_ge(T.sem[own[q]], count[q])
     for s in sorted(totals):

@@ -36,17 +36,17 @@ _sb(U8, as0=128, as1=128, as2=128, ls0=128, ls1=128, ls2=128)
 _pack("eqc", MXC, eq0=128, eq1=128, eq2=128, eq3=128)
 _pack("esc", U8, es0=128, es1=128, es2=128, es3=128)
 _sb(F32, IOTA=4096, LOWC=640, ENT=512)
-_sb(BF, MASK=512, KEEP=512, I16=512, KP=256)
-_pack("KC", F32, PCF=16, CE=32, CIDX=20, ULF=24, RHO=16, E256=16, NF=16, TF=16, T2=16, T3=16, DUMP=32, REVF=32, LEF=2)
+_sb(BF, MASK=512, KEEP=512, I16=512, KP=128, G2=320, G3=320)
+_pack("KC", F32, PCF=16, CE=32, CIDX=20, ULF=24, NF=8, TF=8, T2=8, T3=8, REVF=32)
 _sb(I32, PCI=8, LBI=20, NBI=160, PI=32)
-_pack("KU16", U16, ULU=24, LB=20, NBL=160, LI=16, LJ=16, LE=2, REV=32)
+_pack("KU16", U16, ULU=24, LB=20, NBL=160, LI=8, LJ=8, LE=2, REV=32)
 _sb(F32, ST=960, NB8=2560, KT=640, YO=320)
 _pack("HB", F32, R=64, S30=16, NS=16, NZ=16, BL=16, DE=64, DO=64, DL=64, D0=64, D0L=64, OUT0=64, OUT1=64, OUT2=64, OUT3=64, ZZ=32, KK0=32, KK1=32,
-      KK2=32, KK3=32, DC=16, PR=16, NV=16, SYV=16, SG1=16, BA=16, BC=16, BI=20, GS=256, SS=256, GK=256, SK0=256, SK1=256, GI=512, SI=512)
-_pack("OB", F32, NN=64, S1=64, S2=64, KD=32, KR=32, NK=4, PS=4, PP=32, PT=32, TA=64, PF=32, T1=32, TM=32, SELF=32, VT_=32, G8=128, S8=128,
+      KK2=32, KK3=32, DC=16, PR0=16, PR1=16, NV=16, SYV=16, SG1=16, BA=16, BC=16, BI=20, GS=256, SS=256, GK=256, SK0=256, SK1=256, GI=512, SI=512)
+_pack("OB", F32, NN=128, KEEP8=128, KD=256, KR=32, NK=4, PS=4, PP=32, PT=32, TA=64, PF=32, T1=32, TM=32, SELF=32, VT_=32, G8=128, S8=128,
       E1=8, E2=8, FCF=32, PP_=32, LZD=32, OF=32, OT=32, M1=40)
-_sb(F32, RK=512, DP=512, SRT=512, SELX=512, LA=672, LBW=672, TLA=640, TLB=640, FX=512, FXR=512)
-_sb(BF, SG0=512, SG1B=512, SG2=512, CMP=514, FM=512, SCN=512, PA_=256, PB_=256, EQ=256, EQS=256, MSG0=128, MSG1=128, MSG2=128, FW0=640, FW1=640, FW2=640)
+_sb(F32, RK=512, DP=512, SRT=512, SELX=512, LA=10240, LBW=10240, TLA=640, TLB=640, FX=512, FXR=512)
+_sb(BF, SG0=512, SG1B=512, SG2=512, CMP=514, FM=512, SCN=512, PA_=256, PB_=256, EQ=256, EQS=272, MSG0=128, MSG1=128, MSG2=128, FW0=640, FW1=640, FW2=640)
 _pack("HI", I32, FCI=32, FA=32, M2=20, M3=20)
 _pack("HU", U16, OFFI=32, KU=16, BKU=16, BIU=20, AL=64, KL=32, PA=32, SEL=32, VL=32, EL2=8, OFF=32, EL=20)
 for _t in range(8):
@@ -56,7 +56,8 @@ SEMAPHORES = ["sv", "st", "ss", "sg", "dx", "du", "dv", "dw", "dp0", "dp1", "dl0
 for _t in range(3):
     SEMAPHORES += ["rq%d" % _t, "rl%d" % _t]
 
-WAKE, LOCAL, REMOTE = 130.0, 1900.0, 2800.0
+WAKE, LOCAL, REMOTE, CYC = 220.0, 1900.0, 2800.0, 0.87
+PASSES, SLIP, PIECE = 2, 20.0, 8
 
 
 def rank_program(g, core, T, topo):
@@ -120,7 +121,7 @@ def rank_program(g, core, T, topo):
             return 55 + 1.25 * width(out)
         if all(SCRATCH[v[0]][2] in (BF, U16) for v in sides):
             per *= 0.5
-        return max(64.0, per * width(ins[0] if ins else out))
+        return CYC * max(64.0, per * width(ins[0] if ins else out))
 
     def node(q, call, reads, writes, busy, kind="op", after=0.0, **more):
         rd, wr = [], []
@@ -148,7 +149,7 @@ def rank_program(g, core, T, topo):
         node("v", lambda: g.vector.tensor_tensor_scan(ap(out), ap(d0), ap(d1), first, o0, o1), [d0, d1], [out], cost(out, [d0, d1]))
 
     def red(out, a):
-        node("v", lambda: g.vector.tensor_reduce(ap(out), ap(a), AxisListType.X, add), [a], [out], float(width(a)))
+        node("v", lambda: g.vector.tensor_reduce(ap(out), ap(a), AxisListType.X, add), [a], [out], CYC * width(a))
 
     def fill(out, c):
         node("v", lambda: g.vector.memset(ap(out), c), [], [out], cost(out, []))
@@ -166,7 +167,7 @@ def rank_program(g, core, T, topo):
         if acc is not None:
             more["accum_out"] = ap(acc)
         f = func or (ACT.Copy if bias is None else ACT.Identity)
-        busy = cost(out, [a]) if N(a)[0] == "I" else max(64.0, width(a))
+        busy = cost(out, [a]) if N(a)[0] == "I" else CYC * max(64.0, width(a))
         node("s", lambda: g.scalar.activation(ap(out), ap(a), f, **more), [a] + ([bias] if isinstance(bias, tuple) else []), [out] + ([acc] if acc else []), busy + 20)
 
     def iota(out, pattern, base, mult):
@@ -203,7 +204,7 @@ def rank_program(g, core, T, topo):
                 if code:
                     o, i = o.bitcast(dt.uint8), i.bitcast(dt.uint8)
                 g.remote_dma(o, i, T.sem[sem], T.sem["rsend"], a_nxt[1], a_nxt[0], m_nxt)
-        node("g", call, [src for _o, src, _c in items], [out for out, _s, _c in items], 400.0 * len(items), "send", REMOTE, sem=sem, total=e_in * len(items), left=e_out * len(items))
+        node("g", call, [src for _o, src, _c in items], [out for out, _s, _c in items], 400.0 * len(items), "send", REMOTE + 600.0 * (len(items) - 1), sem=sem, total=e_in * len(items), left=e_out * len(items))
 
     dmas("y", "dx", [("XT", T.x[:, :])])
     dmas("s", "du", [("UT", T.u[:, :])])
@@ -253,9 +254,8 @@ def rank_program(g, core, T, topo):
     for k in (1, 2):
         fill(Q("NBI", k), 0)
     cp("NBL", "NBI")
-    act(W("NB8", 0, 1280), I(CELLS, W("NBL", 0, 80)))
-    for k in range(4):
-        cp(W("NB8", 1280 + 320 * k, 1600 + 320 * k), I(CELLS, W("NBL", 80 + 20 * k, 100 + 20 * k)))
+    for k in range(8):
+        (act if k < 6 else cp)(W("NB8", 320 * k, 320 * k + 320), I(CELLS, W("NBL", 20 * k, 20 * k + 20)))
     iota("CIDX", [[16, 20]], 0, 0)
     ts(pf(5), c7, 320.0, mul, ch, add)
     ts("CIDX", "CIDX", pf(5), add)
@@ -265,50 +265,48 @@ def rank_program(g, core, T, topo):
     fill("KEEP", 1.0)
     fill(W("KEEP", 0, 512, 16), 0.0)
     fill(W("ST", 640, 960), 0.0)
-    for k in ("DE", "DO", "DL", "D0", "D0L", "ZZ", "NN"):
+    for k in ("DE", "DO", "DL", "D0", "D0L", "ZZ", "PR0", "PR1"):
         fill(k, 0.0)
     fill("BKU", 0)
     fill(W("D0", 3, 64, 4), -1.0)
     fill(W("D0L", 2, 64, 4), -1.0)
     fill(W("D0L", 3, 64, 4), 1.0)
     ts(W("R", 0, 32), "PI", 0.0, add)
-    fill("ON", 1.0)
+    fill("ON", 0.5)
     for b in range(4):
         select("CT%d" % b, "ON", [[1, 512]], -b, -4)
         quant("eq%d" % b, "es%d" % b, "CT%d" % b)
-    iota(Q(W("KR", 0, 16), 3), [[16, 16]], -ZERO, 1)
+    iota(Q(W("KR", 0, 16), 0), [[16, 16]], -ZERO, 1)
     ts(pf(6), ce, 240.0, mul)
-    ts(Q(W("NN", 3, 64, 4), 3), Q(W("KR", 0, 16), 3), Q(pf(6), 3), add)
+    ts(Q(W("NN", 7, 128, 8), 0), Q(W("KR", 0, 16), 0), Q(pf(6), 0), add)
+    fill("KEEP8", 1.0)
+    fill(W("KEEP8", 0, 128, 8), 0.0)
     fill(W("CMP", 512, 513), -256.0)
     fill(W("CMP", 513, 514), -255.0)
     iota("CE", [[16, 32]], 128, 0)
     ts("CE", "CE", cq, add)
     act("ENT", W("IOTA", ZERO, ZERO + 512), 1.0 / 2048)
-    iota("RHO", [[0, 2], [1, 8]], 1, 0)
-    iota("E256", [[256, 2], [0, 8]], 15, 0)
-    ts("NF", "RHO", cq, le)
-    tt("TF", "NF", "RHO", mul)
+    RHO = W("IOTA", ZERO + 1, ZERO + 9)
+    ts("NF", RHO, cq, le)
+    tt("TF", "NF", RHO, mul)
     ts("T2", "TF", cq, sub, -16.0, mul)
-    tt("T2", "T2", "E256", add)
-    cp("LI", "T2")
+    ts("LI", "T2", 15.0, add)
     ts("T3", "TF", -2.0, mul)
-    tt("T3", "T3", "RHO", add)
+    tt("T3", "T3", RHO, add)
     ts("NF", "NF", 16.0, mul)
     tt("T3", "T3", "NF", add)
-    ts("T3", "T3", 16.0, mul)
-    tt("T3", "T3", "E256", add)
-    cp("LJ", "T3")
+    ts("LJ", "T3", 16.0, mul, 15.0, add)
     fill("KP", 1.0)
-    fill(W("KP", 0, 256, 16), 0.0)
-    for e in range(2):
-        fill(W("KP", 128 * e + 1, 128 * e + 128, 17), 0.0)
+    fill(W("KP", 0, 128, 16), 0.0)
+    fill(W("KP", 1, 128, 17), 0.0)
     ts(pf(7), cq, 17.0, mul, -17.0, add)
     ts(pf(8), cq, -16.0, mul, 255.0, add)
     ts(pf(9), pf(7), pf(8), mn_)
-    ts(W("LE", 0, 1), pf(9), 0.0, add)
-    ts(W("LE", 1, 2), pf(9), 128.0, add)
-    iota("DUMP", [[0, 2], [1, 16]], 640, 0)
-    fill(W("DUMP", 0, 32, 16), 0.0)
+    for e in range(2):
+        ts(pf(14 + e), cq, 0.0, eq, 273.0 - 128 * e, mul)
+        ts(pf(14 + e), pf(14 + e), pf(9), add)
+        ts(W("LE", e, e + 1), pf(14 + e), 128.0 * e, add)
+    fill(W("EQS", 256, 272), 0.0)
     iota("LOWC", [[16, 20], [0, 2], [1, 16]], 3 * 1024 + 640, 0)
     ts(pf(10), ce, 2048.0, mul)
     ts(pf(11), ce, 2048.0, mul, 1024.0, add)
@@ -349,9 +347,11 @@ def rank_program(g, core, T, topo):
             cp("KU", kk)
         tt("GS", I(W("ST", 0, 640) if even else W("ST", 320, 960), "KU"), MASK(256), mul)
         sm, sy, sn = (slot(d1, 1), slot(d1, 2), slot(d1, 3)) if h < 3 else (slot(d1, 0), slot(d1, 1), slot(d1, 2))
-        tt("DC", kk, n, sub)
-        tt("PR", "DC", s3, mul)
-        ts("NV", "PR", 0.0, ne, FAR, mul)
+        pr, ns = "PR%d" % (h % 2), W("R", 48, 64) if h == 3 else "NS"
+        for q, k in ((1, 1), (2, 2)) if even else ((0, 3),):
+            tt(Q("DC", q, k), Q(ns, q, k), Q(y, q, k), sub)
+            tt(Q(pr, q, k), Q("DC", q, k), Q(s3, q, k), mul)
+        ts("NV", pr, 0.0, ne, FAR, mul)
         tt("SYV", S, "NV", add)
         tt(sm, kk, y, sub)
         cp(sy, y)
@@ -380,8 +380,7 @@ def rank_program(g, core, T, topo):
 
     for rd in range(ROUNDS):
         mq, ms, fw, msg = "mq%d" % rd, "ms%d" % rd, "FW%d" % rd, "MSG%d" % rd
-        ts(W("OFFI", 0, 16), E, 0.0, add)
-        ts(W("OFFI", 16, 32), O, 320.0, add)
+        cp("OFFI", W("R", 0, 32))
         tt("S30", E, O, sub)
         kk0 = W("KK0", 1, 32, 2)
         other(kk0, O, "S30", True, "NS")
@@ -391,12 +390,15 @@ def rank_program(g, core, T, topo):
         tt(Q("BL", 0), Q("NZ", 0), Q(O, 0), add)
         cp(Q("BKU", 0), Q("BL", 0))
         cp(Q("BKU", 3), Q(O, 3))
-        for k in range(3):
+        for k in range(2):
+            mm(3 * k, W("ur", 0, 128), W("urs", 0, 128), W(mq, 160 * k, 160 * k + 160), W(ms, 160 * k, 160 * k + 160))
+            (cp if k else act)(W("W07", 160 * k, 160 * k + 160), W("ps%d" % (3 * k), 0, 160))
+        for k in (1, 2):
             mm(k, W("ur", 128 * k, 128 * k + 128), W("urs", 128 * k, 128 * k + 128), mq, ms)
-        act("W07", W("ps0", 0, 320))
         cp(W("ST", 0, 320), W("ps1", 0, 320))
         act(W("ST", 320, 640), W("ps2", 0, 320))
-        cp("GB", I("W07", "LB"))
+        cp(W("GB", 0, 160), I("W07", W("LB", 0, 10)))
+        act(W("GB", 160, 320), I("W07", W("LB", 10, 20)))
         scan("RM", "K8", "GB", add, mx_)
         for t in range(7):
             at = 80 * (t // 2) + t % 2
@@ -406,18 +408,21 @@ def rank_program(g, core, T, topo):
             mm(3, "bq", "bs", W("dq", 20 * k, 20 * k + 128), W("dsc", 20 * k, 20 * k + 128), k == 0, k == 3)
         tt("BI", W("ps3", 0, 20), "CIDX", add)
         cp("BIU", "BI")
-        act(W("KT", 0, 320), I("NB8", "BIU"))
+        cp(W("KT", 0, 160), I("NB8", W("BIU", 0, 10)))
+        act(W("KT", 160, 320), I("NB8", W("BIU", 10, 20)))
         lookup("GK", "SK0", "KT", "BKU")
         cp(Q("KU", 0), Q(ends("SK0"), 0))
         cp(Q(kk0, 0), Q(ends("SK0"), 0))
         tt(Q(slot("DE", 0), 3), Q(ends("SK0"), 3), Q(O, 3), sub)
-        lookup("GI", "SI", W("ST", 0, 640), "OFFI")
+        for k in range(4):
+            lookup(W("GI", 128 * k, 128 * k + 128), W("SI", 128 * k, 128 * k + 128), W("ST", 320 * (k // 2), 320 * (k // 2) + 320), W("OFFI", 8 * k, 8 * k + 8))
         for t in range(4):
             f = W("ps%d" % (4 + t), 0, 320)
             mm(4 + t, "eq%d" % t, "es%d" % t, mq, ms)
-            act("FQ%d" % t, f, 0.25)
-            act("FH%d" % t, f, 0.5)
-            act(W("YW%d" % t, 640, 960), f, 0.5)
+            act("FQ%d" % t, f, 0.5)
+            act(W("YW%d" % t, 640, 960), f)
+            if t < 2:
+                act("FH%d" % t, f)
         act(W("LA", 0, 640), "LOWC", bias=pf(12))
         act(W("LBW", 0, 640), "LOWC", bias=8192.0)
         for h in range(4):
@@ -427,16 +432,14 @@ def rank_program(g, core, T, topo):
         tr("TA", "R")
         cp("AL", "TA")
         al, bl = W("AL", 0, 32), W("AL", 32, 64)
-        ts(Q("NN", 0, 3), Q("OUT3", 0, 3), 0.0, eq, 512.0, mul)
-        ts(Q(slot("NN", 2), 3), Q(slot("OUT3", 2), 3), 0.0, eq, 512.0, mul)
-        tt(Q("S1", 0, 2), Q("NN", 0, 2), Q("NN", 2, 2), add)
-        tt(Q("S2", 0), Q("S1", 0), Q("S1", 1), add)
+        for k in range(7):
+            ts(Q(W("NN", k, 128, 8), 0), Q(slot("OUT3", 2 + k % 2), k // 2), 0.0, eq, 512.0, mul)
         for k in range(2):
-            tt(Q(W("KD", 16 * k, 16 * k + 16), 0), Q(slot("S2", 2), 0), Q(slot("S2", 3), 0), add)
-        tr(Q("KR", 0), Q("KD", 0))
+            scan(Q(W("KD", 128 * k, 128 * k + 128), 0), Q("KEEP8", 0), Q("NN", 0))
+        tr(Q("KR", 0), Q(W("KD", 7, 256, 8), 0))
         for q in range(4):
             ts(Q("KL", q), Q("KR", 0), float(ZERO), add)
-            act(Q("NK", q), Q(W("KD", 4 * q, 4 * q + 4), 0))
+            act(Q("NK", q), Q(W("KD", 32 * q + 7, 32 * q + 32, 8), 0))
         act("RK", I("IOTA", "KL"))
         for b in range(3):
             act(("SG0", "SG1B", "SG2")[b], "RK", -1.0, W("NK", b, b + 1), ACT.Sign, W("PS", b, b + 1))
@@ -454,8 +457,10 @@ def rank_program(g, core, T, topo):
         send("rl%d" % rd, [(W(fw, 0, 128), msg, False)])
         act(W(fw, 128, 640), I(CELLM, al))
         for t in range(4):
-            act("ZG%d" % t, I("FQ%d" % t, al))
-            tt(W("YW%d" % t, 128, 640), I("FQ%d" % t, bl), "ZG%d" % t, add)
+            for k in range(0, 32, PIECE):
+                zg = W("ZG%d" % t, 16 * k, 16 * (k + PIECE))
+                (act if t else cp)(zg, I("FQ%d" % t, W("AL", k, k + PIECE)))
+                tt(W("YW%d" % t, 128 + 16 * k, 128 + 16 * (k + PIECE)), I("FQ%d" % t, W("AL", 32 + k, 32 + k + PIECE)), zg, add)
         tt("G8", W("SRT", 0, 128), MASK(128), mul)
         scan("S8", KEEP(128), "G8")
         ts("E1", ends("S8", 128), ROUND, add, ROUND, sub)
@@ -467,8 +472,8 @@ def rank_program(g, core, T, topo):
         quant(aq, asc, "HT")
         send("rq%d" % rd, [(lq, aq, True), (ls, asc, False)])
         for b in range(4):
-            mm(4 + b, W("wq", 128 * b, 128 * b + 128), W("wsc", 128 * b, 128 * b + 128), lq, ls)
-            act(W("YW%d" % b, 0, 128), W("ps%d" % (4 + b), 0, 128), 2.0 ** -6)
+            mm(b, W("wq", 128 * b, 128 * b + 128), W("wsc", 128 * b, 128 * b + 128), lq, ls)
+            act(W("YW%d" % b, 0, 128), W("ps%d" % b, 0, 128), 2.0 ** -6)
         cp("PF", "PA")
         ts("T1", "PA", 128.0, ge, 1024.0, mul)
         tt("TM", "T1", "PF", mx_)
@@ -479,20 +484,21 @@ def rank_program(g, core, T, topo):
             cp(W("VL", par, 32, 2), W("VT_", 16 * par, 16 * par + 16))
         for w in range(2):
             act(W("SELX", 256 * w, 256 * w + 256), I(COLS, W("VL", 16 * w, 16 * w + 16)), bias=pf(10 + w))
-        tt("FM", I(fw, "SEL"), "MASK", mul)
-        scan("SCN", "KEEP", "FM")
-        cp("PA_", I("SCN", "LI"))
-        act("PB_", I("SCN", "LJ"))
-        tt("EQ", "PA_", "PB_", eq)
-        scan("EQS", "KP", "EQ", mul, mx_)
-        tt("LZD", I("EQS", "LE"), "DUMP", mul)
+        for e in range(2):
+            half = lambda name, n: W(name, n * e, n * e + n)
+            lookup(half("FM", 256), half("SCN", 256), fw, half("SEL", 16))
+            cp(half("PA_", 128), I(half("SCN", 256), "LI"))
+            act(half("PB_", 128), I(half("SCN", 256), "LJ"))
+            tt(half("EQ", 128), half("PA_", 128), half("PB_", 128), eq)
+            scan(half("EQS", 128), "KP", half("EQ", 128))
         ts("FCI", ends("SCN", 512), float(MID), add)
         ts("FA", "FCI", 496, bw)
-        tt("PP_", "FA", "FCI", add)
-        tt("OF", "PP_", "LZD", mx_)
+        tt("LZD", "FA", "FCI", add)
+        ts("PP_", "LZD", 1.0 / 640, mul)
+        tt("OF", I("EQS", "LE"), "PP_", add)
         tr("OT", "OF")
         for par in range(2):
-            ts(W("OFF", par, 32, 2), W("OT", 16 * par, 16 * par + 16), 16.0 * par, add)
+            ts(W("OFF", par, 32, 2), W("OT", 16 * par, 16 * par + 16), 640.0, mul, 16.0 * par + 0.25, add)
         if rd + 1 < ROUNDS:
             ts("FCF", ends("SCN", 512), float(MID), add)
             tr(W("R", 0, 32), "FCF")
@@ -510,9 +516,12 @@ def rank_program(g, core, T, topo):
         tt("M2", W("M1", 0, 40, 2), W("M1", 1, 40, 2), mn_)
         ts("M3", "M2", 1023, bw)
         cp("EL", "M3")
-        for t in range(4):
+        for t in range(2):
             tt(W("MT", t, 1280, 4), I("YW%d" % t, "EL"), "FH%d" % t, add)
-        quant("mq%d" % (rd + 1), "ms%d" % (rd + 1), "MT")
+            act("G%d" % (2 + t), I("YW%d" % (2 + t), "EL"))
+            tt(W("MT", 2 + t, 1280, 4), W("ps%d" % (6 + t), 0, 320), "G%d" % (2 + t), add)
+        for k in range(2):
+            quant(W("mq%d" % (rd + 1), 160 * k, 160 * k + 160), W("ms%d" % (rd + 1), 160 * k, 160 * k + 160), W("MT", 640 * k, 640 * k + 640))
 
     mq, ms = "mq%d" % ROUNDS, "ms%d" % ROUNDS
     mm(0, "vq", "vs", mq, ms)
@@ -535,36 +544,41 @@ def rank_program(g, core, T, topo):
             nodes[j]["post"].append(i)
     for n in reversed(nodes):
         n["way"] = n["busy"] + n["after"] + max([WAKE + nodes[j]["way"] for j in n["post"]] or [0.0])
-    free = {q: 0.0 for q in queue}
-    left = [len(n["pre"]) for n in nodes]
-    ready = {i: 0.0 for i, n in enumerate(nodes) if not n["pre"]}
-    order = []
-    while ready:
-        picks = []
-        for q in queue:
-            mine = [i for i in ready if nodes[i]["q"] == q]
-            if not mine:
-                continue
-            best = max(mine, key=lambda i: (nodes[i]["way"], -i))
-            start = max(free[q], ready[best])
-            for i in sorted(mine, key=lambda i: (-nodes[i]["way"], i)):
-                at = max(free[q], ready[i])
-                first = max(max(start, at + nodes[i]["busy"]) + nodes[best]["way"], at + nodes[i]["way"])
-                second = max(start + nodes[best]["way"], start + nodes[best]["busy"] + nodes[i]["way"])
-                if i != best and at < start and first <= second:
-                    best, start = i, at
-                    break
-            picks.append((start, best))
-        start, i = min(picks)
-        n = nodes[i]
-        del ready[i]
-        order.append(i)
-        free[n["q"]] = start + n["busy"] + (WAKE if n.get("drain") else 0.0)
-        n["done"] = start + n["busy"] + n["after"]
-        for j in n["post"]:
-            left[j] -= 1
-            if left[j] == 0:
-                ready[j] = max(nodes[k]["done"] + (0.0 if nodes[j].get("chain") and nodes[k]["q"] == "t" else WAKE) for k in nodes[j]["pre"])
+
+    def lag(i, j):
+        return 0.0 if nodes[j].get("chain") and nodes[i]["q"] == "t" else WAKE
+
+    def lay(rank_of, back):
+        before, behind = ("post", "pre") if back else ("pre", "post")
+        left = [len(n[before]) for n in nodes]
+        ready = [i for i, k in enumerate(left) if k == 0]
+        taken, start, done = {q: [] for q in queue}, {}, {}
+        while ready:
+            i = min(ready, key=lambda i: (rank_of[i], i))
+            ready.remove(i)
+            n = nodes[i]
+            at = max([done[k] + (lag(i, k) if back else lag(k, i)) for k in n[before]] or [0.0]) + (n["after"] if back else 0.0)
+            busy, line, k = n["busy"] + (WAKE if n.get("drain") else 0.0), taken[n["q"]], len(taken[n["q"]])
+            while k > 0 and line[k - 1][1] > at:
+                k -= 1
+            while k < len(line) and line[k][0] < at + busy - SLIP:
+                at = max(at, line[k][1])
+                k += 1
+            line.insert(k, (at, at + busy))
+            start[i], done[i] = at, at + n["busy"] + (0.0 if back else n["after"])
+            for j in n[behind]:
+                left[j] -= 1
+                if left[j] == 0:
+                    ready.append(j)
+        return start, done
+
+    start, done = lay([-n["way"] for n in nodes], False)
+    best = (max(done.values()), start)
+    for _pass in range(PASSES):
+        _start, done = lay([-done[i] for i in range(len(nodes))], True)
+        start, done = lay([-done[i] for i in range(len(nodes))], False)
+        best = min(best, (max(done.values()), start), key=lambda x: x[0])
+    order = sorted(range(len(nodes)), key=lambda i: (best[1][i], i))
 
     count, know, totals, sent = {k: 0 for k in own}, {k: {} for k in queue}, {}, 0
     drain = False

@@ -24,10 +24,12 @@ def _pack(buf, dtype, **kw):
 
 _sb(BF, XT=1280, MT=1280, UT=512, VT=512, BY=128, ON=512, DT=512, ZT=512, HT=512, CB=512)
 _pack("CTB", BF, CT0=512, CT1=512, CT2=512, CT3=512)
-_pack("YW", BF, YW0=960, YW1=960, YW2=960, YW3=960)
-_pack("FH", BF, FH0=320, FH1=320, FH2=320, FH3=320)
+_pack("YW", BF, YW0=1472, YW1=1472, YW2=1472, YW3=1472)
+_pack("FH", BF, FH0=320, FH1=320)
 _pack("FQ", BF, FQ0=320, FQ1=320, FQ2=320, FQ3=320)
-_pack("ZG", BF, ZG0=512, ZG1=512, ZG2=512, ZG3=512)
+_pack("ZG", BF, ZG0=1024, ZG1=1024, ZG2=1024, ZG3=1024)
+_sb(BF, KEEP2=512)
+_sb(F32, YC=640)
 _sb(F32, W07=320, GB=320, RM=320, K8=320)
 _sb(MXC, uq=128, ur=384, vq=128, dq=256, bq=128, wq=512, mq0=320, mq1=320, mq2=320, mq3=320)
 _sb(U8, us=128, urs=384, vs=128, dsc=256, bs=128, wsc=512, ms0=320, ms1=320, ms2=320, ms3=320)
@@ -36,28 +38,31 @@ _sb(U8, as0=128, as1=128, as2=128, ls0=128, ls1=128, ls2=128)
 _pack("eqc", MXC, eq0=128, eq1=128, eq2=128, eq3=128)
 _pack("esc", U8, es0=128, es1=128, es2=128, es3=128)
 _sb(F32, IOTA=4096, LOWC=640, ENT=512)
-_sb(BF, MASK=512, KEEP=512, I16=512, KP=128, G2=320, G3=320)
-_pack("KC", F32, PCF=16, CE=32, CIDX=20, ULF=24, NF=8, TF=8, T2=8, T3=8, REVF=32)
+_sb(BF, MASK=512, KEEP=512, KP=128, G2=320, G3=320)
+_pack("KC", F32, PCF=32, CE=32, CIDX=20, ULF=24, NF=8, TF=8, T2=8, T3=8, REVF=32)
 _sb(I32, PCI=8, LBI=20, NBI=160, PI=32)
 _pack("KU16", U16, ULU=24, LB=20, NBL=160, LI=8, LJ=8, LE=2, REV=32)
 _sb(F32, ST=960, NB8=2560, KT=640, YO=320)
-_pack("HB", F32, R=64, S30=16, NS=16, NZ=16, BL=16, DE=64, DO=64, DL=64, D0=64, D0L=64, OUT0=64, OUT1=64, OUT2=64, OUT3=64, ZZ=32, KK0=32, KK1=32,
-      KK2=32, KK3=32, DC=16, PR0=16, PR1=16, NV=16, SYV=16, SG1=16, BA=16, BC=16, BI=20, GS=256, SS=256, GK=256, SK0=256, SK1=256, GI=512, SI=512)
-_pack("OB", F32, NN=128, KEEP8=128, KD=256, KR=32, NK=4, PS=4, PP=32, PT=32, TA=64, PF=32, T1=32, TM=32, SELF=32, VT_=32, G8=128, S8=128,
+_pack("HB", F32, R=80, S30=16, NS=16, NZ=16, BL=16, DE=112, DO=112, DL=64, D0E=112, D0O=112, D0L=64, OUT0=112, OUT1=112, OUT2=112, OUT3=64,
+      Z1=16, KK0=16, KK1=16, KK2=16, KK3=16, DC=16, PR=16, NV=16, SYV=16, SG1=16, BA=16, BC=16, BI=20, GS=256, SS=256, GK=128, SK=128, B0=16, B1=16, GI=512, SI=512)
+_pack("OB", F32, NN=128, KEEP8=128, KD=256, KR=32, NK=4, PS=4, PP=32, PT=32, TA=96, PF=32, T1=32, TM=32, SELF=32, VT_=32, G8=128, S8=128,
       E1=8, E2=8, FCF=32, PP_=32, LZD=32, OF=32, OT=32, M1=40)
-_sb(F32, RK=512, DP=512, SRT=512, SELX=512, LA=10240, LBW=10240, TLA=640, TLB=640, FX=512, FXR=512)
+_sb(F32, RK=512, DP=512, SRT=512, VA=80)
+_sb(BF, LA=10240, LBW=10240, TLA=640, TLB=640, SELX=512, LOWB=640)
 _sb(BF, SG0=512, SG1B=512, SG2=512, CMP=514, FM=512, SCN=512, PA_=256, PB_=256, EQ=256, EQS=272, MSG0=128, MSG1=128, MSG2=128, FW0=640, FW1=640, FW2=640)
 _pack("HI", I32, FCI=32, FA=32, M2=20, M3=20)
-_pack("HU", U16, OFFI=32, KU=16, BKU=16, BIU=20, AL=64, KL=32, PA=32, SEL=32, VL=32, EL2=8, OFF=32, EL=20)
+_pack("HU", U16, OFFI=32, KU=16, BKU=8, BIU=20, AL=96, KL=32, PA=32, SEL=32, VL=32, EL2=8, OFF=32, EL=20)
 for _t in range(8):
     SCRATCH["ps%d" % _t] = ("psum", [128, 512], F32)
 
-SEMAPHORES = ["sv", "st", "ss", "sg", "dx", "du", "dv", "dw", "dp0", "dp1", "dl0", "dl1", "dn", "rsend", "dad", "doc", "dy"]
+SEMAPHORES = ["sv", "st", "ss", "sg", "dx", "du", "dv", "dw", "dp0", "dp1", "dl0", "dl1", "dn", "rsend", "dad", "dy1", "doc", "dy"]
 for _t in range(3):
     SEMAPHORES += ["rq%d" % _t, "rl%d" % _t]
 
-WAKE, LOCAL, REMOTE, CYC = 220.0, 1900.0, 2800.0, 0.87
-PASSES, SLIP, PIECE = 2, 20.0, 8
+WAKE, LOCAL, REMOTE, CYC = 220.0, 2200.0, 2800.0, 0.87
+PASSES, SLIP, PIECE = 1, 20.0, 8
+BONDV = 2
+ORDER = []
 
 
 def rank_program(g, core, T, topo):
@@ -152,6 +157,12 @@ def rank_program(g, core, T, topo):
         node("v", lambda: g.vector.tensor_reduce(ap(out), ap(a), AxisListType.X, add), [a], [out], CYC * width(a))
 
     def fill(out, c):
+        out = N(out)
+        if cost(out, []) > WAKE - SLIP:
+            mid = out[1] + (out[2] - out[1]) // 2
+            fill(out[:2] + (mid,) + out[3:], c)
+            fill(out[:1] + (mid,) + out[2:], c)
+            return
         node("v", lambda: g.vector.memset(ap(out), c), [], [out], cost(out, []))
 
     def tr(out, a):
@@ -161,14 +172,14 @@ def rank_program(g, core, T, topo):
         node("v", lambda: g.vector.quantize_mx(ap(q), ap(s), ap(a)), [a], [q, s], 12 + 0.26 * width(a))
 
     def act(out, a, scale=1.0, bias=None, func=None, acc=None):
-        more = {} if scale == 1.0 else {"scale": scale}
+        more = {} if scale == 1.0 else {"scale": ap(scale) if isinstance(scale, tuple) else scale}
         if bias is not None:
             more["bias"] = ap(bias) if isinstance(bias, tuple) else bias
         if acc is not None:
             more["accum_out"] = ap(acc)
         f = func or (ACT.Copy if bias is None else ACT.Identity)
         busy = cost(out, [a]) if N(a)[0] == "I" else CYC * max(64.0, width(a))
-        node("s", lambda: g.scalar.activation(ap(out), ap(a), f, **more), [a] + ([bias] if isinstance(bias, tuple) else []), [out] + ([acc] if acc else []), busy + 20)
+        node("s", lambda: g.scalar.activation(ap(out), ap(a), f, **more), [a] + [x for x in (bias, scale) if isinstance(x, tuple)], [out] + ([acc] if acc else []), busy + 20)
 
     def iota(out, pattern, base, mult):
         more = {} if SCRATCH[N(out)[0]][2] == I32 else {"allow_small_or_imprecise_dtypes": True}
@@ -210,7 +221,7 @@ def rank_program(g, core, T, topo):
     dmas("s", "du", [("UT", T.u[:, :])])
     for y in range(2):
         dmas("ys"[y], "dl%d" % y, [(W("LBI", 0, 20, 1, 8 * y + t, 128, 16), T.nb[16 * t + y:16 * t + 16:2, :]) for t in range(8)])
-    dmas("y", "dn", [(W("NBI", 0, 160, 1, 16 * k, 16 * k + 16), T.nb[:, :]) for k in (0, 1, 6, 7)])
+    dmas("y", "dn", [(W("NBI", 0, 160, 1, 16 * k, 16 * k + 16), T.nb[:, :]) for k in (0, 1)])
     for e in range(2):
         dmas("ys"[e], "dp%d" % e, [(W("PI", 16 * par, 16 * par + 16, 1, 32 * a + 16 * e, 32 * a + 16 * e + 16),
                                     T.p[32 * a + 16 * par:32 * a + 16 * par + 16, 16 * e:16 * e + 16]) for a in range(4) for par in range(2)])
@@ -230,20 +241,24 @@ def rank_program(g, core, T, topo):
     ts(W("ULU", 0, 8), W("ULF", 0, 8), ch, mul)
     cp(W("ULU", 8, 24), W("ULF", 8, 24))
     quant("uq", "us", "UT")
-    node("v", lambda: g.vector.tensor_copy(ap("ur").bitcast(dt.uint32), ap("uq").bitcast(dt.uint32).indirect(ap("ULU"))), ["uq", "ULU"], ["ur"], 530.0)
-    act("urs", I("us", "ULU"))
-    quant("mq0", "ms0", "XT")
+    for k in range(3):
+        ul, o = W("ULU", 8 * k, 8 * k + 8), W("ur", 128 * k, 128 * k + 128)
+        node("v", lambda ul=ul, o=o: g.vector.tensor_copy(ap(o).bitcast(dt.uint32), ap("uq").bitcast(dt.uint32).indirect(ap(ul))), ["uq", ul], [o], 215.0)
+        act(W("urs", 128 * k, 128 * k + 128), I("us", ul))
+    for k in range(2):
+        quant(W("mq0", 160 * k, 160 * k + 160), W("ms0", 160 * k, 160 * k + 160), W("XT", 640 * k, 640 * k + 640))
     ZERO = 2048
-    iota(W("IOTA", 1888, 2688), [[1, 800]], 1888 - ZERO, 0)
-    iota(W("IOTA", 0, 1888), [[1, 1888]], -ZERO, 0)
-    iota(W("IOTA", 2688, 4096), [[1, 1408]], 2688 - ZERO, 0)
+    iota(W("IOTA", ZERO, ZERO + 320), [[1, 320]], 0, 0)
+    for k in list(range(ZERO + 320, 4096, 320)) + list(range(ZERO - 320, -320, -320)):
+        a, b = max(k, 0), min(k + 320, 4096)
+        act(W("IOTA", a, b), W("IOTA", ZERO + a - k, ZERO + b - k), bias=float(k - ZERO))
     CELLS, CELLM, COLS = W("IOTA", ZERO, ZERO + 320), W("IOTA", ZERO - MID, ZERO - MID + 320), W("IOTA", ZERO, ZERO + 640)
     fill("BY", 0.0)
     for k in (0, 1, 6, 7):
         fill(W("BY", k, 128, 8), 2.0)
-    fill(W("CB", 128, 384), 0.0)
     for e in range(2):
         select(W("CB", 384 * e, 384 * e + 128), "BY", [[0, 2], [-16, 8], [0, 8]], -8 * e, 1)
+        cp(W("CB", 128 + 128 * e, 256 + 128 * e), W("CB", 384 * e, 384 * e + 128))
     quant("bq", "bs", "CB")
     fill("DT", 0.0)
     fill("ZT", 0.0)
@@ -251,24 +266,24 @@ def rank_program(g, core, T, topo):
     fill("K8", 0.0)
     fill(W("K8", 0, 320, 8), -FAR)
     cp("LB", "LBI")
-    for k in (1, 2):
-        fill(Q("NBI", k), 0)
-    cp("NBL", "NBI")
+    for k in range(4):
+        cp(Q("NBL", k), Q("NBI", 0))
     for k in range(8):
-        (act if k < 6 else cp)(W("NB8", 320 * k, 320 * k + 320), I(CELLS, W("NBL", 20 * k, 20 * k + 20)))
+        (act if k < 7 else cp)(W("NB8", 320 * k, 320 * k + 320), I(CELLS, W("NBL", 20 * k, 20 * k + 20)))
     iota("CIDX", [[16, 20]], 0, 0)
     ts(pf(5), c7, 320.0, mul, ch, add)
     ts("CIDX", "CIDX", pf(5), add)
     act(W("KT", 320, 640), CELLS)
-    iota("I16", [[0, 32], [1, 16]], 0, 0)
-    ts("MASK", "I16", cq, eq)
+    iota("FM", [[0, 32], [1, 16]], 0, 0)
+    ts("MASK", "FM", cq, eq)
     fill("KEEP", 1.0)
     fill(W("KEEP", 0, 512, 16), 0.0)
     fill(W("ST", 640, 960), 0.0)
-    for k in ("DE", "DO", "DL", "D0", "D0L", "ZZ", "PR0", "PR1"):
+    for k in ("DE", "DO", "DL", "D0E", "D0O", "D0L", "DC"):
         fill(k, 0.0)
-    fill("BKU", 0)
-    fill(W("D0", 3, 64, 4), -1.0)
+    for k in ("D0E", "D0O"):
+        fill(W(k, 2, 112, 7), -1.0)
+        fill(W(k, 6, 112, 7), 1.0)
     fill(W("D0L", 2, 64, 4), -1.0)
     fill(W("D0L", 3, 64, 4), 1.0)
     ts(W("R", 0, 32), "PI", 0.0, add)
@@ -307,10 +322,32 @@ def rank_program(g, core, T, topo):
         ts(pf(14 + e), pf(14 + e), pf(9), add)
         ts(W("LE", e, e + 1), pf(14 + e), 128.0 * e, add)
     fill(W("EQS", 256, 272), 0.0)
-    iota("LOWC", [[16, 20], [0, 2], [1, 16]], 3 * 1024 + 640, 0)
-    ts(pf(10), ce, 2048.0, mul)
-    ts(pf(11), ce, 2048.0, mul, 1024.0, add)
-    ts(pf(12), ce, -8192.0, mul, 8192.0, add)
+    iota("LOWC", [[16, 20], [0, 2], [1, 16]], 0, 0)
+    ts(pc(5), pc(0), 1, bw)
+    lo, hi, lo2 = pf(16), pf(17), pf(18)
+    ts(lo, pc(5), 0.0, add)
+    ts(hi, pc(5), -1.0, mul, 1.0, add)
+    ts(lo2, pc(5), 2.0, mul)
+    ts(pf(10), ce, 4096.0, mul, hi, mul)
+    ts(pf(11), hi, 2048.0, mul, pf(10), add)
+    ts(pf(19), hi, 16384.0, mul)
+    ts(pf(12), ce, -1.0, mul, 1.0, add)
+    ts(pf(12), pf(12), pf(19), mul)
+
+    def split(k, out, src, scale, high, low):
+        ts(pf(k), lo, float(low - high), mul, float(high), add)
+        act(out, src, scale, pf(k))
+    split(20, W("YC", 0, 128), W("IOTA", ZERO, ZERO + 128), lo, 0, 0)
+    split(21, W("YC", 128, 192), W("IOTA", ZERO, ZERO + 64), lo2, 0, 129)
+    for m in range(4):
+        n_ = min(128, 448 - 128 * m)
+        split(22 + m, W("YC", 192 + 128 * m, 192 + 128 * m + n_), W("IOTA", ZERO, ZERO + n_), lo2, 256 * (m + 1), 1)
+    split(26, W("LOWB", 0, 256), W("LOWC", 0, 256), lo, 3 * 2048 + 1024, 128)
+    split(27, W("LOWB", 256, 640), W("LOWC", 256, 640), lo, 3 * 2048 + 1280, -128)
+    for t in range(BONDV):
+        act(W("YW%d" % t, 128, 1152, 2), W("IOTA", ZERO, ZERO + 512), 0.0)
+    fill("KEEP2", 1.0)
+    fill(W("KEEP2", 0, 512, 2), 0.0)
     iota("REVF", [[256, 2], [1, 16]], 0, 0)
     ts(pf(13), cq, 16.0, mul)
     ts("REV", "REVF", pf(13), add)
@@ -325,77 +362,98 @@ def rank_program(g, core, T, topo):
         tt(g_, I(win, off), MASK(16 * width(off)), mul)
         scan(s_, KEEP(16 * width(off)), g_)
 
-    def other(kk, n, s3, even, ns):
+    def shift(out, a, up, eng):
         for q in range(3):
-            cp(Q(ns, q + 1 if even else q), Q(n, q if even else q + 1))
-        for q, k in ((1, 1), (2, 2)) if even else ((0, 3),):
-            tt(Q(kk, q, k), Q(ns, q, k), Q(s3, q, k), sub)
+            eng(Q(out, q + 1 if up else q), Q(a, q if up else q + 1))
+
+    run = lambda name, k: W(name, k, 112, 7)
+
+    def eight(v, k):
+        n, a, _b, st = N(v)[:4]
+        return (n, a + 8 * k * st, a + (8 * k + 7) * st + 1, st, 0, 128, 1)
+
+    def best_of(first, last, to_first, to_last):
+        for k in range(2):
+            cp(Q("BKU", k), Q(eight(first, k), 0))
+            cp(Q("BKU", 2 + k), Q(eight(last, k), 3))
+        lookup("GK", "SK", "KT", "BKU")
+        for k in range(2):
+            act(Q(eight(to_first, k), 0), Q(ends("SK", 128), k))
+            act(Q(eight(to_last, k), 3), Q(ends("SK", 128), 2 + k))
 
     def halfstep(h):
         even = h % 2 == 0
-        kk, out, d1 = W("KK%d" % h, 1, 32, 2), "OUT%d" % h, ("DE", "DO", "DE", "DL")[h]
+        kk, out, d0, d1 = "KK%d" % h, "OUT%d" % h, ("D0E", "D0O", "D0E", "D0L")[h], ("DE", "DO", "DE", "DL")[h]
         S = W("SI", 15, 256, 16) if even else W("SI", 271, 512, 16)
         if h == 0:
-            y, n, s3 = E, O, "S30"
+            y, n, s3, o, dc = E, O, "S30", "NS", "DC"
         else:
             before = "OUT%d" % (h - 1)
-            y, n, s3 = slot(("DE", "DO", "DE")[h - 1], 3), slot(before, 2), slot(before, 3)
-            end = 0 if even else 3
-            other(kk, n, s3, even, W("R", 48, 64) if h == 3 else "NS")
-            ts(Q(W("ZZ", 1, 32, 2), end), Q(s3, end), 0.0, eq)
-            scan(Q("KK%d" % h, end), Q("ZZ", end), Q(W(before, 0, 64, 2), end))
+            y, n, s3, o, dc = run(("DE", "DO", "DE")[h - 1], 2), run(before, 1), run(before, 2), run(before, 5), run(before, 6)
+            tt(kk, o, s3, sub)
             cp("KU", kk)
         tt("GS", I(W("ST", 0, 640) if even else W("ST", 320, 960), "KU"), MASK(256), mul)
-        sm, sy, sn = (slot(d1, 1), slot(d1, 2), slot(d1, 3)) if h < 3 else (slot(d1, 0), slot(d1, 1), slot(d1, 2))
-        pr, ns = "PR%d" % (h % 2), W("R", 48, 64) if h == 3 else "NS"
-        for q, k in ((1, 1), (2, 2)) if even else ((0, 3),):
-            tt(Q("DC", q, k), Q(ns, q, k), Q(y, q, k), sub)
-            tt(Q(pr, q, k), Q("DC", q, k), Q(s3, q, k), mul)
-        ts("NV", pr, 0.0, ne, FAR, mul)
+        sl = run if h < 3 else slot
+        tt("PR", dc, s3, mul)
+        act("NV", "PR", 1e24, func=ACT.Abs)
         tt("SYV", S, "NV", add)
-        tt(sm, kk, y, sub)
-        cp(sy, y)
-        cp(sn, n)
+        tt(sl(d1, 0), kk, y, sub)
+        act(sl(d1, 1), y)
+        act(sl(d1, 2), n)
+        end = 3 if even else 0
+        if h < 3:
+            act(run(d1, 6), n, -1.0)
+            shift(run(d1, 4), run(d1, 0), not even, act)
+            shift(run(d1, 5), y, not even, act)
+            act(Q(run(d1, 5), end), Q(n, end))
+            ts(Q(run(d1, 4), end), Q(s3, end), 0.0, eq)
+            tt(Q("Z1", end), Q(kk, end), Q(n, end), eq)
+            tt(Q(run(d1, 3), end), Q("Z1", end), Q(run(d1, 4), end), sub)
         if h == 1:
-            ts(Q("BKU", 0), Q(n, 0), 0.0, add)
-            ts(Q("BKU", 3), Q(kk, 3), 0.0, add)
-            lookup("GK", "SK1", "KT", "BKU")
-            tt(Q(slot("DO", 0), 0), Q(ends("SK1"), 0), Q(n, 0), sub)
-            tt(Q("BA", 3), Q(ends("SK1"), 3), Q(ends("SK0"), 3), sub)
+            best_of(n, kk, "B1", "B1")
+            tt(Q(run("D0O", 5), 0), Q("B1", 0), Q(n, 0), sub)
+            tt(Q("BA", 3), Q("B1", 3), Q("B0", 3), sub)
         if h == 3:
-            cp(E, n)
-            tt(Q(slot("DL", 3), 0, 3), Q(W("R", 48, 64), 0, 3), Q(n, 0, 3), sub)
-            cp(Q(W("R", 48, 64), 3), Q(n, 3))
+            act(W("R", 48, 64), n)
+            act(Q(W("R", 64, 80), 0, 3), Q(o, 0, 3))
+            act(Q(W("R", 64, 80), 3), Q(n, 3))
+            act(E, n)
+            tt(Q(slot("DL", 3), 0, 3), Q(o, 0, 3), Q(n, 0, 3), sub)
         scan("SS", KEEP(256), "GS")
-        d0 = slot("D0", 2) if h < 3 else slot("D0L", 1)
-        tt(d0, ends("SS"), "SYV", gt)
-        scan(out, "D0" if h < 3 else "D0L", d1)
+        tt(sl(d0, 1), ends("SS"), "SYV", gt)
+        if h < 3:
+            tt(Q(run(d0, 4), end), Q(ends("SS"), end), Q("SYV", end), gt)
+            for q in range(3):
+                a, b = (q + 1, q) if even else (q, q + 1)
+                tt(Q(run(d0, 5), b), Q(ends("SS"), a), Q("SYV", a), gt)
+        scan(out, d0, d1)
         if h < 2:
             tt("SG1", ends("SS"), "NV", sub)
             tt(S, S, "SG1", mx_)
         if h == 1:
-            tt(Q("BC", 3), Q("BA", 3), Q(d0, 3), mul)
-            tt(Q("BC", 3), Q("BC", 3), Q(ends("SK0"), 3), add)
-            tt(Q(slot("DE", 0), 3), Q("BC", 3), Q(slot(out, 2), 3), sub)
+            tt(Q("BC", 3), Q("BA", 3), Q(run(d0, 1), 3), mul)
+            tt(Q("BC", 3), Q("BC", 3), Q("B0", 3), add)
+            tt(Q(run("D0E", 5), 3), Q("BC", 3), Q(run(out, 1), 3), sub)
 
     for rd in range(ROUNDS):
         mq, ms, fw, msg = "mq%d" % rd, "ms%d" % rd, "FW%d" % rd, "MSG%d" % rd
         cp("OFFI", W("R", 0, 32))
         tt("S30", E, O, sub)
-        kk0 = W("KK0", 1, 32, 2)
-        other(kk0, O, "S30", True, "NS")
+        kk0 = "KK0"
+        shift("NS", O, True, act)
+        for q, k in ((1, 1), (2, 2)):
+            tt(Q(kk0, q, k), Q("NS", q, k), Q("S30", q, k), sub)
+            tt(Q("DC", q, k), Q("NS", q, k), Q(E, q, k), sub)
         cp(Q("KU", 1), Q(kk0, 1))
         cp(Q("KU", 2, 2), Q(kk0, 2, 2))
         ts(Q("NZ", 0), Q("S30", 0), 0.0, ne, 320.0, mul)
         tt(Q("BL", 0), Q("NZ", 0), Q(O, 0), add)
-        cp(Q("BKU", 0), Q("BL", 0))
-        cp(Q("BKU", 3), Q(O, 3))
         for k in range(2):
             mm(3 * k, W("ur", 0, 128), W("urs", 0, 128), W(mq, 160 * k, 160 * k + 160), W(ms, 160 * k, 160 * k + 160))
             (cp if k else act)(W("W07", 160 * k, 160 * k + 160), W("ps%d" % (3 * k), 0, 160))
         for k in (1, 2):
             mm(k, W("ur", 128 * k, 128 * k + 128), W("urs", 128 * k, 128 * k + 128), mq, ms)
-        cp(W("ST", 0, 320), W("ps1", 0, 320))
+        act(W("ST", 0, 320), W("ps1", 0, 320))
         act(W("ST", 320, 640), W("ps2", 0, 320))
         cp(W("GB", 0, 160), I("W07", W("LB", 0, 10)))
         act(W("GB", 160, 320), I("W07", W("LB", 10, 20)))
@@ -410,28 +468,29 @@ def rank_program(g, core, T, topo):
         cp("BIU", "BI")
         cp(W("KT", 0, 160), I("NB8", W("BIU", 0, 10)))
         act(W("KT", 160, 320), I("NB8", W("BIU", 10, 20)))
-        lookup("GK", "SK0", "KT", "BKU")
-        cp(Q("KU", 0), Q(ends("SK0"), 0))
-        cp(Q(kk0, 0), Q(ends("SK0"), 0))
-        tt(Q(slot("DE", 0), 3), Q(ends("SK0"), 3), Q(O, 3), sub)
+        best_of("BL", O, kk0, "B0")
+        for k in range(2):
+            cp(Q(eight("KU", k), 0), Q(ends("SK", 128), k))
+        tt(Q(run("D0E", 5), 3), Q("B0", 3), Q(O, 3), sub)
         for k in range(4):
             lookup(W("GI", 128 * k, 128 * k + 128), W("SI", 128 * k, 128 * k + 128), W("ST", 320 * (k // 2), 320 * (k // 2) + 320), W("OFFI", 8 * k, 8 * k + 8))
         for t in range(4):
             f = W("ps%d" % (4 + t), 0, 320)
             mm(4 + t, "eq%d" % t, "es%d" % t, mq, ms)
             act("FQ%d" % t, f, 0.5)
-            act(W("YW%d" % t, 640, 960), f)
+            act(W("YW%d" % t, 1152, 1472), f)
             if t < 2:
                 act("FH%d" % t, f)
-        act(W("LA", 0, 640), "LOWC", bias=pf(12))
-        act(W("LBW", 0, 640), "LOWC", bias=8192.0)
+        act(W("LA", 0, 640), "LOWB", ce, pf(12))
+        act(W("LBW", 0, 640), "LOWB", 0.0, pf(19))
         for h in range(4):
             halfstep(h)
-        cp(O, slot("OUT3", 1))
-        cp(W("R", 32, 48), slot("OUT3", 1))
-        tr("TA", "R")
-        cp("AL", "TA")
-        al, bl = W("AL", 0, 32), W("AL", 32, 64)
+        act(O, slot("OUT3", 1))
+        act(W("R", 32, 48), slot("OUT3", 1))
+        for k, src in enumerate((W("R", 0, 32), W("R", 16, 48), W("R", 48, 80))):
+            tr(W("TA", 32 * k, 32 * k + 32), src)
+            cp(W("AL", 32 * k, 32 * k + 32), W("TA", 32 * k, 32 * k + 32))
+        al = W("AL", 0, 32)
         for k in range(7):
             ts(Q(W("NN", k, 128, 8), 0), Q(slot("OUT3", 2 + k % 2), k // 2), 0.0, eq, 512.0, mul)
         for k in range(2):
@@ -440,7 +499,8 @@ def rank_program(g, core, T, topo):
         for q in range(4):
             ts(Q("KL", q), Q("KR", 0), float(ZERO), add)
             act(Q("NK", q), Q(W("KD", 32 * q + 7, 32 * q + 32, 8), 0))
-        act("RK", I("IOTA", "KL"))
+        cp(W("RK", 0, 256), I("IOTA", W("KL", 0, 16)))
+        act(W("RK", 256, 512), I("IOTA", W("KL", 16, 32)))
         for b in range(3):
             act(("SG0", "SG1B", "SG2")[b], "RK", -1.0, W("NK", b, b + 1), ACT.Sign, W("PS", b, b + 1))
         ts(W("CMP", 0, 512), "RK", W("NK", 3, 4), lt, 2.0, mul)
@@ -451,23 +511,31 @@ def rank_program(g, core, T, topo):
         tr(Q("PT", 0), Q("PP", 0))
         for q in range(4):
             cp(Q("PA", q), Q("PT", 0))
-        tt("DP", I(CELLM, al), "ENT", add)
+        for k in range(0, 32, PIECE):
+            tt(W("DP", 16 * k, 16 * (k + PIECE)), I(CELLM, W("AL", k, k + PIECE)), W("ENT", 16 * k, 16 * (k + PIECE)), add)
         cp(I("SRT", "PA"), "DP")
         ts(msg, W("SRT", 0, 128), ROUND, add, ROUND, sub)
         send("rl%d" % rd, [(W(fw, 0, 128), msg, False)])
         act(W(fw, 128, 640), I(CELLM, al))
         for t in range(4):
-            for k in range(0, 32, PIECE):
-                zg = W("ZG%d" % t, 16 * k, 16 * (k + PIECE))
-                (act if t else cp)(zg, I("FQ%d" % t, W("AL", k, k + PIECE)))
-                tt(W("YW%d" % t, 128 + 16 * k, 128 + 16 * (k + PIECE)), I("FQ%d" % t, W("AL", 32 + k, 32 + k + PIECE)), zg, add)
+            for k in range(2):
+                if t < BONDV:
+                    zg = W("ZG%d" % t, 256 * k, 256 * k + 256)
+                    act(zg, I("FQ%d" % t, W("AL", 64 + 16 * k, 80 + 16 * k)))
+                    for j in range(2):
+                        at = 129 + 512 * k + 256 * j
+                        tt(W("YW%d" % t, at, at + 255, 2), I("FQ%d" % t, W("AL", 32 + 16 * k + 8 * j, 40 + 16 * k + 8 * j)), W("ZG%d" % t, 256 * k + 128 * j, 256 * k + 128 * j + 128), add)
+                    continue
+                for j in range(2):
+                    act(W("ZG%d" % t, 512 * k + j, 512 * k + 512, 2), I("FQ%d" % t, W("AL", 64 - 32 * j + 16 * k, 80 - 32 * j + 16 * k)))
+                scan(W("YW%d" % t, 128 + 512 * k, 640 + 512 * k), "KEEP2", W("ZG%d" % t, 512 * k, 512 * k + 512))
         tt("G8", W("SRT", 0, 128), MASK(128), mul)
         scan("S8", KEEP(128), "G8")
         ts("E1", ends("S8", 128), ROUND, add, ROUND, sub)
         tt("E2", ends("S8", 128), "E1", sub)
-        ts("EL2", "E2", 2048.0, mul)
+        ts("EL2", "E2", 4096.0, mul, 1.0, add)
         for t in range(4):
-            act(W("HT", t, 512, 4), I(W("YW%d" % t, 128, 640), "EL2"), 2.0)
+            act(W("HT", t, 512, 4), I(W("YW%d" % t, 128, 1152), "EL2"), 2.0)
         aq, asc, lq, ls = "aq%d" % rd, "as%d" % rd, "lq%d" % rd, "ls%d" % rd
         quant(aq, asc, "HT")
         send("rq%d" % rd, [(lq, aq, True), (ls, asc, False)])
@@ -483,7 +551,7 @@ def rank_program(g, core, T, topo):
         for par in range(2):
             cp(W("VL", par, 32, 2), W("VT_", 16 * par, 16 * par + 16))
         for w in range(2):
-            act(W("SELX", 256 * w, 256 * w + 256), I(COLS, W("VL", 16 * w, 16 * w + 16)), bias=pf(10 + w))
+            act(W("SELX", 256 * w, 256 * w + 256), I("YC", W("VL", 16 * w, 16 * w + 16)), bias=pf(10 + w))
         for e in range(2):
             half = lambda name, n: W(name, n * e, n * e + n)
             lookup(half("FM", 256), half("SCN", 256), fw, half("SEL", 16))
@@ -494,27 +562,29 @@ def rank_program(g, core, T, topo):
         ts("FCI", ends("SCN", 512), float(MID), add)
         ts("FA", "FCI", 496, bw)
         tt("LZD", "FA", "FCI", add)
-        ts("PP_", "LZD", 1.0 / 640, mul)
+        act("PP_", "LZD", 1.0 / 640)
         tt("OF", I("EQS", "LE"), "PP_", add)
         tr("OT", "OF")
         for par in range(2):
             ts(W("OFF", par, 32, 2), W("OT", 16 * par, 16 * par + 16), 640.0, mul, 16.0 * par + 0.25, add)
         if rd + 1 < ROUNDS:
-            ts("FCF", ends("SCN", 512), float(MID), add)
+            act("FCF", ends("SCN", 512), bias=float(MID))
             tr(W("R", 0, 32), "FCF")
         else:
-            act("FX", I(fw, "SEL"), bias=float(MID))
-            act("FXR", I("FX", "REV"))
-            dmas("y", "dad", [(T.ad[:, :], W("FXR", 0, 512, 1, 0, 128, 16))])
+            act("RK", I(fw, "SEL"), bias=float(MID))
+            act("DP", I("RK", "REV"))
+            dmas("y", "dad", [(T.ad[:, :], W("DP", 0, 512, 1, 0, 128, 16))])
         for y in range(7, -1, -1):
             for w in (1, 0):
                 k = 8 * w + y
                 cp(I("LA" if w else "LBW", W("OFF", 2 * k, 2 * k + 2)), W("SELX", 32 * k, 32 * k + 32))
         tr("TLA", W("LA", 0, 640))
         tr("TLB", W("LBW", 0, 640))
-        tt("M1", W("TLA", 0, 640, 16), W("TLB", 0, 640, 16), mn_)
+        for k, name in enumerate(("TLA", "TLB")):
+            tt(W("VA", 40 * k, 40 * k + 40), W(name, 0, 640, 16), W(name, 1, 640, 16), add)
+        tt("M1", W("VA", 0, 40), W("VA", 40, 80), mn_)
         tt("M2", W("M1", 0, 40, 2), W("M1", 1, 40, 2), mn_)
-        ts("M3", "M2", 1023, bw)
+        ts("M3", "M2", 2047, bw)
         cp("EL", "M3")
         for t in range(2):
             tt(W("MT", t, 1280, 4), I("YW%d" % t, "EL"), "FH%d" % t, add)
@@ -524,10 +594,11 @@ def rank_program(g, core, T, topo):
             quant(W("mq%d" % (rd + 1), 160 * k, 160 * k + 160), W("ms%d" % (rd + 1), 160 * k, 160 * k + 160), W("MT", 640 * k, 640 * k + 640))
 
     mq, ms = "mq%d" % ROUNDS, "ms%d" % ROUNDS
-    mm(0, "vq", "vs", mq, ms)
-    act("YO", W("ps0", 0, 320))
+    for k in range(2):
+        mm(k, "vq", "vs", W(mq, 160 * k, 160 * k + 160), W(ms, 160 * k, 160 * k + 160))
+        (cp if k else act)(W("YO", 160 * k, 160 * k + 160), W("ps%d" % k, 0, 160))
+        dmas("ys"[1 - k], ("dy", "dy1")[k], [(T.y[:, 160 * k:160 * k + 160], W("YO", 160 * k, 160 * k + 160))])
     dmas("y", "doc", [(T.oc[:, :], ("C", mq))] + [(T.osc[4 * k:4 * k + 4, :], W(ms, 0, 320, 1, 32 * k, 32 * k + 4)) for k in range(4)])
-    dmas("s", "dy", [(T.y[:, :], "YO")])
 
     seen = {}
     for i, n in enumerate(nodes):
@@ -572,13 +643,15 @@ def rank_program(g, core, T, topo):
                     ready.append(j)
         return start, done
 
-    start, done = lay([-n["way"] for n in nodes], False)
-    best = (max(done.values()), start)
-    for _pass in range(PASSES):
-        _start, done = lay([-done[i] for i in range(len(nodes))], True)
-        start, done = lay([-done[i] for i in range(len(nodes))], False)
-        best = min(best, (max(done.values()), start), key=lambda x: x[0])
-    order = sorted(range(len(nodes)), key=lambda i: (best[1][i], i))
+    if not ORDER:
+        start, done = lay([-n["way"] for n in nodes], False)
+        best = (max(done.values()), start)
+        for _pass in range(PASSES):
+            _start, done = lay([-done[i] for i in range(len(nodes))], True)
+            start, done = lay([-done[i] for i in range(len(nodes))], False)
+            best = min(best, (max(done.values()), start), key=lambda x: x[0])
+        ORDER.extend(sorted(range(len(nodes)), key=lambda i: (best[1][i], i)))
+    order = ORDER
 
     count, know, totals, sent = {k: 0 for k in own}, {k: {} for k in queue}, {}, 0
     drain = False

@@ -22,7 +22,7 @@ def _pack(buf, dtype, **kw):
     SCRATCH[buf] = ("sbuf", [128, at], dtype)
 
 
-_sb(BF, XT=1280, MT=1280, UT=512, VT=512, BY=128, ON=512, DT=512, ZT=512, HT=512, CB=512)
+_sb(BF, XT=1280, MT=1280, UT=512, VT=512, BY=128, ON=512, DT=512, HT=512, CB=512)
 _pack("CTB", BF, CT0=512, CT1=512, CT2=512, CT3=512)
 _pack("YW", BF, YW0=1472, YW1=1472, YW2=1472, YW3=1472)
 _pack("FH", BF, FH0=320, FH1=320)
@@ -30,37 +30,45 @@ _pack("FQ", BF, FQ0=320, FQ1=320, FQ2=320, FQ3=320)
 _pack("ZG", BF, ZG0=1024, ZG1=1024, ZG2=1024, ZG3=1024)
 _sb(BF, KEEP2=512)
 _sb(F32, YC=640)
-_sb(F32, W07=320, GB=320, RM=320, K8=320)
-_sb(MXC, uq=128, ur=384, vq=128, dq=256, bq=128, wq=512, mq0=320, mq1=320, mq2=320, mq3=320)
-_sb(U8, us=128, urs=384, vs=128, dsc=256, bs=128, wsc=512, ms0=320, ms1=320, ms2=320, ms3=320)
+_sb(F32, W07=320, GB=320, RM=320, K8=320, GO=48)
+_sb(BF, CB3=512)
+_sb(MXC, bq3=128)
+_sb(U8, bs3=128)
+_sb(MXC, uq=128, ur=512, vq=128, dq=256, bq=128, wq=512, mq0=320, mq1=320, mq2=320, mq3=320)
+_sb(U8, us=128, urs=512, vs=128, dsc=256, bs=128, wsc=512, ms0=320, ms1=320, ms2=320, ms3=320)
 _sb(MXC, aq0=128, aq1=128, aq2=128, lq0=128, lq1=128, lq2=128)
 _sb(U8, as0=128, as1=128, as2=128, ls0=128, ls1=128, ls2=128)
 _pack("eqc", MXC, eq0=128, eq1=128, eq2=128, eq3=128)
 _pack("esc", U8, es0=128, es1=128, es2=128, es3=128)
 _sb(F32, IOTA=4096, LOWC=640, ENT=512)
 _sb(BF, MASK=512, KEEP=512, KP=128, G2=320, G3=320)
-_pack("KC", F32, PCF=32, CE=32, CIDX=20, ULF=24, NF=8, TF=8, T2=8, T3=8, REVF=32)
+_pack("KC", F32, PCF=32, CE=32, CIDX=20, ULF=32, LSF=4, NF=8, TF=8, T2=8, T3=8, REVF=32)
 _sb(I32, PCI=8, LBI=20, NBI=160, PI=32)
-_pack("KU16", U16, ULU=24, LB=20, NBL=160, LI=8, LJ=8, LE=2, REV=32)
-_sb(F32, ST=960, NB8=2560, KT=640, YO=320)
-_pack("HB", F32, R=80, S30=16, NS=16, NZ=16, BL=16, DE=112, DO=112, DL=64, D0E=112, D0O=112, D0L=64, OUT0=112, OUT1=112, OUT2=112, OUT3=64,
-      Z1=16, KK0=16, KK1=16, KK2=16, KK3=16, DC=16, PR=16, NV=16, SYV=16, SG1=16, BA=16, BC=16, BI=20, GS=256, SS=256, GK=128, SK=128, B0=16, B1=16, GI=512, SI=512)
-_pack("OB", F32, NN=128, KEEP8=128, KD=256, KR=32, NK=4, PS=4, PP=32, PT=32, TA=96, PF=32, T1=32, TM=32, SELF=32, VT_=32, G8=128, S8=128,
+_pack("KU16", U16, ULU=32, LS=3, LB=20, NBL=160, LI=8, LJ=8, LE=2, REV=32)
+_sb(F32, ST=960, NB8=5120, KT=640, YO=320, W0=320, W3=320)
+_pack("HB", F32, R=80, SD=32, NS=16, NZ=16, BL=16, DE=96, DO=96, DL=32, D0E=96, D0O=96, D0L=32, OUT0=96, OUT1=96, OUT2=96, OUT3=96,
+      Z1=16, KK0=16, KK1=16, KK2=16, KK3=16, PR=16, NV=16, SYV=16, SG1=16, BA=16, BC=16, BI=20, GS=256, SS=256, GK0=128, SK0=128, GK1=128, SK1=128, B0=16, GI=512, SI=512)
+_pack("OB", F32, PLK=16, NN=192, KEEP8=192, KS=192, N3=80, KEEP3=80, KD=160, KR=32, NK=4, PS=4, PP=32, PT=32, TA=96, PF=32, T1=32, TM=32, SELF=32, VT_=32, G8=128, S8=128,
       E1=8, E2=8, FCF=32, PP_=32, LZD=32, OF=32, OT=32, M1=40)
 _sb(F32, RK=512, DP=512, SRT=512, VA=80)
-_sb(BF, LA=10240, LBW=10240, TLA=640, TLB=640, SELX=512, LOWB=640)
-_sb(BF, SG0=512, SG1B=512, SG2=512, CMP=514, FM=512, SCN=512, PA_=256, PB_=256, EQ=256, EQS=272, MSG0=128, MSG1=128, MSG2=128, FW0=640, FW1=640, FW2=640)
+_sb(BF, LA=10240, LBW=10240, TL=1280, SELX=512, LOWB=640)
+_sb(BF, SG0=512, SG1B=512, SG2=512, CMP=512, CNT=512, KEEPH=512, FM=512, SCN=512, PA_=256, PB_=256, EQ=256, EQS=272, MSG0=128, MSG1=128, MSG2=128, FW0=640, FW1=640, FW2=640)
 _pack("HI", I32, FCI=32, FA=32, M2=20, M3=20)
 _pack("HU", U16, OFFI=32, KU=16, BKU=8, BIU=20, AL=96, KL=32, PA=32, SEL=32, VL=32, EL2=8, OFF=32, EL=20)
 for _t in range(8):
     SCRATCH["ps%d" % _t] = ("psum", [128, 512], F32)
 
-SEMAPHORES = ["sv", "st", "ss", "sg", "dx", "du", "dv", "dw", "dp0", "dp1", "dl0", "dl1", "dn", "rsend", "dad", "dy1", "doc", "dy"]
+SEMAPHORES = ["sv", "st", "ss", "sg", "dx0", "dx1", "du", "dv", "dw", "dp0", "dp1", "dl0", "dl1", "dn", "rsend", "dad", "dy1", "doc", "dy"]
 for _t in range(3):
     SEMAPHORES += ["rq%d" % _t, "rl%d" % _t]
 
-WAKE, LOCAL, REMOTE, CYC = 220.0, 2200.0, 2800.0, 0.87
-PASSES, SLIP, PIECE = 1, 20.0, 8
+WAKE, LOCAL, REMOTE, CYC = 220.0, 1800.0, 2800.0, 0.87
+PASSES, SLIP, PIECE, PUSH = 30, 20.0, 8, 0.1
+SIB = 1.0
+E0_ = 12000.0
+E4_ = 2000.0
+E5_ = 1000.0
+E1_, E2_, E3_ = 12000.0, 500.0, 6000.0
 BONDV = 2
 ORDER = []
 
@@ -192,7 +200,7 @@ def rank_program(g, core, T, topo):
         o = W("ps%d" % bank, 0, width(rq))
         node("t", lambda: g.tensor.matmul_mx(ap(o), ap(lq), ap(ls), ap(rq), ap(rs), start, stop), [lq, ls, rq, rs], [o], 60 + 0.63 * (width(rq) + 16), chain=not start)
 
-    def dmas(q, sem, items):
+    def dmas(q, sem, items, more=0.0):
         def side(v):
             if isinstance(v, tuple) and v[0] == "C":
                 return ap(v[1]).bitcast(dt.uint8), [v[1]]
@@ -202,7 +210,7 @@ def rank_program(g, core, T, topo):
         def call():
             for (o, _w), (a, _r) in sides:
                 queue[q].dma_start(o, a).then_inc(T.sem[sem], 16)
-        node(q, call, [v for _o, a in sides for v in a[1]], [v for o, _a in sides for v in o[1]], 60.0 * len(items), "dma", LOCAL, sem=sem, total=16 * len(items))
+        node(q, call, [v for _o, a in sides for v in a[1]], [v for o, _a in sides for v in o[1]], 60.0 * len(items), "dma", LOCAL + more, sem=sem, total=16 * len(items))
 
     nxt, prv = T.cores[(rank + 1) % len(T.cores)], T.cores[(rank - 1) % len(T.cores)]
     a_nxt, m_nxt = topo.addr(nxt), topo.mask(core, nxt)
@@ -217,11 +225,12 @@ def rank_program(g, core, T, topo):
                 g.remote_dma(o, i, T.sem[sem], T.sem["rsend"], a_nxt[1], a_nxt[0], m_nxt)
         node("g", call, [src for _o, src, _c in items], [out for out, _s, _c in items], 400.0 * len(items), "send", REMOTE + 600.0 * (len(items) - 1), sem=sem, total=e_in * len(items), left=e_out * len(items))
 
-    dmas("y", "dx", [("XT", T.x[:, :])])
-    dmas("s", "du", [("UT", T.u[:, :])])
+    dmas("s", "du", [("UT", T.u[:, :])], 500.0)
+    for k in range(2):
+        dmas("ys"[k], "dx%d" % k, [(W("XT", 640 * k, 640 * k + 640), T.x[:, 640 * k:640 * k + 640])], 600.0)
     for y in range(2):
         dmas("ys"[y], "dl%d" % y, [(W("LBI", 0, 20, 1, 8 * y + t, 128, 16), T.nb[16 * t + y:16 * t + 16:2, :]) for t in range(8)])
-    dmas("y", "dn", [(W("NBI", 0, 160, 1, 16 * k, 16 * k + 16), T.nb[:, :]) for k in (0, 1)])
+    dmas("y", "dn", [(W("NBI", 0, 160, 1, 16 * k, 16 * k + 16), T.nb[:, :]) for k in range(4)])
     for e in range(2):
         dmas("ys"[e], "dp%d" % e, [(W("PI", 16 * par, 16 * par + 16, 1, 32 * a + 16 * e, 32 * a + 16 * e + 16),
                                     T.p[32 * a + 16 * par:32 * a + 16 * par + 16, 16 * e:16 * e + 16]) for a in range(4) for par in range(2)])
@@ -239,9 +248,10 @@ def rank_program(g, core, T, topo):
     iota(W("ULF", 0, 8), [[0, 8]], 112, 0)
     iota(W("ULF", 8, 24), [[16, 2], [32, 4], [0, 2]], 0, 0)
     ts(W("ULU", 0, 8), W("ULF", 0, 8), ch, mul)
-    cp(W("ULU", 8, 24), W("ULF", 8, 24))
+    iota(W("ULF", 24, 32), [[112, 2], [0, 4]], 0, 0)
+    cp(W("ULU", 8, 32), W("ULF", 8, 32))
     quant("uq", "us", "UT")
-    for k in range(3):
+    for k in range(4):
         ul, o = W("ULU", 8 * k, 8 * k + 8), W("ur", 128 * k, 128 * k + 128)
         node("v", lambda ul=ul, o=o: g.vector.tensor_copy(ap(o).bitcast(dt.uint32), ap("uq").bitcast(dt.uint32).indirect(ap(ul))), ["uq", ul], [o], 215.0)
         act(W("urs", 128 * k, 128 * k + 128), I("us", ul))
@@ -249,9 +259,10 @@ def rank_program(g, core, T, topo):
         quant(W("mq0", 160 * k, 160 * k + 160), W("ms0", 160 * k, 160 * k + 160), W("XT", 640 * k, 640 * k + 640))
     ZERO = 2048
     iota(W("IOTA", ZERO, ZERO + 320), [[1, 320]], 0, 0)
-    for k in list(range(ZERO + 320, 4096, 320)) + list(range(ZERO - 320, -320, -320)):
-        a, b = max(k, 0), min(k + 320, 4096)
-        act(W("IOTA", a, b), W("IOTA", ZERO + a - k, ZERO + b - k), bias=float(k - ZERO))
+    for k in list(range(ZERO + 320, 4096, 320)) + [ZERO - 320]:
+        b = min(k + 320, 4096)
+        act(W("IOTA", k, b), W("IOTA", ZERO, ZERO + b - k), bias=float(k - ZERO))
+    iota(W("IOTA", 0, ZERO - 320), [[1, ZERO - 320]], -ZERO, 0)
     CELLS, CELLM, COLS = W("IOTA", ZERO, ZERO + 320), W("IOTA", ZERO - MID, ZERO - MID + 320), W("IOTA", ZERO, ZERO + 640)
     fill("BY", 0.0)
     for k in (0, 1, 6, 7):
@@ -260,82 +271,92 @@ def rank_program(g, core, T, topo):
         select(W("CB", 384 * e, 384 * e + 128), "BY", [[0, 2], [-16, 8], [0, 8]], -8 * e, 1)
         cp(W("CB", 128 + 128 * e, 256 + 128 * e), W("CB", 384 * e, 384 * e + 128))
     quant("bq", "bs", "CB")
+    act(W("CB3", 0, 512, 2), W("CB", 0, 512, 2))
+    act(W("CB3", 1, 512, 2), W("CB", 1, 512, 2), 1280.0)
+    quant("bq3", "bs3", "CB3")
+    iota(W("NB8", 2560, 2880), [[16, 20], [0, 8], [8, 2]], 0, 0)
+    for k in range(1, 8):
+        act(W("NB8", 2560 + 320 * k, 2880 + 320 * k), W("NB8", 2560, 2880), bias=float(k))
+        nodes[-1]["early"] = 6000.0
+    ts(pc(5), pc(0), 1, bw)
+    ts(pc(6), pc(0), 1, shr, 7, bw)
+    ts(pc(7), pc(0), 4, shr)
+    cp(W("PCF", 28, 31), W("PCI", 5, 8))
+    ts(pf(29), pf(29), 16.0, mul, pf(28), add)
+    ts(pf(30), pf(30), 2.0, mul, pf(29), add)
+    ts("LS", W("IOTA", ZERO, ZERO + 320, 128), pf(30), add, 319.0, mn_)
     fill("DT", 0.0)
-    fill("ZT", 0.0)
-    quant(W("dq", 128, 256), W("dsc", 128, 256), "ZT")
+    quant(W("dq", 128, 256), W("dsc", 128, 256), "DT")
     fill("K8", 0.0)
     fill(W("K8", 0, 320, 8), -FAR)
     cp("LB", "LBI")
-    for k in range(4):
-        cp(Q("NBL", k), Q("NBI", 0))
+    for k in range(2):
+        cp(Q("NBL", 2 * k, 2), Q("NBI", 0, 2))
     for k in range(8):
-        (act if k < 7 else cp)(W("NB8", 320 * k, 320 * k + 320), I(CELLS, W("NBL", 20 * k, 20 * k + 20)))
-    iota("CIDX", [[16, 20]], 0, 0)
+        (act if k < 6 else cp)(W("NB8", 320 * k, 320 * k + 320), I(CELLS, W("NBL", 20 * k, 20 * k + 20)))
+        nodes[-1]["early"] = E5_
     ts(pf(5), c7, 320.0, mul, ch, add)
-    ts("CIDX", "CIDX", pf(5), add)
+    ts("CIDX", W("IOTA", ZERO, ZERO + 320, 16), pf(5), add)
     act(W("KT", 320, 640), CELLS)
     iota("FM", [[0, 32], [1, 16]], 0, 0)
     ts("MASK", "FM", cq, eq)
     fill("KEEP", 1.0)
     fill(W("KEEP", 0, 512, 16), 0.0)
-    fill(W("ST", 640, 960), 0.0)
-    for k in ("DE", "DO", "DL", "D0E", "D0O", "D0L", "DC"):
+    iota(W("ST", 640, 960), [[0, 320]], 0, 0)
+    for k in ("DE", "DO", "D0E", "D0O", "D0L"):
         fill(k, 0.0)
     for k in ("D0E", "D0O"):
-        fill(W(k, 2, 112, 7), -1.0)
-        fill(W(k, 6, 112, 7), 1.0)
-    fill(W("D0L", 2, 64, 4), -1.0)
-    fill(W("D0L", 3, 64, 4), 1.0)
+        fill(W(k, 2, 96, 6), -1.0)
+        fill(W(k, 5, 96, 6), 1.0)
     ts(W("R", 0, 32), "PI", 0.0, add)
     fill("ON", 0.5)
+    for n in nodes[-2:]:
+        n["early"] = E0_
     for b in range(4):
         select("CT%d" % b, "ON", [[1, 512]], -b, -4)
         quant("eq%d" % b, "es%d" % b, "CT%d" % b)
-    iota(Q(W("KR", 0, 16), 0), [[16, 16]], -ZERO, 1)
-    ts(pf(6), ce, 240.0, mul)
-    ts(Q(W("NN", 7, 128, 8), 0), Q(W("KR", 0, 16), 0), Q(pf(6), 0), add)
-    fill("KEEP8", 1.0)
-    fill(W("KEEP8", 0, 128, 8), 0.0)
-    fill(W("CMP", 512, 513), -256.0)
-    fill(W("CMP", 513, 514), -255.0)
-    iota("CE", [[16, 32]], 128, 0)
-    ts("CE", "CE", cq, add)
+        nodes[-1]["early"] = E1_
+    mark = len(nodes)
+    act(pf(6), cq, 1.0 / 512, -ZERO / 512 - 1.0)
+    act(pf(6), ce, 0.5, pf(6))
+    act(Q("PLK", 0), Q(W("IOTA", ZERO, ZERO + 256, 16), 0), 1.0 / 512, Q(pf(6), 0))
+    for name, k in (("KEEP8", 12), ("KEEP3", 5), ("KP", 16)):
+        iota(name, [[0, width(name)]], 1, 0)
+        iota(W(name, 0, width(name), k), [[0, width(name) // k]], 0, 0)
+    iota(W("KP", 1, 128, 17), [[0, 8]], 0, 0)
+    iota("KEEPH", [[0, 512]], 1, 0)
+    iota(W("KEEPH", 0, 512, 256), [[0, 2]], 0, 0)
+    act("CE", W("IOTA", ZERO + 128, ZERO + 640, 16), bias=cq)
     act("ENT", W("IOTA", ZERO, ZERO + 512), 1.0 / 2048)
     RHO = W("IOTA", ZERO + 1, ZERO + 9)
+    act(pf(13), cq, 16.0)
+    act(pf(31), cq, 16.0, 15.0)
+    act("T2", RHO, -2.0, 16.0)
     ts("NF", RHO, cq, le)
     tt("TF", "NF", RHO, mul)
-    ts("T2", "TF", cq, sub, -16.0, mul)
-    ts("LI", "T2", 15.0, add)
-    ts("T3", "TF", -2.0, mul)
+    ts("LI", "TF", -16.0, mul, pf(31), add)
+    tt("T3", "NF", "T2", mul)
     tt("T3", "T3", RHO, add)
-    ts("NF", "NF", 16.0, mul)
-    tt("T3", "T3", "NF", add)
     ts("LJ", "T3", 16.0, mul, 15.0, add)
-    fill("KP", 1.0)
-    fill(W("KP", 0, 128, 16), 0.0)
-    fill(W("KP", 1, 128, 17), 0.0)
-    ts(pf(7), cq, 17.0, mul, -17.0, add)
-    ts(pf(8), cq, -16.0, mul, 255.0, add)
-    ts(pf(9), pf(7), pf(8), mn_)
+    act(pf(7), cq, 17.0, -17.0)
+    act(pf(8), cq, -16.0, 255.0)
     for e in range(2):
-        ts(pf(14 + e), cq, 0.0, eq, 273.0 - 128 * e, mul)
-        ts(pf(14 + e), pf(14 + e), pf(9), add)
-        ts(W("LE", e, e + 1), pf(14 + e), 128.0 * e, add)
-    fill(W("EQS", 256, 272), 0.0)
+        ts(pf(9), pf(7), pf(8), mn_, 128.0 * e, add)
+        ts(pf(14), cq, 0.0, eq, 273.0 - 128 * e, mul)
+        ts(W("LE", e, e + 1), pf(14), pf(9), add)
+    iota(W("EQS", 256, 272), [[0, 16]], 0, 0)
     iota("LOWC", [[16, 20], [0, 2], [1, 16]], 0, 0)
-    ts(pc(5), pc(0), 1, bw)
-    lo, hi, lo2 = pf(16), pf(17), pf(18)
-    ts(lo, pc(5), 0.0, add)
-    ts(hi, pc(5), -1.0, mul, 1.0, add)
-    ts(lo2, pc(5), 2.0, mul)
-    ts(pf(10), ce, 4096.0, mul, hi, mul)
-    ts(pf(11), hi, 2048.0, mul, pf(10), add)
-    ts(pf(19), hi, 16384.0, mul)
-    ts(pf(12), ce, -1.0, mul, 1.0, add)
-    ts(pf(12), pf(12), pf(19), mul)
+    lo, hi, lo2 = pf(28), pf(17), pf(18)
+    act(hi, lo, -1.0, 1.0)
+    act(lo2, lo, 2.0)
+    act(pf(19), hi, 16384.0)
+    act(pf(16), ce, 4096.0)
+    act(pf(10), pf(16), hi, 0.0)
+    act(pf(11), hi, 2048.0, pf(10))
+    act(pf(12), pf(10), -4.0, pf(19))
 
     def split(k, out, src, scale, high, low):
-        ts(pf(k), lo, float(low - high), mul, float(high), add)
+        act(pf(k), lo, float(low - high), float(high))
         act(out, src, scale, pf(k))
     split(20, W("YC", 0, 128), W("IOTA", ZERO, ZERO + 128), lo, 0, 0)
     split(21, W("YC", 128, 192), W("IOTA", ZERO, ZERO + 64), lo2, 0, 129)
@@ -345,18 +366,18 @@ def rank_program(g, core, T, topo):
     split(26, W("LOWB", 0, 256), W("LOWC", 0, 256), lo, 3 * 2048 + 1024, 128)
     split(27, W("LOWB", 256, 640), W("LOWC", 256, 640), lo, 3 * 2048 + 1280, -128)
     for t in range(BONDV):
-        act(W("YW%d" % t, 128, 1152, 2), W("IOTA", ZERO, ZERO + 512), 0.0)
-    fill("KEEP2", 1.0)
-    fill(W("KEEP2", 0, 512, 2), 0.0)
+        iota(W("YW%d" % t, 128, 1152, 2), [[0, 512]], 0, 0)
+    iota("KEEP2", [[0, 256], [1, 2]], 0, 0)
     iota("REVF", [[256, 2], [1, 16]], 0, 0)
-    ts(pf(13), cq, 16.0, mul)
     ts("REV", "REVF", pf(13), add)
+    for n in nodes[mark:]:
+        n["early"] = E2_
     quant("vq", "vs", "VT")
 
     MASK, KEEP = (lambda n: W("MASK", 0, n)), (lambda n: W("KEEP", 0, n))
-    slot = lambda name, k: W(name, k, 64, 4)
+    slot = lambda name, k: W(name, k, 32, 2)
     ends = lambda name, n=256: W(name, 15, n, 16)
-    E, O = W("R", 0, 16), W("R", 16, 32)
+    E, O, S30, DC = W("R", 0, 16), W("R", 16, 32), W("SD", 0, 32, 2), W("SD", 1, 32, 2)
 
     def lookup(g_, s_, win, off):
         tt(g_, I(win, off), MASK(16 * width(off)), mul)
@@ -366,88 +387,115 @@ def rank_program(g, core, T, topo):
         for q in range(3):
             eng(Q(out, q + 1 if up else q), Q(a, q if up else q + 1))
 
-    run = lambda name, k: W(name, k, 112, 7)
+    run = lambda name, k: W(name, k, 96, 6)
 
     def eight(v, k):
         n, a, _b, st = N(v)[:4]
         return (n, a + 8 * k * st, a + (8 * k + 7) * st + 1, st, 0, 128, 1)
 
-    def best_of(first, last, to_first, to_last):
+    def end_list(first, last):
         for k in range(2):
-            cp(Q("BKU", k), Q(eight(first, k), 0))
-            cp(Q("BKU", 2 + k), Q(eight(last, k), 3))
-        lookup("GK", "SK", "KT", "BKU")
+            if first:
+                cp(Q("BKU", k), Q(eight(first, k), 0))
+            if last:
+                cp(Q("BKU", 2 + k), Q(eight(last, k), 3))
+
+    def end_lookup(table, j, to_first, to_last):
+        lookup("GK%d" % j, "SK%d" % j, table, "BKU")
         for k in range(2):
-            act(Q(eight(to_first, k), 0), Q(ends("SK", 128), k))
-            act(Q(eight(to_last, k), 3), Q(ends("SK", 128), 2 + k))
+            if to_first:
+                cp(Q(eight(to_first, k), 0), Q(ends("SK%d" % j, 128), k))
+            if to_last:
+                act(Q(eight(to_last, k), 3), Q(ends("SK%d" % j, 128), 2 + k))
+
+    def where_equal(y, s3):
+        ts(Q("NZ", 0), Q(s3, 0), 0.0, ne, 320.0, mul)
+        tt(Q("BL", 0), Q("NZ", 0), Q(y, 0), add)
 
     def halfstep(h):
         even = h % 2 == 0
         kk, out, d0, d1 = "KK%d" % h, "OUT%d" % h, ("D0E", "D0O", "D0E", "D0L")[h], ("DE", "DO", "DE", "DL")[h]
         S = W("SI", 15, 256, 16) if even else W("SI", 271, 512, 16)
         if h == 0:
-            y, n, s3, o, dc = E, O, "S30", "NS", "DC"
+            y, n, s3, o, dc = E, O, S30, "NS", DC
         else:
             before = "OUT%d" % (h - 1)
-            y, n, s3, o, dc = run(("DE", "DO", "DE")[h - 1], 2), run(before, 1), run(before, 2), run(before, 5), run(before, 6)
+            y, n, s3, o, dc = run(("DE", "DO", "DE")[h - 1], 2), run(before, 1), run(before, 2), run(before, 4), run(before, 5)
             tt(kk, o, s3, sub)
             cp("KU", kk)
-        tt("GS", I(W("ST", 0, 640) if even else W("ST", 320, 960), "KU"), MASK(256), mul)
+        parts = 2 if h in (0, 3) else 1
+        for k in range(parts):
+            w = 16 // parts
+            lookup(W("GS", 16 * w * k, 16 * w * (k + 1)), W("SS", 16 * w * k, 16 * w * (k + 1)), W("ST", 0, 640) if even else W("ST", 320, 960), W("KU", w * k, w * (k + 1)))
         sl = run if h < 3 else slot
         tt("PR", dc, s3, mul)
         act("NV", "PR", 1e24, func=ACT.Abs)
         tt("SYV", S, "NV", add)
         tt(sl(d1, 0), kk, y, sub)
-        act(sl(d1, 1), y)
-        act(sl(d1, 2), n)
+        for q, k in ((1, 1), (2, 2)) if even else ((0, 3),):
+            act(Q(sl(d1, 1), q, k), Q(y, q, k))
         end = 3 if even else 0
         if h < 3:
-            act(run(d1, 6), n, -1.0)
-            shift(run(d1, 4), run(d1, 0), not even, act)
-            shift(run(d1, 5), y, not even, act)
-            act(Q(run(d1, 5), end), Q(n, end))
-            ts(Q(run(d1, 4), end), Q(s3, end), 0.0, eq)
-            tt(Q("Z1", end), Q(kk, end), Q(n, end), eq)
-            tt(Q(run(d1, 3), end), Q("Z1", end), Q(run(d1, 4), end), sub)
-        if h == 1:
-            best_of(n, kk, "B1", "B1")
-            tt(Q(run("D0O", 5), 0), Q("B1", 0), Q(n, 0), sub)
-            tt(Q("BA", 3), Q("B1", 3), Q("B0", 3), sub)
+            act(sl(d1, 2), n)
+            act(run(d1, 5), n, -1.0)
+            shift(run(d1, 3), run(d1, 0), not even, act)
+            shift(run(d1, 4), y, not even, act)
+            act(Q(run(d1, 4), end), Q(n, end))
+        if h > 0:
+            now = 3 - end
+            tt(Q("BA", now), Q("B0", now), Q(y, now), sub)
+            ts(Q("Z1", now), Q(s3, now), 0.0, eq)
+            tt(Q("BC", now), Q("BA", now), Q("Z1", now), mul)
+            tt(Q(sl(d1, 1), now), Q("BC", now), Q(y, now), add)
+        else:
+            now = 0
+            tt(Q("BC", 0), Q(sl(d1, 1), 0), Q(y, 0), sub)
+        ts(Q(W("NN", 4 + h, 192, 12) if h < 2 else W("N3", h - 1, 80, 5), 0), Q("BC", now), 0.0, ne, -1.0, mul)
+        if h in (1, 2):
+            for q in range(4):
+                cp(Q("BKU", q), Q(eight(n, q % 2), end))
+            lookup("GK1", "SK1", "W%d" % end, "BKU")
+            for q in range(4):
+                to = (W("SI", 15, 256, 16) if end == 0 else W("SI", 271, 512, 16)) if q // 2 == end // 2 else "B0"
+                act(Q(eight(to, q % 2), end), Q(ends("SK1", 128), q))
         if h == 3:
             act(W("R", 48, 64), n)
             act(Q(W("R", 64, 80), 0, 3), Q(o, 0, 3))
             act(Q(W("R", 64, 80), 3), Q(n, 3))
-            act(E, n)
-            tt(Q(slot("DL", 3), 0, 3), Q(o, 0, 3), Q(n, 0, 3), sub)
-        scan("SS", KEEP(256), "GS")
+            act(W("OUT3", 1, 32, 2), n)
+            scan(Q("KS", 0), Q("KEEP8", 0), Q("NN", 0))
+            tt(Q(W("N3", 0, 80, 5), 0), Q(W("KS", 11, 192, 12), 0), Q("PLK", 0), add)
+            for k in range(2):
+                cp(Q("BKU", 2 + k), Q(eight(n, k), 3))
+            lookup("GK0", "SK0", "W3", "BKU")
+            for k in range(2):
+                tt(Q(W("N3", 40 * k + 4, 40 * k + 40, 5), 0), Q(ends("SK0", 128), 2 + k), Q(ends("SK1", 128), 2 + k), gt)
         tt(sl(d0, 1), ends("SS"), "SYV", gt)
         if h < 3:
-            tt(Q(run(d0, 4), end), Q(ends("SS"), end), Q("SYV", end), gt)
             for q in range(3):
                 a, b = (q + 1, q) if even else (q, q + 1)
-                tt(Q(run(d0, 5), b), Q(ends("SS"), a), Q("SYV", a), gt)
-        scan(out, d0, d1)
+                tt(Q(run(d0, 4), b), Q(ends("SS"), a), Q("SYV", a), gt)
+            act(Q(W("NN", 10 + h, 192, 12) if h < 2 else W("N3", 3, 80, 5), 0), Q(run(d0, 1), now))
         if h < 2:
             tt("SG1", ends("SS"), "NV", sub)
             tt(S, S, "SG1", mx_)
-        if h == 1:
-            tt(Q("BC", 3), Q("BA", 3), Q(run(d0, 1), 3), mul)
-            tt(Q("BC", 3), Q("BC", 3), Q("B0", 3), add)
-            tt(Q(run("D0E", 5), 3), Q("BC", 3), Q(run(out, 1), 3), sub)
+        for o_ in [out] if h < 3 else [W(out, 32, 64), W(out, 64, 96)]:
+            scan(o_, d0, d1)
 
     for rd in range(ROUNDS):
         mq, ms, fw, msg = "mq%d" % rd, "ms%d" % rd, "FW%d" % rd, "MSG%d" % rd
         cp("OFFI", W("R", 0, 32))
-        tt("S30", E, O, sub)
+        tt(S30, E, O, sub)
         kk0 = "KK0"
         shift("NS", O, True, act)
-        for q, k in ((1, 1), (2, 2)):
-            tt(Q(kk0, q, k), Q("NS", q, k), Q("S30", q, k), sub)
-            tt(Q("DC", q, k), Q("NS", q, k), Q(E, q, k), sub)
-        cp(Q("KU", 1), Q(kk0, 1))
-        cp(Q("KU", 2, 2), Q(kk0, 2, 2))
-        ts(Q("NZ", 0), Q("S30", 0), 0.0, ne, 320.0, mul)
-        tt(Q("BL", 0), Q("NZ", 0), Q(O, 0), add)
+        act(Q("NS", 0), Q(E, 0))
+        tt(kk0, "NS", S30, sub)
+        tt(DC, "NS", E, sub)
+        for q in range(4):
+            ts(Q(W("NN", q, 192, 6), 0), Q("SD", q), 0.0, eq)
+        cp("KU", kk0)
+        where_equal(E, S30)
+        end_list("BL", O)
         for k in range(2):
             mm(3 * k, W("ur", 0, 128), W("urs", 0, 128), W(mq, 160 * k, 160 * k + 160), W(ms, 160 * k, 160 * k + 160))
             (cp if k else act)(W("W07", 160 * k, 160 * k + 160), W("ps%d" % (3 * k), 0, 160))
@@ -455,23 +503,27 @@ def rank_program(g, core, T, topo):
             mm(k, W("ur", 128 * k, 128 * k + 128), W("urs", 128 * k, 128 * k + 128), mq, ms)
         act(W("ST", 0, 320), W("ps1", 0, 320))
         act(W("ST", 320, 640), W("ps2", 0, 320))
+        mm(0, W("ur", 384, 512), W("urs", 384, 512), mq, ms)
+        act(Q("W0", 0, 2), Q(W("ps0", 0, 320), 0, 2))
+        act(Q("W3", 2, 2), Q(W("ps0", 0, 320), 2, 2))
+        cp("GO", I("W07", "LS"))
         cp(W("GB", 0, 160), I("W07", W("LB", 0, 10)))
         act(W("GB", 160, 320), I("W07", W("LB", 10, 20)))
         scan("RM", "K8", "GB", add, mx_)
         for t in range(7):
             at = 80 * (t // 2) + t % 2
             tt(W("DT", at, at + 79, 2), W("RM", t, 320, 8), W("RM", 7, 320, 8), ne)
+        tt(W("DT", 241, 320, 2), W("GO", 0, 40), W("RM", 7, 320, 8), ge)
         quant(W("dq", 0, 128), W("dsc", 0, 128), "DT")
         for k in range(4):
-            mm(3, "bq", "bs", W("dq", 20 * k, 20 * k + 128), W("dsc", 20 * k, 20 * k + 128), k == 0, k == 3)
+            mm(3, *(("bq", "bs") if k < 3 else ("bq3", "bs3")), W("dq", 20 * k, 20 * k + 128), W("dsc", 20 * k, 20 * k + 128), k == 0, k == 3)
         tt("BI", W("ps3", 0, 20), "CIDX", add)
         cp("BIU", "BI")
         cp(W("KT", 0, 160), I("NB8", W("BIU", 0, 10)))
         act(W("KT", 160, 320), I("NB8", W("BIU", 10, 20)))
-        best_of("BL", O, kk0, "B0")
-        for k in range(2):
-            cp(Q(eight("KU", k), 0), Q(ends("SK", 128), k))
-        tt(Q(run("D0E", 5), 3), Q("B0", 3), Q(O, 3), sub)
+        end_lookup("KT", 0, run("DE", 1), "B0")
+        act(Q("W0", 2, 2), Q(W("KT", 0, 320), 0, 2))
+        act(Q("W3", 0, 2), Q(W("KT", 0, 320), 2, 2))
         for k in range(4):
             lookup(W("GI", 128 * k, 128 * k + 128), W("SI", 128 * k, 128 * k + 128), W("ST", 320 * (k // 2), 320 * (k // 2) + 320), W("OFFI", 8 * k, 8 * k + 8))
         for t in range(4):
@@ -485,26 +537,24 @@ def rank_program(g, core, T, topo):
         act(W("LBW", 0, 640), "LOWB", 0.0, pf(19))
         for h in range(4):
             halfstep(h)
-        act(O, slot("OUT3", 1))
-        act(W("R", 32, 48), slot("OUT3", 1))
-        for k, src in enumerate((W("R", 0, 32), W("R", 16, 48), W("R", 48, 80))):
+        for k, src in enumerate((W("OUT3", 1, 64, 2), W("OUT3", 33, 96, 2), W("R", 48, 80))):
             tr(W("TA", 32 * k, 32 * k + 32), src)
             cp(W("AL", 32 * k, 32 * k + 32), W("TA", 32 * k, 32 * k + 32))
+            nodes[-1]["early"] = (E4_, 0.0, E3_)[k]
         al = W("AL", 0, 32)
-        for k in range(7):
-            ts(Q(W("NN", k, 128, 8), 0), Q(slot("OUT3", 2 + k % 2), k // 2), 0.0, eq, 512.0, mul)
         for k in range(2):
-            scan(Q(W("KD", 128 * k, 128 * k + 128), 0), Q("KEEP8", 0), Q("NN", 0))
-        tr(Q("KR", 0), Q(W("KD", 7, 256, 8), 0))
+            scan(Q(W("KD", 80 * k, 80 * k + 80), 0), Q("KEEP3", 0), Q("N3", 0))
+        tr(Q("KR", 0), Q(W("KD", 4, 160, 5), 0))
         for q in range(4):
-            ts(Q("KL", q), Q("KR", 0), float(ZERO), add)
-            act(Q("NK", q), Q(W("KD", 32 * q + 7, 32 * q + 32, 8), 0))
+            ts(Q("KL", q), Q("KR", 0), 512.0, mul, float(ZERO), add)
+            act(Q("NK", q), Q(W("KD", 20 * q + 4, 20 * q + 20, 5), 0), 512.0)
         cp(W("RK", 0, 256), I("IOTA", W("KL", 0, 16)))
         act(W("RK", 256, 512), I("IOTA", W("KL", 16, 32)))
         for b in range(3):
             act(("SG0", "SG1B", "SG2")[b], "RK", -1.0, W("NK", b, b + 1), ACT.Sign, W("PS", b, b + 1))
         ts(W("CMP", 0, 512), "RK", W("NK", 3, 4), lt, 2.0, mul)
-        red(W("PS", 3, 4), "CMP")
+        scan("CNT", "KEEPH", "CMP")
+        ts(W("PS", 3, 4), W("CNT", 255, 256), W("CNT", 511, 512), add, -511.0, add)
         for q in range(4):
             ts(Q(W("PP", 4 * q, 4 * q + 4), 0), Q("PS", q), 511.0, add, 0.5, mul)
             act(Q(W("PP", 16 + 4 * q, 20 + 4 * q), 0), Q("PS", q), 0.5, 255.5)
@@ -522,9 +572,7 @@ def rank_program(g, core, T, topo):
                 if t < BONDV:
                     zg = W("ZG%d" % t, 256 * k, 256 * k + 256)
                     act(zg, I("FQ%d" % t, W("AL", 64 + 16 * k, 80 + 16 * k)))
-                    for j in range(2):
-                        at = 129 + 512 * k + 256 * j
-                        tt(W("YW%d" % t, at, at + 255, 2), I("FQ%d" % t, W("AL", 32 + 16 * k + 8 * j, 40 + 16 * k + 8 * j)), W("ZG%d" % t, 256 * k + 128 * j, 256 * k + 128 * j + 128), add)
+                    tt(W("YW%d" % t, 129 + 512 * k, 640 + 512 * k, 2), I("FQ%d" % t, W("AL", 32 + 16 * k, 48 + 16 * k)), zg, add)
                     continue
                 for j in range(2):
                     act(W("ZG%d" % t, 512 * k + j, 512 * k + 512, 2), I("FQ%d" % t, W("AL", 64 - 32 * j + 16 * k, 80 - 32 * j + 16 * k)))
@@ -570,6 +618,7 @@ def rank_program(g, core, T, topo):
         if rd + 1 < ROUNDS:
             act("FCF", ends("SCN", 512), bias=float(MID))
             tr(W("R", 0, 32), "FCF")
+            nodes[-1]["rd"].append(N("OFF"))
         else:
             act("RK", I(fw, "SEL"), bias=float(MID))
             act("DP", I("RK", "REV"))
@@ -578,19 +627,19 @@ def rank_program(g, core, T, topo):
             for w in (1, 0):
                 k = 8 * w + y
                 cp(I("LA" if w else "LBW", W("OFF", 2 * k, 2 * k + 2)), W("SELX", 32 * k, 32 * k + 32))
-        tr("TLA", W("LA", 0, 640))
-        tr("TLB", W("LBW", 0, 640))
-        for k, name in enumerate(("TLA", "TLB")):
-            tt(W("VA", 40 * k, 40 * k + 40), W(name, 0, 640, 16), W(name, 1, 640, 16), add)
-        tt("M1", W("VA", 0, 40), W("VA", 40, 80), mn_)
-        tt("M2", W("M1", 0, 40, 2), W("M1", 1, 40, 2), mn_)
-        ts("M3", "M2", 2047, bw)
-        cp("EL", "M3")
-        for t in range(2):
-            tt(W("MT", t, 1280, 4), I("YW%d" % t, "EL"), "FH%d" % t, add)
-            act("G%d" % (2 + t), I("YW%d" % (2 + t), "EL"))
-            tt(W("MT", 2 + t, 1280, 4), W("ps%d" % (6 + t), 0, 320), "G%d" % (2 + t), add)
         for k in range(2):
+            half = lambda name, n: W(name, n * k, n * k + n)
+            for j, win in enumerate(("LA", "LBW")):
+                tr(W("TL", 640 * k + 320 * j, 640 * k + 320 * j + 320), half(win, 320))
+            tt(half("VA", 40), W("TL", 640 * k, 640 * k + 640, 16), W("TL", 640 * k + 1, 640 * k + 640, 16), add)
+            tt(half("M1", 20), W("VA", 40 * k, 40 * k + 20), W("VA", 40 * k + 20, 40 * k + 40), mn_)
+            tt(half("M2", 10), W("M1", 20 * k, 20 * k + 20, 2), W("M1", 20 * k + 1, 20 * k + 20, 2), mn_)
+            ts(half("M3", 10), half("M2", 10), 2047, bw)
+            cp(half("EL", 10), half("M3", 10))
+            for t in range(2):
+                tt(W("MT", 640 * k + t, 640 * k + 640, 4), I("YW%d" % t, half("EL", 10)), half("FH%d" % t, 160), add)
+                act(half("G%d" % (2 + t), 160), I("YW%d" % (2 + t), half("EL", 10)))
+                tt(W("MT", 640 * k + 2 + t, 640 * k + 640, 4), half("ps%d" % (6 + t), 160), half("G%d" % (2 + t), 160), add)
             quant(W("mq%d" % (rd + 1), 160 * k, 160 * k + 160), W("ms%d" % (rd + 1), 160 * k, 160 * k + 160), W("MT", 640 * k, 640 * k + 640))
 
     mq, ms = "mq%d" % ROUNDS, "ms%d" % ROUNDS
@@ -604,7 +653,10 @@ def rank_program(g, core, T, topo):
     for i, n in enumerate(nodes):
         n["pre"], n["post"] = set(), []
         for v, w in [(v, False) for v in n["rd"]] + [(v, True) for v in n["wr"]]:
+            if w:
+                n.setdefault("src", set(n["pre"]))
             n["pre"].update(h["i"] for h in seen.get(v[0], ()) if clash(v, w, n["q"], h))
+        n.setdefault("src", set(n["pre"]))
         for v, w in [(v, False) for v in n["rd"]] + [(v, True) for v in n["wr"]]:
             old = seen.setdefault(v[0], [])
             if w:
@@ -614,7 +666,10 @@ def rank_program(g, core, T, topo):
         for j in n["pre"]:
             nodes[j]["post"].append(i)
     for n in reversed(nodes):
-        n["way"] = n["busy"] + n["after"] + max([WAKE + nodes[j]["way"] for j in n["post"]] or [0.0])
+        n["way"] = n["busy"] + n["after"] + n.get("early", 0.0) + max([WAKE + nodes[j]["way"] for j in n["post"]] or [0.0])
+
+    def beside(i, j):
+        return sum(nodes[k]["busy"] for k in nodes[j]["src"] if k > i and nodes[k]["q"] == nodes[i]["q"])
 
     def lag(i, j):
         return 0.0 if nodes[j].get("chain") and nodes[i]["q"] == "t" else WAKE
@@ -644,13 +699,29 @@ def rank_program(g, core, T, topo):
         return start, done
 
     if not ORDER:
-        start, done = lay([-n["way"] for n in nodes], False)
-        best = (max(done.values()), start)
+        best = None
         for _pass in range(PASSES):
-            _start, done = lay([-done[i] for i in range(len(nodes))], True)
-            start, done = lay([-done[i] for i in range(len(nodes))], False)
-            best = min(best, (max(done.values()), start), key=lambda x: x[0])
-        ORDER.extend(sorted(range(len(nodes)), key=lambda i: (best[1][i], i)))
+            for i in reversed(range(len(nodes))):
+                n = nodes[i]
+                n["way"] = n["busy"] + n["after"] + n.get("early", 0.0) + max([WAKE + nodes[j]["way"] + SIB * beside(i, j) for j in n["post"]] or [0.0])
+            start, _done = lay([-n["way"] for n in nodes], False)
+            order = sorted(range(len(nodes)), key=lambda i: (start[i], i))
+            last, ready, done, cause = {}, {}, {}, {}
+            for i in order:
+                n = nodes[i]
+                ready[i], cause[i] = max([(done[k] + lag(k, i), k) for k in n["pre"]] or [(0.0, None)])
+                start[i] = ready[i]
+                if n["q"] in last and last[n["q"]][0] > ready[i]:
+                    start[i], cause[i] = last[n["q"]]
+                last[n["q"]] = (start[i] + n["busy"], i)
+                done[i] = start[i] + n["busy"] + n["after"]
+            i = max(done, key=done.get)
+            if best is None or done[i] < best[0]:
+                best = (done[i], order)
+            while i is not None:
+                nodes[i]["early"] = nodes[i].get("early", 0.0) + PUSH * min(start[i] - ready[i], 1000.0)
+                i = cause[i]
+        ORDER.extend(best[1])
     order = ORDER
 
     count, know, totals, sent = {k: 0 for k in own}, {k: {} for k in queue}, {}, 0

@@ -1,9 +1,9 @@
-from concourse.mybir import dt, AluOpType, AxisListType, ActivationFunctionType
+from concourse.mybir import dt, AluOpType, ActivationFunctionType
 
 ROUNDS = 3
 FAR = 1e29
+BIG = 2.0 ** 96
 MID = 160
-ROUND = 12582912.0
 F32, BF, I32, U16, MXC, U8 = "float32", "bfloat16", "int32", "uint16", "float8_e4m3fn_x4", "uint8"
 SCRATCH, PART = {}, {}
 
@@ -22,54 +22,68 @@ def _pack(buf, dtype, **kw):
     SCRATCH[buf] = ("sbuf", [128, at], dtype)
 
 
-_sb(BF, XT=1280, MT=1280, UT=512, VT=512, BY=128, ON=512, DT=512, HT=512, CB=512)
+_sb(BF, XT=1280, MT=1280, UT=512, VT=512, BY=128, DT=512, HT=512, CB=512)
+_pack("ONB", BF, ON=512, ON4=512)
 _pack("CTB", BF, CT0=512, CT1=512, CT2=512, CT3=512)
-_pack("YW", BF, YW0=1472, YW1=1472, YW2=1472, YW3=1472)
+_pack("YW", BF, YW0=960, YW1=960, YW2=960, YW3=960)
 _pack("FH", BF, FH0=320, FH1=320)
-_pack("FQ", BF, FQ0=320, FQ1=320, FQ2=320, FQ3=320)
-_pack("ZG", BF, ZG0=1024, ZG1=1024, ZG2=1024, ZG3=1024)
-_sb(BF, KEEP2=512)
+_pack("ZG", BF, ZG0=512, ZG1=512, ZG2=512, ZG3=512)
+_pack("CTC", BF, CU0=512, CU1=512, CU2=512, CU3=512)
+_pack("fqc", MXC, fq0=128, fq1=128, fq2=128, fq3=128)
+_pack("fsc", U8, fs0=128, fs1=128, fs2=128, fs3=128)
+_sb(MXC, zq0=512, zq1=512, zq2=512)
+_sb(U8, zs0=512, zs1=512, zs2=512)
 _sb(F32, YC=640)
 _sb(F32, W07=320, GB=320, RM=320, K8=320, GO=48)
 _sb(BF, CB3=512)
 _sb(MXC, bq3=128)
 _sb(U8, bs3=128)
-_sb(MXC, uq=128, ur=512, vq=128, dq=256, bq=128, wq=512, mq0=320, mq1=320, mq2=320, mq3=320)
-_sb(U8, us=128, urs=512, vs=128, dsc=256, bs=128, wsc=512, ms0=320, ms1=320, ms2=320, ms3=320)
+_sb(MXC, uq=128, ur=640, vq=128, bq=128, wq=512, mq1=320, mq2=320, mq3=320)
+_sb(U8, us=128, urs=640, vs=128, bs=128, wsc=512, ms1=320, ms2=320, ms3=320)
+_pack("dqm", MXC, dq=128, mq0=320)
+_pack("dsm", U8, dsc=128, ms0=320)
 _sb(MXC, aq0=128, aq1=128, aq2=128, lq0=128, lq1=128, lq2=128)
 _sb(U8, as0=128, as1=128, as2=128, ls0=128, ls1=128, ls2=128)
 _pack("eqc", MXC, eq0=128, eq1=128, eq2=128, eq3=128)
 _pack("esc", U8, es0=128, es1=128, es2=128, es3=128)
-_sb(F32, IOTA=4096, LOWC=640, ENT=512)
-_sb(BF, MASK=512, KEEP=512, KP=128, G2=320, G3=320)
-_pack("KC", F32, PCF=32, CE=32, CIDX=20, ULF=32, LSF=4, NF=8, TF=8, T2=8, T3=8, REVF=32)
-_sb(I32, PCI=8, LBI=20, NBI=160, PI=32)
-_pack("KU16", U16, ULU=32, LS=3, LB=20, NBL=160, LI=8, LJ=8, LE=2, REV=32)
-_sb(F32, ST=960, NB8=5120, KT=640, YO=320, W0=320, W3=320)
-_pack("HB", F32, R=80, SD=32, NS=16, NZ=16, BL=16, DE=96, DO=96, DL=32, D0E=96, D0O=96, D0L=32, OUT0=96, OUT1=96, OUT2=96, OUT3=96,
-      Z1=16, KK0=16, KK1=16, KK2=16, KK3=16, PR=16, NV=16, SYV=16, SG1=16, BA=16, BC=16, BI=20, GS=256, SS=256, GK0=128, SK0=128, GK1=128, SK1=128, B0=16, GI=512, SI=512)
-_pack("OB", F32, PLK=16, NN=192, KEEP8=192, KS=192, N3=80, KEEP3=80, KD=160, KR=32, NK=4, PS=4, PP=32, PT=32, TA=96, PF=32, T1=32, TM=32, SELF=32, VT_=32, G8=128, S8=128,
-      E1=8, E2=8, FCF=32, PP_=32, LZD=32, OF=32, OT=32, M1=40)
-_sb(F32, RK=512, DP=512, SRT=512, VA=80)
-_sb(BF, LA=10240, LBW=10240, TL=1280, SELX=512, LOWB=640)
-_sb(BF, SG0=512, SG1B=512, SG2=512, CMP=512, CNT=512, KEEPH=512, FM=512, SCN=512, PA_=256, PB_=256, EQ=256, EQS=272, MSG0=128, MSG1=128, MSG2=128, FW0=640, FW1=640, FW2=640)
-_pack("HI", I32, FCI=32, FA=32, M2=20, M3=20)
-_pack("HU", U16, OFFI=32, KU=16, BKU=8, BIU=20, AL=96, KL=32, PA=32, SEL=32, VL=32, EL2=8, OFF=32, EL=20)
+_sb(F32, IOTA=4096, LOWC=640)
+_sb(BF, MASK=256, KEEP=256, KP=128, G2=320, G3=320)
+_pack("KC", F32, PCF=32, CE=32, CIDX=20, ULF=40, NF=8, TF=8, T2=8, T3=8, REVF=32)
+_sb(I32, PCI=8, LBI=20, NBI=160, PI=32, PL=32)
+_pack("KU16", U16, ULU=40, LS=3, LB=20, NBL=160, LI=8, LJ=8, LE=2, REV=32)
+_sb(F32, ST=960, NB8=2576, KT=960, YO=320, SN=320)
+_pack("HB", F32, NS=16, R=80, SD=32, SE0=32, NZ=16, BL=16, DE=96, DO=96, DL=48, D0E=96, D0O=96, D0L=48, OUT0=96, OUT1=96, OUT2=96, OUT3=144,
+      Z1=16, KK0=16, KK1=16, KK2=16, KK3=16, PR=16, NV=16, SYV=16, SG1=16, KY=16, NE=16, S6=16, A7=16, NBF=160, NBC=160, BC=16, BI=20,
+      GS=256, SS=256, GK0=128, SK0=128, GK1=128, SK1=128, B0=16, GI=512, SI=512, AB=64, AT=64, UF=32)
+_pack("OB", F32, NN=128, KEEP8=128, KS=128, N5=112, KEEP5=112, K5=112, N3=128, K3=128, KD=256, KR=32, NK=4, PS=8, PP=32, PT=32, TA=96,
+      PF=32, T1=32, TM=32, SELF=32, VT_=32, E4=32, E8=16, ES=32, KEEP4=32, FCF=32, PP_=32, LZD=32, OF=32, OT=32, XD=80, XS=80)
+_sb(F32, RK=512, DP=512, VA=80)
+_sb(BF, ENT=128, SRT=512, G8=128, S8=128, FW=1024, FWP=512)
+_sb(U16, ao0=32, ao1=32, ao2=32, po0=32, po1=32, po2=32)
+_sb(U16, al0=32, al1=32, al2=32, pa0=32, pa1=32, pa2=32)
+_sb(BF, LA=10240, LBW=10240, TL=1280, SELX=512, LAI=640, LBI0=160)
+_pack("SGN", BF, SG0=512, SG1B=512, SG2=512, CMP=512, CNT=512, KEEPH=512)
+_sb(BF, FM=512, SCN=512, PB_=256, EQ=256, EQS=272)
+_pack("HI", I32, FCI=32, FA=32)
+_pack("HU", U16, OFFI=32, KU=16, BKU=8, BK2=8, BIU=20, AL=96, KL=32, PQ=8, SEL=32, VL=32, EL2=8, OFF=32, EL=20)
 for _t in range(8):
     SCRATCH["ps%d" % _t] = ("psum", [128, 512], F32)
 
-SEMAPHORES = ["sv", "st", "ss", "sg", "dx0", "dx1", "du", "dv", "dw", "dp0", "dp1", "dl0", "dl1", "dn", "rsend", "dad", "dy1", "doc", "dy"]
+SEMAPHORES = ["sv", "st", "ss", "sg", "dx0", "dx1", "du", "dv", "dw", "dp0", "dp1", "dp2", "dl0", "dl1", "dn", "rsend", "dad", "dy1", "doc", "dy"]
 for _t in range(3):
-    SEMAPHORES += ["rq%d" % _t, "rl%d" % _t]
+    SEMAPHORES += ["rq%d" % _t, "rl%d" % _t, "ra%d" % _t, "dla%d" % _t, "dlb%d" % _t]
 
-WAKE, LOCAL, REMOTE, CYC = 220.0, 1800.0, 2800.0, 0.87
-PASSES, SLIP, PIECE, PUSH = 30, 20.0, 8, 0.1
-SIB = 1.0
+WAKE, LOCAL, REMOTE, FIRST, CYC = 220.0, 1800.0, 2400.0, 2000.0, 0.87
+PASSES, SLIP, SEED = 4000, 20.0, 1
+SLACK = 0.001
+CASES = ((220.0, 1.0, 0.0, 0.0, 0.0, 0.0), (160.0, 0.95, -0.25, -0.7, -500.0, 0.0), (220.0, 1.25, 0.4, 0.5, 1000.0, 600.0))
+PER_ROUND = ("mq", "ms", "aq", "as", "lq", "ls", "al", "pa", "ao", "po", "zq", "zs")
 E0_ = 12000.0
 E4_ = 2000.0
+E6_ = 2000.0
 E5_ = 1000.0
 E1_, E2_, E3_ = 12000.0, 500.0, 6000.0
-BONDV = 2
+SP, VP, VS = 16, 16, 16
 ORDER = []
 
 
@@ -143,6 +157,8 @@ def rank_program(g, core, T, topo):
         for v in map(N, writes):
             wr.append(v[1] if v[0] == "I" else v)
             rd += [v[2]] if v[0] == "I" else []
+        more["gathers"] = sum(width(v) for v in reads if N(v)[0] == "I")
+        more["scatters"] = sum(width(v) for v in writes if N(v)[0] == "I")
         nodes.append(dict(q=q, call=call, rd=rd, wr=wr, busy=busy, kind=kind, after=after, **more))
 
     def cp(out, a):
@@ -150,8 +166,7 @@ def rank_program(g, core, T, topo):
 
     def tt(out, a, b, o):
         per = 1.0 if N(a)[0].startswith("ps") else 2.0
-        node("v", lambda: g.vector.tensor_tensor(ap(out), ap(a), ap(b), o), [a, b], [out], cost(out, [a, b], per),
-             drain=N(a)[0] != "I" and N(a)[4] != N(b)[4])
+        node("v", lambda: g.vector.tensor_tensor(ap(out), ap(a), ap(b), o), [a, b], [out], cost(out, [a, b], per))
 
     def ts(out, a, s1, o0, s2=None, o1=None):
         x1, x2 = [ap(s) if isinstance(s, tuple) else s for s in (s1, s2)]
@@ -160,9 +175,6 @@ def rank_program(g, core, T, topo):
 
     def scan(out, d0, d1, o0=mul, o1=add, first=0.0):
         node("v", lambda: g.vector.tensor_tensor_scan(ap(out), ap(d0), ap(d1), first, o0, o1), [d0, d1], [out], cost(out, [d0, d1]))
-
-    def red(out, a):
-        node("v", lambda: g.vector.tensor_reduce(ap(out), ap(a), AxisListType.X, add), [a], [out], CYC * width(a))
 
     def fill(out, c):
         out = N(out)
@@ -186,19 +198,23 @@ def rank_program(g, core, T, topo):
         if acc is not None:
             more["accum_out"] = ap(acc)
         f = func or (ACT.Copy if bias is None else ACT.Identity)
-        busy = cost(out, [a]) if N(a)[0] == "I" else CYC * max(64.0, width(a))
-        node("s", lambda: g.scalar.activation(ap(out), ap(a), f, **more), [a] + [x for x in (bias, scale) if isinstance(x, tuple)], [out] + ([acc] if acc else []), busy + 20)
+        busy = cost(out, [a]) + 10 if N(a)[0] == "I" else CYC * max(64.0, width(a))
+        node("s", lambda: g.scalar.activation(ap(out), ap(a), f, **more), [a] + [x for x in (bias, scale) if isinstance(x, tuple)], [out] + ([acc] if acc else []), busy + (20 if acc else 5))
 
     def iota(out, pattern, base, mult):
         more = {} if SCRATCH[N(out)[0]][2] == I32 else {"allow_small_or_imprecise_dtypes": True}
-        node("g", lambda: g.iota(ap(out), pattern, base, mult, **more), [], [out], 130 + WAKE + 2.0 * width(out))
+        node("g", lambda: g.iota(ap(out), pattern, base, mult, **more), [], [out], 130 + 1.75 * width(out))
 
     def select(out, a, pattern, base, mult):
-        node("g", lambda: g.affine_select(ap(out), ap(a), pattern, eq, 0.0, base, mult), [a], [out], 170 + WAKE + 2.0 * width(out))
+        node("g", lambda: g.affine_select(ap(out), ap(a), pattern, eq, 0.0, base, mult), [a], [out], 170 + 1.75 * width(out))
 
     def mm(bank, lq, ls, rq, rs, start=True, stop=True):
         o = W("ps%d" % bank, 0, width(rq))
-        node("t", lambda: g.tensor.matmul_mx(ap(o), ap(lq), ap(ls), ap(rq), ap(rs), start, stop), [lq, ls, rq, rs], [o], 60 + 0.63 * (width(rq) + 16), chain=not start)
+        node("t", lambda: g.tensor.matmul_mx(ap(o), ap(lq), ap(ls), ap(rq), ap(rs), start, stop), [lq, ls, rq, rs], [o], 30 + 0.63 * (width(rq) + 16), chain=not start)
+
+    def pick_codes(q, s, from_q, from_s, by):
+        node("v", lambda: g.vector.tensor_copy(ap(q).bitcast(dt.uint32), ap(from_q).bitcast(dt.uint32).indirect(ap(by))), [I(from_q, by)], [q], 55 + 20.0 * width(by))
+        act(s, I(from_s, by))
 
     def dmas(q, sem, items, more=0.0):
         def side(v):
@@ -215,6 +231,7 @@ def rank_program(g, core, T, topo):
     nxt, prv = T.cores[(rank + 1) % len(T.cores)], T.cores[(rank - 1) % len(T.cores)]
     a_nxt, m_nxt = topo.addr(nxt), topo.mask(core, nxt)
     e_out, e_in = len(topo.engines(core, nxt)), len(topo.engines(prv, core))
+    sends = []
 
     def send(sem, items):
         def call():
@@ -223,17 +240,20 @@ def rank_program(g, core, T, topo):
                 if code:
                     o, i = o.bitcast(dt.uint8), i.bitcast(dt.uint8)
                 g.remote_dma(o, i, T.sem[sem], T.sem["rsend"], a_nxt[1], a_nxt[0], m_nxt)
-        node("g", call, [src for _o, src, _c in items], [out for out, _s, _c in items], 400.0 * len(items), "send", REMOTE + 600.0 * (len(items) - 1), sem=sem, total=e_in * len(items), left=e_out * len(items))
+        node("g", call, [src for _o, src, _c in items], [out for out, _s, _c in items], 400.0 * len(items) + (0.0 if sends else FIRST), "send",
+             REMOTE + 600.0 * (len(items) - 1), sem=sem, total=e_in * len(items), left=e_out * len(items))
+        sends.append(sem)
 
     dmas("s", "du", [("UT", T.u[:, :])], 500.0)
     for k in range(2):
         dmas("ys"[k], "dx%d" % k, [(W("XT", 640 * k, 640 * k + 640), T.x[:, 640 * k:640 * k + 640])], 600.0)
     for y in range(2):
-        dmas("ys"[y], "dl%d" % y, [(W("LBI", 0, 20, 1, 8 * y + t, 128, 16), T.nb[16 * t + y:16 * t + 16:2, :]) for t in range(8)])
+        dmas("y", "dl%d" % y, [(W("LBI", 0, 20, 1, 8 * y + t, 128, 16), T.nb[16 * t + y:16 * t + 16:2, :]) for t in range(8)])
     dmas("y", "dn", [(W("NBI", 0, 160, 1, 16 * k, 16 * k + 16), T.nb[:, :]) for k in range(4)])
     for e in range(2):
-        dmas("ys"[e], "dp%d" % e, [(W("PI", 16 * par, 16 * par + 16, 1, 32 * a + 16 * e, 32 * a + 16 * e + 16),
-                                    T.p[32 * a + 16 * par:32 * a + 16 * par + 16, 16 * e:16 * e + 16]) for a in range(4) for par in range(2)])
+        dmas("y", "dp%d" % e, [(W("PI", 16 * par, 16 * par + 16, 1, 32 * a + 16 * e, 32 * a + 16 * e + 16),
+                                    T.p[32 * a + 16 * par:32 * a + 16 * par + 16, 16 - 16 * e:32 - 16 * e]) for a in range(4) for par in range(2)])
+    dmas("y", "dp2", [("PL", T.p[:, :])])
     dmas("y", "dw", [(("C", "wq"), T.wc[:, :]), ("wsc", T.ws[:, :])])
     dmas("y", "dv", [("VT", T.v[:, :])])
 
@@ -248,13 +268,12 @@ def rank_program(g, core, T, topo):
     iota(W("ULF", 0, 8), [[0, 8]], 112, 0)
     iota(W("ULF", 8, 24), [[16, 2], [32, 4], [0, 2]], 0, 0)
     ts(W("ULU", 0, 8), W("ULF", 0, 8), ch, mul)
-    iota(W("ULF", 24, 32), [[112, 2], [0, 4]], 0, 0)
-    cp(W("ULU", 8, 32), W("ULF", 8, 32))
+    iota(W("ULF", 24, 32), [[-112, 2], [0, 4]], 112, 0)
+    iota(W("ULF", 32, 40), [[16, 8]], 0, 0)
+    cp(W("ULU", 8, 40), W("ULF", 8, 40))
     quant("uq", "us", "UT")
-    for k in range(4):
-        ul, o = W("ULU", 8 * k, 8 * k + 8), W("ur", 128 * k, 128 * k + 128)
-        node("v", lambda ul=ul, o=o: g.vector.tensor_copy(ap(o).bitcast(dt.uint32), ap("uq").bitcast(dt.uint32).indirect(ap(ul))), ["uq", ul], [o], 215.0)
-        act(W("urs", 128 * k, 128 * k + 128), I("us", ul))
+    for a, b in ((0, 1), (1, 3), (3, 5)):
+        pick_codes(W("ur", 128 * a, 128 * b), W("urs", 128 * a, 128 * b), "uq", "us", W("ULU", 8 * a, 8 * b))
     for k in range(2):
         quant(W("mq0", 160 * k, 160 * k + 160), W("ms0", 160 * k, 160 * k + 160), W("XT", 640 * k, 640 * k + 640))
     ZERO = 2048
@@ -263,7 +282,7 @@ def rank_program(g, core, T, topo):
         b = min(k + 320, 4096)
         act(W("IOTA", k, b), W("IOTA", ZERO, ZERO + b - k), bias=float(k - ZERO))
     iota(W("IOTA", 0, ZERO - 320), [[1, ZERO - 320]], -ZERO, 0)
-    CELLS, CELLM, COLS = W("IOTA", ZERO, ZERO + 320), W("IOTA", ZERO - MID, ZERO - MID + 320), W("IOTA", ZERO, ZERO + 640)
+    CELLS, CELLM = W("IOTA", ZERO, ZERO + 320), W("IOTA", ZERO - MID, ZERO - MID + 320)
     fill("BY", 0.0)
     for k in (0, 1, 6, 7):
         fill(W("BY", k, 128, 8), 2.0)
@@ -274,10 +293,8 @@ def rank_program(g, core, T, topo):
     act(W("CB3", 0, 512, 2), W("CB", 0, 512, 2))
     act(W("CB3", 1, 512, 2), W("CB", 1, 512, 2), 1280.0)
     quant("bq3", "bs3", "CB3")
-    iota(W("NB8", 2560, 2880), [[16, 20], [0, 8], [8, 2]], 0, 0)
-    for k in range(1, 8):
-        act(W("NB8", 2560 + 320 * k, 2880 + 320 * k), W("NB8", 2560, 2880), bias=float(k))
-        nodes[-1]["early"] = 6000.0
+    iota(W("NB8", 2560, 2576), [[0, 16]], 0, 0)
+    iota("NBC", [[1, 8], [16, 20]], -320, 0)
     ts(pc(5), pc(0), 1, bw)
     ts(pc(6), pc(0), 1, shr, 7, bw)
     ts(pc(7), pc(0), 4, shr)
@@ -285,30 +302,33 @@ def rank_program(g, core, T, topo):
     ts(pf(29), pf(29), 16.0, mul, pf(28), add)
     ts(pf(30), pf(30), 2.0, mul, pf(29), add)
     ts("LS", W("IOTA", ZERO, ZERO + 320, 128), pf(30), add, 319.0, mn_)
-    fill("DT", 0.0)
-    quant(W("dq", 128, 256), W("dsc", 128, 256), "DT")
+    fill(W("DT", 320, 512), 0.0)
     fill("K8", 0.0)
     fill(W("K8", 0, 320, 8), -FAR)
     cp("LB", "LBI")
+    act(pf(9), pf(28), 8.0)
+    tt(Q("NBF", 0, 2), Q("NBI", 0, 2), Q("NBC", 0, 2), sub)
     for k in range(2):
-        cp(Q("NBL", 2 * k, 2), Q("NBI", 0, 2))
+        ts(Q("NBL", 2 * k, 2), Q("NBF", 0, 2), Q(pf(9), 0, 2), sub)
     for k in range(8):
-        (act if k < 6 else cp)(W("NB8", 320 * k, 320 * k + 320), I(CELLS, W("NBL", 20 * k, 20 * k + 20)))
+        (act if k < 5 else cp)(W("NB8", 320 * k, 320 * k + 320), I(W("IOTA", ZERO - 320, ZERO + 320), W("NBL", 20 * k, 20 * k + 20)))
         nodes[-1]["early"] = E5_
     ts(pf(5), c7, 320.0, mul, ch, add)
     ts("CIDX", W("IOTA", ZERO, ZERO + 320, 16), pf(5), add)
-    act(W("KT", 320, 640), CELLS)
-    iota("FM", [[0, 32], [1, 16]], 0, 0)
-    ts("MASK", "FM", cq, eq)
+    iota(W("KT", 320, 640), [[0, 320]], 0, 0)
+    iota(W("FM", 0, 256), [[0, 16], [1, 16]], 0, 0)
+    ts("MASK", W("FM", 0, 256), cq, eq)
     fill("KEEP", 1.0)
-    fill(W("KEEP", 0, 512, 16), 0.0)
+    fill(W("KEEP", 0, 256, 16), 0.0)
     iota(W("ST", 640, 960), [[0, 320]], 0, 0)
-    for k in ("DE", "DO", "D0E", "D0O", "D0L"):
+    for k in ("DE", "DO", "DL", "D0E", "D0O", "D0L"):
         fill(k, 0.0)
     for k in ("D0E", "D0O"):
         fill(W(k, 2, 96, 6), -1.0)
         fill(W(k, 5, 96, 6), 1.0)
     ts(W("R", 0, 32), "PI", 0.0, add)
+    fill("BK2", 0)
+    fill("ON4", 0.25)
     fill("ON", 0.5)
     for n in nodes[-2:]:
         n["early"] = E0_
@@ -317,17 +337,21 @@ def rank_program(g, core, T, topo):
         quant("eq%d" % b, "es%d" % b, "CT%d" % b)
         nodes[-1]["early"] = E1_
     mark = len(nodes)
-    act(pf(6), cq, 1.0 / 512, -ZERO / 512 - 1.0)
-    act(pf(6), ce, 0.5, pf(6))
-    act(Q("PLK", 0), Q(W("IOTA", ZERO, ZERO + 256, 16), 0), 1.0 / 512, Q(pf(6), 0))
-    for name, k in (("KEEP8", 12), ("KEEP3", 5), ("KP", 16)):
+    act(pf(6), cq, 1.0 / 512, -ZERO / 512 - 0.5)
+    act(pf(6), ce, -0.5, pf(6))
+    act(Q(W("N5", 0, 112, 7), 0), Q(W("IOTA", ZERO, ZERO + 256, 16), 0), 1.0 / 512, Q(pf(6), 0))
+    for name, k in (("KEEP8", 4), ("KEEP5", 7), ("K3", 8), ("KEEP4", 4), ("KP", 16)):
         iota(name, [[0, width(name)]], 1, 0)
         iota(W(name, 0, width(name), k), [[0, width(name) // k]], 0, 0)
+    iota(W("K3", 2, 128, 8), [[0, 16]], -1, 0)
     iota(W("KP", 1, 128, 17), [[0, 8]], 0, 0)
     iota("KEEPH", [[0, 512]], 1, 0)
     iota(W("KEEPH", 0, 512, 256), [[0, 2]], 0, 0)
     act("CE", W("IOTA", ZERO + 128, ZERO + 640, 16), bias=cq)
-    act("ENT", W("IOTA", ZERO, ZERO + 512), 1.0 / 2048)
+    ts(pc(7), pc(0), 5, shr)
+    ts(pf(15), pc(7), 128.0, mul)
+    act("ENT", W("IOTA", ZERO - 256, ZERO - 128), bias=pf(15))
+    iota("SRT", [[0, 512]], 0, 0)
     RHO = W("IOTA", ZERO + 1, ZERO + 9)
     act(pf(13), cq, 16.0)
     act(pf(31), cq, 16.0, 15.0)
@@ -346,156 +370,174 @@ def rank_program(g, core, T, topo):
         ts(W("LE", e, e + 1), pf(14), pf(9), add)
     iota(W("EQS", 256, 272), [[0, 16]], 0, 0)
     iota("LOWC", [[16, 20], [0, 2], [1, 16]], 0, 0)
-    lo, hi, lo2 = pf(28), pf(17), pf(18)
-    act(hi, lo, -1.0, 1.0)
-    act(lo2, lo, 2.0)
-    act(pf(19), hi, 16384.0)
-    act(pf(16), ce, 4096.0)
-    act(pf(10), pf(16), hi, 0.0)
-    act(pf(11), hi, 2048.0, pf(10))
-    act(pf(12), pf(10), -4.0, pf(19))
+    lo = pf(28)
+    two, rest = pf(19), pf(16)
+    ts(two, cq, 2.0, eq)
+    act(rest, two, -1.0, 1.0)
+    act(pf(10), two, ce, 0.0)
+    act(pf(11), ce, -1.0, 1.0)
 
     def split(k, out, src, scale, high, low):
         act(pf(k), lo, float(low - high), float(high))
-        act(out, src, scale, pf(k))
-    split(20, W("YC", 0, 128), W("IOTA", ZERO, ZERO + 128), lo, 0, 0)
-    split(21, W("YC", 128, 192), W("IOTA", ZERO, ZERO + 64), lo2, 0, 129)
-    for m in range(4):
-        n_ = min(128, 448 - 128 * m)
-        split(22 + m, W("YC", 192 + 128 * m, 192 + 128 * m + n_), W("IOTA", ZERO, ZERO + n_), lo2, 256 * (m + 1), 1)
-    split(26, W("LOWB", 0, 256), W("LOWC", 0, 256), lo, 3 * 2048 + 1024, 128)
-    split(27, W("LOWB", 256, 640), W("LOWC", 256, 640), lo, 3 * 2048 + 1280, -128)
-    for t in range(BONDV):
-        iota(W("YW%d" % t, 128, 1152, 2), [[0, 512]], 0, 0)
-    iota("KEEP2", [[0, 256], [1, 2]], 0, 0)
-    iota("REVF", [[256, 2], [1, 16]], 0, 0)
+        act(pf(k), pf(k), rest, 0.0)
+        for a in range(0, width(out), 128):
+            cut = lambda v: (v[0], v[1] + a, min(v[1] + a + 128, v[2])) + v[3:]
+            act(cut(out), cut(src), scale, pf(k))
+    for m in range(3):
+        n_ = min(256, 640 - 256 * m)
+        split(20 + m, W("YC", 256 * m, 256 * m + n_), W("IOTA", ZERO, ZERO + n_), lo, 256 * m, 0)
+    act(pf(12), lo, pf(11), 0.0)
+    for k, (a, b, high, low) in enumerate(((0, 256, 512, 128), (256, 640, 768, -128))):
+        act(pf(26 + k), lo, float(low - high), float(high))
+        act(pf(26 + k), pf(26 + k), rest, 0.0)
+        act(pf(26 + k), pf(26 + k), pf(11), pf(10))
+        for c in range(a, b, 128):
+            act(W("LAI", c, c + 128), W("LOWC", c, c + 128), pf(12), pf(26 + k))
+    act("LBI0", W("IOTA", ZERO, ZERO + 160), 0.0, two)
+    for b in range(4):
+        select("CU%d" % b, "ON4", [[1, 512]], -b, -4)
+        quant("fq%d" % b, "fs%d" % b, "CU%d" % b)
+    iota("REVF", [[-256, 2], [1, 16]], 256, 0)
     ts("REV", "REVF", pf(13), add)
     for n in nodes[mark:]:
         n["early"] = E2_
     quant("vq", "vs", "VT")
 
     MASK, KEEP = (lambda n: W("MASK", 0, n)), (lambda n: W("KEEP", 0, n))
-    slot = lambda name, k: W(name, k, 32, 2)
+    run = lambda name, k: W(name, k, 96, 6)
+    slot = lambda name, k: W(name, k + 1, 48, 3)
+    key = lambda k, name="N3": W(name, k, 128, 8)
+    links = lambda k, name="N5": W(name, k, 112, 7)
     ends = lambda name, n=256: W(name, 15, n, 16)
-    E, O, S30, DC = W("R", 0, 16), W("R", 16, 32), W("SD", 0, 32, 2), W("SD", 1, 32, 2)
+    SE, SO = W("SI", 0, 512, 32), W("SI", 16, 512, 32)
+    E, O, S30, DC = W("R", 0, 16), W("R", 16, 32), W("SD", 16, 32), W("SD", 0, 16)
 
     def lookup(g_, s_, win, off):
         tt(g_, I(win, off), MASK(16 * width(off)), mul)
         scan(s_, KEEP(16 * width(off)), g_)
 
-    def shift(out, a, up, eng):
+    def shift(out, a, up):
         for q in range(3):
-            eng(Q(out, q + 1 if up else q), Q(a, q if up else q + 1))
-
-    run = lambda name, k: W(name, k, 96, 6)
+            act(Q(out, q + 1 if up else q), Q(a, q if up else q + 1))
 
     def eight(v, k):
         n, a, _b, st = N(v)[:4]
         return (n, a + 8 * k * st, a + (8 * k + 7) * st + 1, st, 0, 128, 1)
 
-    def end_list(first, last):
-        for k in range(2):
-            if first:
-                cp(Q("BKU", k), Q(eight(first, k), 0))
-            if last:
-                cp(Q("BKU", 2 + k), Q(eight(last, k), 3))
-
-    def end_lookup(table, j, to_first, to_last):
-        lookup("GK%d" % j, "SK%d" % j, table, "BKU")
-        for k in range(2):
-            if to_first:
-                cp(Q(eight(to_first, k), 0), Q(ends("SK%d" % j, 128), k))
-            if to_last:
-                act(Q(eight(to_last, k), 3), Q(ends("SK%d" % j, 128), 2 + k))
-
-    def where_equal(y, s3):
-        ts(Q("NZ", 0), Q(s3, 0), 0.0, ne, 320.0, mul)
-        tt(Q("BL", 0), Q("NZ", 0), Q(y, 0), add)
-
     def halfstep(h):
         even = h % 2 == 0
         kk, out, d0, d1 = "KK%d" % h, "OUT%d" % h, ("D0E", "D0O", "D0E", "D0L")[h], ("DE", "DO", "DE", "DL")[h]
-        S = W("SI", 15, 256, 16) if even else W("SI", 271, 512, 16)
+        S = SE if even else SO
         if h == 0:
             y, n, s3, o, dc = E, O, S30, "NS", DC
         else:
             before = "OUT%d" % (h - 1)
             y, n, s3, o, dc = run(("DE", "DO", "DE")[h - 1], 2), run(before, 1), run(before, 2), run(before, 4), run(before, 5)
             tt(kk, o, s3, sub)
+            if h == 1:
+                act(Q(eight("KY", 1), 1), Q(eight(kk, 1), 0))
+                act(Q(eight("KY", 0), 1), Q(eight(s3, 1), 0))
+                for k in range(2):
+                    tt(Q(eight(kk, k), 0), Q(ends("SK0", 128), k), Q(eight("KY" if k else kk, k), k), add)
+                    act(Q(eight("BC", k), 0), Q(ends("SK0", 128), k))
+                for k in range(2):
+                    tt(Q(eight(s3, k), 0), Q(eight("KY" if k else s3, 0), k), Q(ends("SK0", 128), k), sub)
+                tt(Q(n, 0), Q(n, 0), Q("BC", 0), add)
+                ts(Q(links(1), 0), Q("BC", 0), 0.0, ne, -1.0, mul)
             cp("KU", kk)
-        parts = 2 if h in (0, 3) else 1
+        parts = 2 if h == 0 else 1
         for k in range(parts):
             w = 16 // parts
             lookup(W("GS", 16 * w * k, 16 * w * (k + 1)), W("SS", 16 * w * k, 16 * w * (k + 1)), W("ST", 0, 640) if even else W("ST", 320, 960), W("KU", w * k, w * (k + 1)))
         sl = run if h < 3 else slot
         tt("PR", dc, s3, mul)
-        act("NV", "PR", 1e24, func=ACT.Abs)
+        act(Q("NV", 0, 4 if h < 3 else 3), Q("PR", 0, 4 if h < 3 else 3), 1e24, func=ACT.Abs)
+        if h == 3:
+            ts(Q("NV", 3), Q(s3, 3), 0.0, eq, -BIG, mul)
+            act(Q(sl(d0, 0), 3), Q("NV", 3), -1.0 / BIG)
         tt("SYV", S, "NV", add)
         tt(sl(d1, 0), kk, y, sub)
-        for q, k in ((1, 1), (2, 2)) if even else ((0, 3),):
+        for q, k in (((0, 4),), ((0, 3),), ((1, 1), (2, 2)), ((0, 4),))[h]:
             act(Q(sl(d1, 1), q, k), Q(y, q, k))
         end = 3 if even else 0
+        now = 3 - end
         if h < 3:
             act(sl(d1, 2), n)
             act(run(d1, 5), n, -1.0)
-            shift(run(d1, 3), run(d1, 0), not even, act)
-            shift(run(d1, 4), y, not even, act)
+            shift(run(d1, 3), run(d1, 0), not even)
+            shift(run(d1, 4), y, not even)
             act(Q(run(d1, 4), end), Q(n, end))
-        if h > 0:
-            now = 3 - end
-            tt(Q("BA", now), Q("B0", now), Q(y, now), sub)
-            ts(Q("Z1", now), Q(s3, now), 0.0, eq)
-            tt(Q("BC", now), Q("BA", now), Q("Z1", now), mul)
-            tt(Q(sl(d1, 1), now), Q("BC", now), Q(y, now), add)
-        else:
-            now = 0
-            tt(Q("BC", 0), Q(sl(d1, 1), 0), Q(y, 0), sub)
-        ts(Q(W("NN", 4 + h, 192, 12) if h < 2 else W("N3", h - 1, 80, 5), 0), Q("BC", now), 0.0, ne, -1.0, mul)
         if h in (1, 2):
+            ts(Q("Z1", now), Q(s3, now), 0.0, eq)
+            tt(Q("BC", now), Q("B0", now), Q("Z1", now), mul)
+            tt(Q(sl(d1, 1), now), Q("BC", now), Q(y, now), add)
+            ts(Q(links(2) if h < 2 else key(6), 0), Q("BC", now), 0.0, ne, -1.0, mul)
             for q in range(4):
-                cp(Q("BKU", q), Q(eight(n, q % 2), end))
-            lookup("GK1", "SK1", "W%d" % end, "BKU")
+                far = 0.0 if q // 2 == end // 2 else 640.0
+                act(Q(W("A7", 0, 8), q), Q(eight(n, q % 2), end), bias=far)
+            cp("BKU", W("A7", 0, 8))
+            lookup("GK1", "SK1", "KT", "BKU")
             for q in range(4):
-                to = (W("SI", 15, 256, 16) if end == 0 else W("SI", 271, 512, 16)) if q // 2 == end // 2 else "B0"
+                to = (SE if end == 0 else SO) if q // 2 != end // 2 else "B0" if h == 1 else slot("DL", -1)
                 act(Q(eight(to, q % 2), end), Q(ends("SK1", 128), q))
         if h == 3:
             act(W("R", 48, 64), n)
             act(Q(W("R", 64, 80), 0, 3), Q(o, 0, 3))
             act(Q(W("R", 64, 80), 3), Q(n, 3))
-            act(W("OUT3", 1, 32, 2), n)
-            scan(Q("KS", 0), Q("KEEP8", 0), Q("NN", 0))
-            tt(Q(W("N3", 0, 80, 5), 0), Q(W("KS", 11, 192, 12), 0), Q("PLK", 0), add)
+            act(W("OUT3", 2, 48, 3), n)
+        if h == 2:
+            scan(Q("K5", 0), Q("KEEP5", 0), Q("N5", 0))
+            act(Q(key(5), 0), Q(links(6, "K5"), 0))
+            ts(Q("NE", 0), Q(s3, 3), 0.0, eq, -1.0, mul)
+            act(Q(key(1, "K3"), 0), Q("NE", 0), 2.0, 1.0)
             for k in range(2):
-                cp(Q("BKU", 2 + k), Q(eight(n, k), 3))
-            lookup("GK0", "SK0", "W3", "BKU")
+                ts(Q("BK2", k), Q(eight(kk, k), 3), 319.0, mn_)
+            lookup("GK0", "SK0", W("KT", 640, 960), "BK2")
             for k in range(2):
-                tt(Q(W("N3", 40 * k + 4, 40 * k + 40, 5), 0), Q(ends("SK0", 128), 2 + k), Q(ends("SK1", 128), 2 + k), gt)
+                ts(Q(eight(key(0), k), 0), Q(ends("SK1", 128), 2 + k), 0.0, ne)
+                tt(Q(eight(key(2), k), 0), Q(ends("SK0", 128), k), Q(ends("SK1", 128), k), gt)
+                tt(Q(key(1 + 2 * k), 0), Q("S6", 3), Q(SO, 3), gt)
+            tt(Q(key(4), 0), Q(key(0), 0), Q("NE", 0), mul)
+            tt(Q(key(3, "K3"), 0), Q(ends("SS"), 3), Q("SYV", 3), gt)
+            tt(Q(key(7), 0), Q(ends("SS"), 0), Q("SYV", 0), gt)
+        if h == 1:
+            act(Q("S6", 3), Q(ends("SS"), 3))
         tt(sl(d0, 1), ends("SS"), "SYV", gt)
         if h < 3:
             for q in range(3):
                 a, b = (q + 1, q) if even else (q, q + 1)
                 tt(Q(run(d0, 4), b), Q(ends("SS"), a), Q("SYV", a), gt)
-            act(Q(W("NN", 10 + h, 192, 12) if h < 2 else W("N3", 3, 80, 5), 0), Q(run(d0, 1), now))
         if h < 2:
+            act(Q(links(3 + h), 0), Q(run(d0, 1), now))
             tt("SG1", ends("SS"), "NV", sub)
             tt(S, S, "SG1", mx_)
-        for o_ in [out] if h < 3 else [W(out, 32, 64), W(out, 64, 96)]:
-            scan(o_, d0, d1)
+        scan(out if h < 3 else W(out, 48, 96), d0, d1)
+        if h == 3:
+            act(W(out, 98, 144, 3), W(out, 50, 96, 3))
 
     for rd in range(ROUNDS):
-        mq, ms, fw, msg = "mq%d" % rd, "ms%d" % rd, "FW%d" % rd, "MSG%d" % rd
-        cp("OFFI", W("R", 0, 32))
-        tt(S30, E, O, sub)
-        kk0 = "KK0"
-        shift("NS", O, True, act)
+        mq, ms, fw, al, pa = "mq%d" % rd, "ms%d" % rd, W("FW", 384, 1024), "ao%d" % rd, "po%d" % rd
+        if rd == 0:
+            for e in range(2):
+                cp(W("OFFI", e, 32, 2), W("PL", 16 - 16 * e, 32 - 16 * e))
         act(Q("NS", 0), Q(E, 0))
-        tt(kk0, "NS", S30, sub)
-        tt(DC, "NS", E, sub)
+        nodes[-1]["first"] = True
+        shift("NS", O, True)
+        tt("SD", W("NS", 0, 32), W("R", 0, 32), sub)
+        tt("KK0", "NS", S30, sub)
+        ts("SE0", "SD", 0.0, eq)
         for q in range(4):
-            ts(Q(W("NN", q, 192, 6), 0), Q("SD", q), 0.0, eq)
-        cp("KU", kk0)
-        where_equal(E, S30)
-        end_list("BL", O)
+            act(Q(W("NN", q, 128, 4), 0), Q("SE0", q))
+        scan(Q("KS", 0), Q("KEEP8", 0), Q("NN", 0))
+        for j in range(2):
+            act(Q(links(5 + j), 0), Q(W("KS", 64 * j + 3, 64 * j + 64, 4), 0))
+        cp("KU", "KK0")
+        ts(Q("NZ", 0), Q(S30, 0), 0.0, ne, 320.0, mul)
+        tt(Q("BL", 0), Q("NZ", 0), Q(E, 0), add)
+        for k in range(2):
+            act(Q(W("A7", 8, 16), k), Q(eight("BL", k), 0))
+            act(Q(W("A7", 8, 16), 2 + k), Q(eight(O, k), 3))
+        cp("BKU", W("A7", 8, 16))
         for k in range(2):
             mm(3 * k, W("ur", 0, 128), W("urs", 0, 128), W(mq, 160 * k, 160 * k + 160), W(ms, 160 * k, 160 * k + 160))
             (cp if k else act)(W("W07", 160 * k, 160 * k + 160), W("ps%d" % (3 * k), 0, 160))
@@ -504,8 +546,7 @@ def rank_program(g, core, T, topo):
         act(W("ST", 0, 320), W("ps1", 0, 320))
         act(W("ST", 320, 640), W("ps2", 0, 320))
         mm(0, W("ur", 384, 512), W("urs", 384, 512), mq, ms)
-        act(Q("W0", 0, 2), Q(W("ps0", 0, 320), 0, 2))
-        act(Q("W3", 2, 2), Q(W("ps0", 0, 320), 2, 2))
+        act(W("KT", 640, 960), W("ps0", 0, 320))
         cp("GO", I("W07", "LS"))
         cp(W("GB", 0, 160), I("W07", W("LB", 0, 10)))
         act(W("GB", 160, 320), I("W07", W("LB", 10, 20)))
@@ -518,80 +559,87 @@ def rank_program(g, core, T, topo):
         for k in range(4):
             mm(3, *(("bq", "bs") if k < 3 else ("bq3", "bs3")), W("dq", 20 * k, 20 * k + 128), W("dsc", 20 * k, 20 * k + 128), k == 0, k == 3)
         tt("BI", W("ps3", 0, 20), "CIDX", add)
-        cp("BIU", "BI")
+        ts("BIU", "BI", 2560.0, mn_)
         cp(W("KT", 0, 160), I("NB8", W("BIU", 0, 10)))
         act(W("KT", 160, 320), I("NB8", W("BIU", 10, 20)))
-        end_lookup("KT", 0, run("DE", 1), "B0")
-        act(Q("W0", 2, 2), Q(W("KT", 0, 320), 0, 2))
-        act(Q("W3", 0, 2), Q(W("KT", 0, 320), 2, 2))
-        for k in range(4):
-            lookup(W("GI", 128 * k, 128 * k + 128), W("SI", 128 * k, 128 * k + 128), W("ST", 320 * (k // 2), 320 * (k // 2) + 320), W("OFFI", 8 * k, 8 * k + 8))
+        lookup("GK0", "SK0", W("KT", 0, 640), "BKU")
+        for k in range(2):
+            act(Q(eight("B0", k), 3), Q(ends("SK0", 128), 2 + k))
+        mm(5, W("ur", 512, 640), W("urs", 512, 640), mq, ms)
+        act("SN", W("ps5", 0, 320))
+        for k in range(2):
+            act(W("GI", 256 * k, 256 * k + 256), I("SN", W("OFFI", 16 * k, 16 * k + 16)))
+            tr(W("SI", 256 * k, 256 * k + 256), W("GI", 256 * k, 256 * k + 256))
         for t in range(4):
             f = W("ps%d" % (4 + t), 0, 320)
             mm(4 + t, "eq%d" % t, "es%d" % t, mq, ms)
-            act("FQ%d" % t, f, 0.5)
-            act(W("YW%d" % t, 1152, 1472), f)
+            act(W("YW%d" % t, 640, 960), f)
             if t < 2:
                 act("FH%d" % t, f)
-        act(W("LA", 0, 640), "LOWB", ce, pf(12))
-        act(W("LBW", 0, 640), "LOWB", 0.0, pf(19))
+        dmas("y", "dla%d" % rd, [(W("LA", 0, 640), "LAI")])
+        dmas("y", "dlb%d" % rd, [(W("LBW", a, a + 160), "LBI0") for a in range(0, 640, 160)])
         for h in range(4):
             halfstep(h)
-        for k, src in enumerate((W("OUT3", 1, 64, 2), W("OUT3", 33, 96, 2), W("R", 48, 80))):
+        for k, src in enumerate((W("OUT3", 2, 96, 3), W("OUT3", 50, 144, 3), W("R", 48, 80))):
             tr(W("TA", 32 * k, 32 * k + 32), src)
-            cp(W("AL", 32 * k, 32 * k + 32), W("TA", 32 * k, 32 * k + 32))
+            cp(W("AL", 32 * k, 32 * k + 32) if k else al, W("TA", 32 * k, 32 * k + 32))
             nodes[-1]["early"] = (E4_, 0.0, E3_)[k]
-        al = W("AL", 0, 32)
+        send("ra%d" % rd, [("al%d" % rd, al, False)])
         for k in range(2):
-            scan(Q(W("KD", 80 * k, 80 * k + 80), 0), Q("KEEP3", 0), Q("N3", 0))
-        tr(Q("KR", 0), Q(W("KD", 4, 160, 5), 0))
+            scan(Q(W("KD", 128 * k, 128 * k + 128), 0), Q("K3", 0), Q("N3", 0))
+        tr(Q("KR", 0), Q(W("KD", 7, 256, 8), 0))
         for q in range(4):
             ts(Q("KL", q), Q("KR", 0), 512.0, mul, float(ZERO), add)
-            act(Q("NK", q), Q(W("KD", 20 * q + 4, 20 * q + 20, 5), 0), 512.0)
+            act(Q("NK", q), Q(W("KD", 32 * q + 7, 32 * q + 32, 8), 0), 512.0)
         cp(W("RK", 0, 256), I("IOTA", W("KL", 0, 16)))
         act(W("RK", 256, 512), I("IOTA", W("KL", 16, 32)))
         for b in range(3):
             act(("SG0", "SG1B", "SG2")[b], "RK", -1.0, W("NK", b, b + 1), ACT.Sign, W("PS", b, b + 1))
-        ts(W("CMP", 0, 512), "RK", W("NK", 3, 4), lt, 2.0, mul)
+        ts("CMP", "RK", W("NK", 3, 4), lt, 2.0, mul)
         scan("CNT", "KEEPH", "CMP")
         ts(W("PS", 3, 4), W("CNT", 255, 256), W("CNT", 511, 512), add, -511.0, add)
         for q in range(4):
-            ts(Q(W("PP", 4 * q, 4 * q + 4), 0), Q("PS", q), 511.0, add, 0.5, mul)
-            act(Q(W("PP", 16 + 4 * q, 20 + 4 * q), 0), Q("PS", q), 0.5, 255.5)
+            ts(Q(W("PP", 4 * q, 4 * q + 4), 0), Q(W("PS", 0, 4), q), -0.5, mul, 255.5, add)
+            act(Q(W("PP", 16 + 4 * q, 20 + 4 * q), 0), Q(W("PS", 0, 4), q), -0.5, 255.5)
         tr(Q("PT", 0), Q("PP", 0))
         for q in range(4):
-            cp(Q("PA", q), Q("PT", 0))
-        for k in range(0, 32, PIECE):
-            tt(W("DP", 16 * k, 16 * (k + PIECE)), I(CELLM, W("AL", k, k + PIECE)), W("ENT", 16 * k, 16 * (k + PIECE)), add)
-        cp(I("SRT", "PA"), "DP")
-        ts(msg, W("SRT", 0, 128), ROUND, add, ROUND, sub)
-        send("rl%d" % rd, [(W(fw, 0, 128), msg, False)])
-        act(W(fw, 128, 640), I(CELLM, al))
+            cp(Q(pa, q), Q("PT", 0))
+        send("rl%d" % rd, [("pa%d" % rd, pa, False)])
+        nodes[-1]["early"] = E6_
+        for q in range(4):
+            cp(Q("PQ", q), Q(W("PT", 8 * q, 8 * q + 8), 0))
+        act(W("SRT", 384, 512), "ENT", 0.0)
+        cp(I("SRT", "PQ"), "ENT")
+        cp(W("FWP", 0, 256), I(CELLM, W("al%d" % rd, 0, 16)))
+        act(W("FWP", 256, 512), I(CELLM, W("al%d" % rd, 16, 32)))
+        cp(I(W("FW", 0, 512), "pa%d" % rd), "FWP")
+        act(W("FW", 512, 1024), I(CELLM, al))
+        zq, zs = "zq%d" % rd, "zs%d" % rd
+        for k in range(0, 32, VP):
+            pick_codes(W(zq, 16 * k, 16 * (k + VP)), W(zs, 16 * k, 16 * (k + VP)), mq, ms, W("AL", 32 + k, 32 + k + VP))
         for t in range(4):
-            for k in range(2):
-                if t < BONDV:
-                    zg = W("ZG%d" % t, 256 * k, 256 * k + 256)
-                    act(zg, I("FQ%d" % t, W("AL", 64 + 16 * k, 80 + 16 * k)))
-                    tt(W("YW%d" % t, 129 + 512 * k, 640 + 512 * k, 2), I("FQ%d" % t, W("AL", 32 + 16 * k, 48 + 16 * k)), zg, add)
-                    continue
-                for j in range(2):
-                    act(W("ZG%d" % t, 512 * k + j, 512 * k + 512, 2), I("FQ%d" % t, W("AL", 64 - 32 * j + 16 * k, 80 - 32 * j + 16 * k)))
-                scan(W("YW%d" % t, 128 + 512 * k, 640 + 512 * k), "KEEP2", W("ZG%d" % t, 512 * k, 512 * k + 512))
-        tt("G8", W("SRT", 0, 128), MASK(128), mul)
+            for k in range(0, 32, SP):
+                act(W("ZG%d" % t, 16 * k, 16 * (k + SP)), I(W("YW%d" % t, 640, 960), W("AL", 64 + k, 64 + k + SP)), 0.5)
+            mm(t, "fq%d" % t, "fs%d" % t, zq, zs)
+            for k in range(0, 32, VS):
+                tt(W("YW%d" % t, 128 + 16 * k, 128 + 16 * (k + VS)), W("ps%d" % t, 16 * k, 16 * (k + VS)), W("ZG%d" % t, 16 * k, 16 * (k + VS)), add)
+        tt("G8", W("SRT", 384, 512), MASK(128), mul)
         scan("S8", KEEP(128), "G8")
-        ts("E1", ends("S8", 128), ROUND, add, ROUND, sub)
-        tt("E2", ends("S8", 128), "E1", sub)
-        ts("EL2", "E2", 4096.0, mul, 1.0, add)
+        for q in range(4):
+            act(Q(W("E4", q, 32, 4), 0), Q(ends("S8", 128), q))
+        scan(Q("ES", 0), Q("KEEP4", 0), Q("E4", 0))
+        for q in range(4):
+            ts(Q("EL2", q), Q(W("ES", 3, 32, 4), 0), 256.0, add)
         for t in range(4):
-            act(W("HT", t, 512, 4), I(W("YW%d" % t, 128, 1152), "EL2"), 2.0)
+            act(W("HT", t, 512, 4), I(W("YW%d" % t, 128, 640), "EL2"), 2.0)
         aq, asc, lq, ls = "aq%d" % rd, "as%d" % rd, "lq%d" % rd, "ls%d" % rd
         quant(aq, asc, "HT")
         send("rq%d" % rd, [(lq, aq, True), (ls, asc, False)])
         for b in range(4):
             mm(b, W("wq", 128 * b, 128 * b + 128), W("wsc", 128 * b, 128 * b + 128), lq, ls)
             act(W("YW%d" % b, 0, 128), W("ps%d" % b, 0, 128), 2.0 ** -6)
-        cp("PF", "PA")
-        ts("T1", "PA", 128.0, ge, 1024.0, mul)
+        ts("PF", pa, 384.0, sub)
+        ts("T1", pa, 384.0, lt, 1024.0, mul)
         tt("TM", "T1", "PF", mx_)
         tt("SELF", "TM", "CE", mn_)
         cp("SEL", "SELF")
@@ -599,18 +647,22 @@ def rank_program(g, core, T, topo):
         for par in range(2):
             cp(W("VL", par, 32, 2), W("VT_", 16 * par, 16 * par + 16))
         for w in range(2):
-            act(W("SELX", 256 * w, 256 * w + 256), I("YC", W("VL", 16 * w, 16 * w + 16)), bias=pf(10 + w))
+            act(W("SELX", 256 * w, 256 * w + 256), I("YC", W("VL", 16 * w, 16 * w + 16)))
         for e in range(2):
             half = lambda name, n: W(name, n * e, n * e + n)
-            lookup(half("FM", 256), half("SCN", 256), fw, half("SEL", 16))
-            cp(half("PA_", 128), I(half("SCN", 256), "LI"))
+            if e == 0:
+                lookup(half("FM", 256), half("SCN", 256), fw, half("SEL", 16))
+            else:
+                act(W("FWP", 0, 256), I(fw, half("SEL", 16)))
+                tt(half("FM", 256), W("FWP", 0, 256), MASK(256), mul)
+                scan(half("SCN", 256), KEEP(256), half("FM", 256))
             act(half("PB_", 128), I(half("SCN", 256), "LJ"))
-            tt(half("EQ", 128), half("PA_", 128), half("PB_", 128), eq)
+            tt(half("EQ", 128), I(half("SCN", 256), "LI"), half("PB_", 128), eq)
             scan(half("EQS", 128), "KP", half("EQ", 128))
-        ts("FCI", ends("SCN", 512), float(MID), add)
-        ts("FA", "FCI", 496, bw)
-        tt("LZD", "FA", "FCI", add)
-        act("PP_", "LZD", 1.0 / 640)
+        ts("FCI", ends("SCN", 512), 1.0 / 16, mul, (MID - 7.5) / 16, add)
+        act("LZD", ends("SCN", 512), 1.0 / 640, MID / 640)
+        ts("T1", "FCI", 16.0 / 640, mul)
+        tt("PP_", "T1", "LZD", add)
         tt("OF", I("EQS", "LE"), "PP_", add)
         tr("OT", "OF")
         for par in range(2):
@@ -619,6 +671,13 @@ def rank_program(g, core, T, topo):
             act("FCF", ends("SCN", 512), bias=float(MID))
             tr(W("R", 0, 32), "FCF")
             nodes[-1]["rd"].append(N("OFF"))
+            for e in range(2):
+                for par in range(2):
+                    act(W("AB", 32 * e + 16 * par, 32 * e + 16 * par + 16), W("FCF", 16 * e, 16 * e + 16), ce if par else pf(11), 0.0)
+            tr("AT", "AB")
+            for e in range(2):
+                tt(W("UF", e, 32, 2), W("AT", 32 * e, 32 * e + 16), W("AT", 32 * e + 16, 32 * e + 32), add)
+            cp("OFFI", "UF")
         else:
             act("RK", I(fw, "SEL"), bias=float(MID))
             act("DP", I("RK", "REV"))
@@ -627,15 +686,15 @@ def rank_program(g, core, T, topo):
             for w in (1, 0):
                 k = 8 * w + y
                 cp(I("LA" if w else "LBW", W("OFF", 2 * k, 2 * k + 2)), W("SELX", 32 * k, 32 * k + 32))
+        for j, win in enumerate(("LA", "LBW")):
+            tr(W("TL", 640 * j, 640 * j + 640), W(win, 0, 640))
+            row = lambda r: W("TL", 640 * j + r, 640 * j + 640, 16)
+            tt(W("VA", j, 80, 2), row(0), row(1), add)
+            act(W("XD", j, 80, 2), row(2))
+        scan("XS", "XD", "VA")
+        cp("EL", W("XS", 3, 80, 4))
         for k in range(2):
             half = lambda name, n: W(name, n * k, n * k + n)
-            for j, win in enumerate(("LA", "LBW")):
-                tr(W("TL", 640 * k + 320 * j, 640 * k + 320 * j + 320), half(win, 320))
-            tt(half("VA", 40), W("TL", 640 * k, 640 * k + 640, 16), W("TL", 640 * k + 1, 640 * k + 640, 16), add)
-            tt(half("M1", 20), W("VA", 40 * k, 40 * k + 20), W("VA", 40 * k + 20, 40 * k + 40), mn_)
-            tt(half("M2", 10), W("M1", 20 * k, 20 * k + 20, 2), W("M1", 20 * k + 1, 20 * k + 20, 2), mn_)
-            ts(half("M3", 10), half("M2", 10), 2047, bw)
-            cp(half("EL", 10), half("M3", 10))
             for t in range(2):
                 tt(W("MT", 640 * k + t, 640 * k + 640, 4), I("YW%d" % t, half("EL", 10)), half("FH%d" % t, 160), add)
                 act(half("G%d" % (2 + t), 160), I("YW%d" % (2 + t), half("EL", 10)))
@@ -665,67 +724,87 @@ def rank_program(g, core, T, topo):
         n["pre"].discard(i)
         for j in n["pre"]:
             nodes[j]["post"].append(i)
-    for n in reversed(nodes):
-        n["way"] = n["busy"] + n["after"] + n.get("early", 0.0) + max([WAKE + nodes[j]["way"] for j in n["post"]] or [0.0])
 
-    def beside(i, j):
-        return sum(nodes[k]["busy"] for k in nodes[j]["src"] if k > i and nodes[k]["q"] == nodes[i]["q"])
-
-    def lag(i, j):
-        return 0.0 if nodes[j].get("chain") and nodes[i]["q"] == "t" else WAKE
-
-    def lay(rank_of, back):
-        before, behind = ("post", "pre") if back else ("pre", "post")
-        left = [len(n[before]) for n in nodes]
-        ready = [i for i, k in enumerate(left) if k == 0]
-        taken, start, done = {q: [] for q in queue}, {}, {}
+    def lay(way):
+        left = [len(p) for p in pre]
+        ready = sorted((way[i], -i) for i, k in enumerate(left) if k == 0)
+        taken, start, done = {q: [] for q in queue}, [0.0] * len(nodes), [0.0] * len(nodes)
         while ready:
-            i = min(ready, key=lambda i: (rank_of[i], i))
-            ready.remove(i)
-            n = nodes[i]
-            at = max([done[k] + (lag(i, k) if back else lag(k, i)) for k in n[before]] or [0.0]) + (n["after"] if back else 0.0)
-            busy, line, k = n["busy"] + (WAKE if n.get("drain") else 0.0), taken[n["q"]], len(taken[n["q"]])
+            i = -ready.pop()[1]
+            at = 0.0
+            for k, w in pre[i]:
+                if done[k] + w * WAKE > at:
+                    at = done[k] + w * WAKE
+            line = taken[on[i]]
+            k = len(line)
             while k > 0 and line[k - 1][1] > at:
                 k -= 1
-            while k < len(line) and line[k][0] < at + busy - SLIP:
-                at = max(at, line[k][1])
+            while k < len(line) and line[k][0] < at + busy[i] - SLIP:
+                if line[k][1] > at:
+                    at = line[k][1]
                 k += 1
-            line.insert(k, (at, at + busy))
-            start[i], done[i] = at, at + n["busy"] + (0.0 if back else n["after"])
-            for j in n[behind]:
+            line.insert(k, (at, at + busy[i]))
+            start[i], done[i] = at, at + busy[i] + after[i]
+            for j in nodes[i]["post"]:
                 left[j] -= 1
                 if left[j] == 0:
-                    ready.append(j)
-        return start, done
+                    ready.append((way[j], -j))
+                    ready.sort()
+        return sorted(range(len(nodes)), key=lambda i: (start[i], i))
+
+    def span(order, wake, busy, after):
+        last, done = {q: 0.0 for q in queue}, [0.0] * len(order)
+        for i in order:
+            at = last[on[i]]
+            for k, w in pre[i]:
+                if done[k] + w * wake > at:
+                    at = done[k] + w * wake
+            at += busy[i]
+            last[on[i]] = at
+            done[i] = at + after[i]
+        return max(done)
 
     if not ORDER:
-        best = None
+        lag = lambda i, j: 0.0 if nodes[j].get("chain") and nodes[i]["q"] == "t" else 1.0
+        beside = lambda i, j: sum(nodes[k]["busy"] for k in nodes[j]["src"] if k > i and nodes[k]["q"] == nodes[i]["q"])
+        busy, after, on = [n["busy"] for n in nodes], [n["after"] for n in nodes], [n["q"] for n in nodes]
+        cases = [(wake, [(n["busy"] + ga * n["gathers"] + sc * n["scatters"]) * slow if n["kind"] == "op" else n["busy"] + issue * (n["kind"] == "send") for n in nodes],
+                  [n["after"] + far * (n["kind"] == "send") for n in nodes]) for wake, slow, ga, sc, far, issue in CASES]
+        pre = [[(k, lag(k, i)) for k in sorted(n["pre"])] for i, n in enumerate(nodes)]
+        way = [0.0] * len(nodes)
+        for i in reversed(range(len(nodes))):
+            way[i] = busy[i] + after[i] + nodes[i].get("early", 0.0) + max([lag(i, j) * WAKE + beside(i, j) + way[j] for j in nodes[i]["post"]] or [0.0])
+        alike, met = {}, {}
+        for i, n in enumerate(nodes):
+            if n.get("first"):
+                met = {}
+            v = (n["wr"] + n["rd"])[0]
+            k = (n["q"], v[0][:2] if v[0][:2] in PER_ROUND else v[0]) + v[1:] + (n["rd"][0][1:] if n["rd"] else ())
+            met[k] = met.get(k, 0) + 1
+            alike.setdefault(k + (met[k],), []).append(i)
+        alike = list(alike.values())
+        seed = [SEED]
+
+        def pick(n):
+            seed[0] = (seed[0] * 1103515245 + 12345) % 2147483648
+            return (seed[0] >> 8) % n
+        best, now = None, 1e9
         for _pass in range(PASSES):
-            for i in reversed(range(len(nodes))):
-                n = nodes[i]
-                n["way"] = n["busy"] + n["after"] + n.get("early", 0.0) + max([WAKE + nodes[j]["way"] + SIB * beside(i, j) for j in n["post"]] or [0.0])
-            start, _done = lay([-n["way"] for n in nodes], False)
-            order = sorted(range(len(nodes)), key=lambda i: (start[i], i))
-            last, ready, done, cause = {}, {}, {}, {}
-            for i in order:
-                n = nodes[i]
-                ready[i], cause[i] = max([(done[k] + lag(k, i), k) for k in n["pre"]] or [(0.0, None)])
-                start[i] = ready[i]
-                if n["q"] in last and last[n["q"]][0] > ready[i]:
-                    start[i], cause[i] = last[n["q"]]
-                last[n["q"]] = (start[i] + n["busy"], i)
-                done[i] = start[i] + n["busy"] + n["after"]
-            i = max(done, key=done.get)
-            if best is None or done[i] < best[0]:
-                best = (done[i], order)
-            while i is not None:
-                nodes[i]["early"] = nodes[i].get("early", 0.0) + PUSH * min(start[i] - ready[i], 1000.0)
-                i = cause[i]
+            trial = list(way)
+            for _k in range(1 + pick(3) // 2 if best else 0):
+                by = (100.0, 400.0, 1500.0)[pick(3)] * (0.3 + pick(100) / 100.0) * (2 * pick(2) - 1)
+                for i in alike[pick(len(alike))]:
+                    trial[i] += by
+            order = lay(trial)
+            worth = sum(span(order, *case) / sum(case[1]) for case in cases)
+            if best is None or worth <= best[0]:
+                best = (worth, order)
+            if worth <= now * (1.0 + SLACK * (1.0 - _pass / PASSES) * pick(100) / 100.0):
+                now, way = worth, trial
         ORDER.extend(best[1])
     order = ORDER
 
     count, know, totals, sent = {k: 0 for k in own}, {k: {} for k in queue}, {}, 0
-    drain = False
     for i in order:
         n = nodes[i]
         q = n["q"]
@@ -743,11 +822,6 @@ def rank_program(g, core, T, topo):
                     know[q][s] = max(know[q].get(s, 0), x)
                 know[q][m["sig"]] = m["val"]
         if n["kind"] == "op":
-            if (q == "g" or (q == "v" and drain)) and know[q].get(own[q], 0) < count[q]:
-                queue[q].wait_ge(T.sem[own[q]], count[q])
-                know[q][own[q]] = count[q]
-            if q == "v":
-                drain = n.get("drain")
             count[q] += 1
             n["call"]().then_inc(T.sem[own[q]], 1)
             n["sig"], n["val"], n["snap"] = own[q], count[q], dict(know[q])

from concourse.mybir import dt, AluOpType, ActivationFunctionType

ROUNDS = 3
FAR = 1e29
BIG = 2.0 ** 96
MID = 160
F32, BF, I32, U16, MXC, U8 = "float32", "bfloat16", "int32", "uint16", "float8_e4m3fn_x4", "uint8"
SCRATCH, PART = {}, {}


def _sb(dtype, **kw):
    for k, n in kw.items():
        SCRATCH[k] = ("sbuf", [128, n], dtype)
        PART[k] = (k, 0, n)


def _pack(buf, dtype, **kw):
    at = 0
    for k, n in kw.items():
        PART[k] = (buf, at, n)
        at += (n + 15) // 16 * 16
    SCRATCH[buf] = ("sbuf", [128, at], dtype)


_sb(BF, XT=1280, MT=1280, UT=512, VT=512, BY=128, DT=512, HT=512, CB=512)
_pack("ONB", BF, ON=512, ON4=512)
_pack("CTB", BF, CT0=512, CT1=512, CT2=512, CT3=512)
_pack("YW", BF, YW0=960, YW1=960, YW2=960, YW3=960)
_pack("FH", BF, FH0=320, FH1=320)
_pack("ZG", BF, ZG0=512, ZG1=512, ZG2=512, ZG3=512)
_pack("CTC", BF, CU0=512, CU1=512, CU2=512, CU3=512)
_pack("fqc", MXC, fq0=128, fq1=128, fq2=128, fq3=128)
_pack("fsc", U8, fs0=128, fs1=128, fs2=128, fs3=128)
_sb(MXC, zq0=512, zq1=512, zq2=512)
_sb(U8, zs0=512, zs1=512, zs2=512)
_sb(F32, YC=640)
_sb(F32, W07=320, GB=320, RM=320, K8=320, GO=48)
_sb(BF, CB3=512)
_sb(MXC, bq3=128)
_sb(U8, bs3=128)
_sb(MXC, uq=128, ur=640, vq=128, bq=128, wq=512, mq1=320, mq2=320, mq3=320)
_sb(U8, us=128, urs=640, vs=128, bs=128, wsc=512, ms1=320, ms2=320, ms3=320)
_pack("dqm", MXC, dq=128, mq0=320)
_pack("dsm", U8, dsc=128, ms0=320)
_sb(MXC, aq0=128, aq1=128, aq2=128, lq0=128, lq1=128, lq2=128)
_sb(U8, as0=128, as1=128, as2=128, ls0=128, ls1=128, ls2=128)
_pack("eqc", MXC, eq0=128, eq1=128, eq2=128, eq3=128)
_pack("esc", U8, es0=128, es1=128, es2=128, es3=128)
_sb(F32, IOTA=4096, LOWC=640)
_sb(BF, MASK=256, KEEP=256, KP=128, G2=320, G3=320)
_pack("KC", F32, PCF=32, CE=32, CIDX=20, ULF=40, NF=8, TF=8, T2=8, T3=8, REVF=32)
_sb(I32, PCI=8, LBI=20, NBI=160, PI=32, PL=32)
_pack("KU16", U16, ULU=40, LS=3, LB=20, NBL=160, LI=8, LJ=8, LE=2, REV=32)
_sb(F32, ST=960, NB8=2576, KT=960, YO=320, SN=320)
_pack("HB", F32, NS=16, R=80, SD=32, SE0=32, NZ=16, BL=16, DE=96, DO=96, DL=48, D0E=96, D0O=96, D0L=48, OUT0=96, OUT1=96, OUT2=96, OUT3=144,
      Z1=16, KK0=16, KK1=16, KK2=16, KK3=16, PR=16, NV=16, SYV=16, SG1=16, KY=16, NE=16, S6=16, A7=16, NBF=160, NBC=160, BC=16, BI=20,
      GS=256, SS=256, GK0=128, SK0=128, GK1=128, SK1=128, B0=16, GI=512, SI=512, AB=64, AT=64, UF=32)
_pack("OB", F32, NN=128, KEEP8=128, KS=128, N5=112, KEEP5=112, K5=112, N3=128, K3=128, KD=256, KR=32, NK=4, PS=8, PP=32, PT=32, TA=96,
      PF=32, T1=32, TM=32, SELF=32, VT_=32, E4=32, E8=16, ES=32, KEEP4=32, FCF=32, PP_=32, LZD=32, OF=32, OT=32, XD=80, XS=80)
_sb(F32, RK=512, DP=512, VA=80)
_sb(BF, ENT=128, SRT=512, G8=128, S8=128, FW=1024, FWP=512)
_sb(U16, ao0=32, ao1=32, ao2=32, po0=32, po1=32, po2=32)
_sb(U16, al0=32, al1=32, al2=32, pa0=32, pa1=32, pa2=32)
_sb(BF, LA=10240, LBW=10240, TL=1280, SELX=512, LAI=640, LBI0=160)
_pack("SGN", BF, SG0=512, SG1B=512, SG2=512, CMP=512, CNT=512, KEEPH=512)
_sb(BF, FM=512, SCN=512, PB_=256, EQ=256, EQS=272)
_pack("HI", I32, FCI=32, FA=32)
_pack("HU", U16, OFFI=32, KU=16, BKU=8, BK2=8, BIU=20, AL=96, KL=32, PQ=8, SEL=32, VL=32, EL2=8, OFF=32, EL=20)
for _t in range(8):
    SCRATCH["ps%d" % _t] = ("psum", [128, 512], F32)

SEMAPHORES = ["sv", "st", "ss", "sg", "dx0", "dx1", "du", "dv", "dw", "dp0", "dp1", "dp2", "dl0", "dl1", "dn", "rsend", "dad", "dy1", "doc", "dy"]
for _t in range(3):
    SEMAPHORES += ["rq%d" % _t, "rl%d" % _t, "ra%d" % _t, "dla%d" % _t, "dlb%d" % _t]

WAKE, LOCAL, REMOTE, FIRST, CYC = 220.0, 1800.0, 2400.0, 2000.0, 0.87
PASSES, SLIP, SEED = 4000, 20.0, 1
SLACK = 0.001
CASES = ((220.0, 1.0, 0.0, 0.0, 0.0, 0.0), (160.0, 0.95, -0.25, -0.7, -500.0, 0.0), (220.0, 1.25, 0.4, 0.5, 1000.0, 600.0))
PER_ROUND = ("mq", "ms", "aq", "as", "lq", "ls", "al", "pa", "ao", "po", "zq", "zs")
E0_ = 12000.0
E4_ = 2000.0
E6_ = 2000.0
E5_ = 1000.0
E1_, E2_, E3_ = 12000.0, 500.0, 6000.0
SP, VP, VS = 16, 16, 16
ORDER = []


def rank_program(g, core, T, topo):
    rank = T.rank_of(core)
    if rank is None:
        return
    A, ACT = AluOpType, ActivationFunctionType
    add, sub, mul, mx_, mn_, eq, ne, gt, lt, ge, le = A.add, A.subtract, A.mult, A.max, A.min, A.is_equal, A.not_equal, A.is_gt, A.is_lt, A.is_ge, A.is_le
    bw, shr = A.bitwise_and, A.arith_shift_right
    queue = {"v": g.vector, "t": g.tensor, "s": g.scalar, "y": g.sync, "g": g}
    own = {"v": "sv", "t": "st", "s": "ss", "g": "sg"}

    def W(name, a, b, st=1, p0=0, p1=128, ps=1):
        buf, at, _n = PART.get(name, (name, 0, 0))
        return (buf, a + at, b + at, st, p0, p1, ps)

    def N(v):
        return W(v, 0, PART[v][2]) if isinstance(v, str) else v

    def Q(v, q, n=1):
        return N(v)[:4] + (32 * q, 32 * (q + n), 1)

    def I(win, off):
        return ("I", N(win), N(off))

    def ap(v):
        v = N(v)
        if v[0] == "I":
            return ap(v[1]).indirect(ap(v[2]))
        n, a, b, st, p0, p1, ps = v
        rows = slice(p0, p1, ps) if ps != 1 else slice(p0, p1)
        cs = slice(a, b, st) if st != 1 else slice(a, b)
        return T[n][rows, cs]

    def meet(a, b, s, c, d, u):
        if b <= c or d <= a:
            return False
        return not (s == u and s > 1 and (a - c) % s)

    def overlap(x, y):
        return meet(x[1], x[2], x[3], y[1], y[2], y[3]) and meet(x[4], x[5], x[6], y[4], y[5], y[6])

    def covers(x, y):
        return (x[3] == 1 or x[1:4] == y[1:4]) and x[6] == 1 and x[1] <= y[1] and x[2] >= y[2] and x[4] <= y[4] and x[5] >= y[5]

    def clash(v, w, q, h):
        bank = v[0].startswith("ps")
        return (w or h["w"] or (bank and h["q"] != q)) and (bank or overlap(v, h["v"]))

    nodes = []

    def width(v):
        v = N(v)
        return 16 * width(v[2]) if v[0] == "I" else len(range(v[1], v[2], v[3]))

    def cost(out, ins, per=1.0):
        sides = [N(v) for v in [out] + ins]
        if sides[0][0] == "I":
            return 50 + 2.5 * width(out)
        if any(v[0] == "I" for v in sides):
            return 55 + 1.25 * width(out)
        if all(SCRATCH[v[0]][2] in (BF, U16) for v in sides):
            per *= 0.5
        return CYC * max(64.0, per * width(ins[0] if ins else out))

    def node(q, call, reads, writes, busy, kind="op", after=0.0, **more):
        rd, wr = [], []
        for v in map(N, reads):
            rd += [v[1], v[2]] if v[0] == "I" else [v]
        for v in map(N, writes):
            wr.append(v[1] if v[0] == "I" else v)
            rd += [v[2]] if v[0] == "I" else []
        more["gathers"] = sum(width(v) for v in reads if N(v)[0] == "I")
        more["scatters"] = sum(width(v) for v in writes if N(v)[0] == "I")
        nodes.append(dict(q=q, call=call, rd=rd, wr=wr, busy=busy, kind=kind, after=after, **more))

    def cp(out, a):
        node("v", lambda: g.vector.tensor_copy(ap(out), ap(a)), [a], [out], cost(out, [a]))

    def tt(out, a, b, o):
        per = 1.0 if N(a)[0].startswith("ps") else 2.0
        node("v", lambda: g.vector.tensor_tensor(ap(out), ap(a), ap(b), o), [a, b], [out], cost(out, [a, b], per))

    def ts(out, a, s1, o0, s2=None, o1=None):
        x1, x2 = [ap(s) if isinstance(s, tuple) else s for s in (s1, s2)]
        more = () if o1 is None else (o1,)
        node("v", lambda: g.vector.tensor_scalar(ap(out), ap(a), x1, x2, o0, *more), [a] + [s for s in (s1, s2) if isinstance(s, tuple)], [out], cost(out, [a]))

    def scan(out, d0, d1, o0=mul, o1=add, first=0.0):
        node("v", lambda: g.vector.tensor_tensor_scan(ap(out), ap(d0), ap(d1), first, o0, o1), [d0, d1], [out], cost(out, [d0, d1]))

    def fill(out, c):
        out = N(out)
        if cost(out, []) > WAKE - SLIP:
            mid = out[1] + (out[2] - out[1]) // 2
            fill(out[:2] + (mid,) + out[3:], c)
            fill(out[:1] + (mid,) + out[2:], c)
            return
        node("v", lambda: g.vector.memset(ap(out), c), [], [out], cost(out, []))

    def tr(out, a):
        node("v", lambda: g.vector.transpose(ap(out), ap(a)), [a], [out], cost(out, [a]))

    def quant(q, s, a):
        node("v", lambda: g.vector.quantize_mx(ap(q), ap(s), ap(a)), [a], [q, s], 12 + 0.26 * width(a))

    def act(out, a, scale=1.0, bias=None, func=None, acc=None):
        more = {} if scale == 1.0 else {"scale": ap(scale) if isinstance(scale, tuple) else scale}
        if bias is not None:
            more["bias"] = ap(bias) if isinstance(bias, tuple) else bias
        if acc is not None:
            more["accum_out"] = ap(acc)
        f = func or (ACT.Copy if bias is None else ACT.Identity)
        busy = cost(out, [a]) + 10 if N(a)[0] == "I" else CYC * max(64.0, width(a))
        node("s", lambda: g.scalar.activation(ap(out), ap(a), f, **more), [a] + [x for x in (bias, scale) if isinstance(x, tuple)], [out] + ([acc] if acc else []), busy + (20 if acc else 5))

    def iota(out, pattern, base, mult):
        more = {} if SCRATCH[N(out)[0]][2] == I32 else {"allow_small_or_imprecise_dtypes": True}
        node("g", lambda: g.iota(ap(out), pattern, base, mult, **more), [], [out], 130 + 1.75 * width(out))

    def select(out, a, pattern, base, mult):
        node("g", lambda: g.affine_select(ap(out), ap(a), pattern, eq, 0.0, base, mult), [a], [out], 170 + 1.75 * width(out))

    def mm(bank, lq, ls, rq, rs, start=True, stop=True):
        o = W("ps%d" % bank, 0, width(rq))
        node("t", lambda: g.tensor.matmul_mx(ap(o), ap(lq), ap(ls), ap(rq), ap(rs), start, stop), [lq, ls, rq, rs], [o], 30 + 0.63 * (width(rq) + 16), chain=not start)

    def pick_codes(q, s, from_q, from_s, by):
        node("v", lambda: g.vector.tensor_copy(ap(q).bitcast(dt.uint32), ap(from_q).bitcast(dt.uint32).indirect(ap(by))), [I(from_q, by)], [q], 55 + 20.0 * width(by))
        act(s, I(from_s, by))

    def dmas(q, sem, items, more=0.0):
        def side(v):
            if isinstance(v, tuple) and v[0] == "C":
                return ap(v[1]).bitcast(dt.uint8), [v[1]]
            return (ap(v), [v]) if isinstance(v, (tuple, str)) else (v, [])
        sides = [(side(o), side(a)) for o, a in items]

        def call():
            for (o, _w), (a, _r) in sides:
                queue[q].dma_start(o, a).then_inc(T.sem[sem], 16)
        node(q, call, [v for _o, a in sides for v in a[1]], [v for o, _a in sides for v in o[1]], 60.0 * len(items), "dma", LOCAL + more, sem=sem, total=16 * len(items))

    nxt, prv = T.cores[(rank + 1) % len(T.cores)], T.cores[(rank - 1) % len(T.cores)]
    a_nxt, m_nxt = topo.addr(nxt), topo.mask(core, nxt)
    e_out, e_in = len(topo.engines(core, nxt)), len(topo.engines(prv, core))
    sends = []

    def send(sem, items):
        def call():
            for out, src, code in items:
                o, i = ap(out), ap(src)
                if code:
                    o, i = o.bitcast(dt.uint8), i.bitcast(dt.uint8)
                g.remote_dma(o, i, T.sem[sem], T.sem["rsend"], a_nxt[1], a_nxt[0], m_nxt)
        node("g", call, [src for _o, src, _c in items], [out for out, _s, _c in items], 400.0 * len(items) + (0.0 if sends else FIRST), "send",
             REMOTE + 600.0 * (len(items) - 1), sem=sem, total=e_in * len(items), left=e_out * len(items))
        sends.append(sem)

    dmas("s", "du", [("UT", T.u[:, :])], 500.0)
    for k in range(2):
        dmas("ys"[k], "dx%d" % k, [(W("XT", 640 * k, 640 * k + 640), T.x[:, 640 * k:640 * k + 640])], 600.0)
    for y in range(2):
        dmas("y", "dl%d" % y, [(W("LBI", 0, 20, 1, 8 * y + t, 128, 16), T.nb[16 * t + y:16 * t + 16:2, :]) for t in range(8)])
    dmas("y", "dn", [(W("NBI", 0, 160, 1, 16 * k, 16 * k + 16), T.nb[:, :]) for k in range(4)])
    for e in range(2):
        dmas("y", "dp%d" % e, [(W("PI", 16 * par, 16 * par + 16, 1, 32 * a + 16 * e, 32 * a + 16 * e + 16),
                                    T.p[32 * a + 16 * par:32 * a + 16 * par + 16, 16 - 16 * e:32 - 16 * e]) for a in range(4) for par in range(2)])
    dmas("y", "dp2", [("PL", T.p[:, :])])
    dmas("y", "dw", [(("C", "wq"), T.wc[:, :]), ("wsc", T.ws[:, :])])
    dmas("y", "dv", [("VT", T.v[:, :])])

    pc, pf = (lambda i: W("PCI", i, i + 1)), (lambda i: W("PCF", i, i + 1))
    iota(pc(0), [[0, 1]], 0, 1)
    ts(pc(1), pc(0), 15, bw)
    ts(pc(2), pc(0), 3, shr, 1, bw)
    ts(pc(3), pc(0), 4, shr, 1, bw)
    ts(pc(4), pc(0), 7, bw)
    cp(W("PCF", 0, 5), W("PCI", 0, 5))
    cq, ch, ce, c7 = pf(1), pf(2), pf(3), pf(4)
    iota(W("ULF", 0, 8), [[0, 8]], 112, 0)
    iota(W("ULF", 8, 24), [[16, 2], [32, 4], [0, 2]], 0, 0)
    ts(W("ULU", 0, 8), W("ULF", 0, 8), ch, mul)
    iota(W("ULF", 24, 32), [[-112, 2], [0, 4]], 112, 0)
    iota(W("ULF", 32, 40), [[16, 8]], 0, 0)
    cp(W("ULU", 8, 40), W("ULF", 8, 40))
    quant("uq", "us", "UT")
    for a, b in ((0, 1), (1, 3), (3, 5)):
        pick_codes(W("ur", 128 * a, 128 * b), W("urs", 128 * a, 128 * b), "uq", "us", W("ULU", 8 * a, 8 * b))
    for k in range(2):
        quant(W("mq0", 160 * k, 160 * k + 160), W("ms0", 160 * k, 160 * k + 160), W("XT", 640 * k, 640 * k + 640))
    ZERO = 2048
    iota(W("IOTA", ZERO, ZERO + 320), [[1, 320]], 0, 0)
    for k in list(range(ZERO + 320, 4096, 320)) + [ZERO - 320]:
        b = min(k + 320, 4096)
        act(W("IOTA", k, b), W("IOTA", ZERO, ZERO + b - k), bias=float(k - ZERO))
    iota(W("IOTA", 0, ZERO - 320), [[1, ZERO - 320]], -ZERO, 0)
    CELLS, CELLM = W("IOTA", ZERO, ZERO + 320), W("IOTA", ZERO - MID, ZERO - MID + 320)
    fill("BY", 0.0)
    for k in (0, 1, 6, 7):
        fill(W("BY", k, 128, 8), 2.0)
    for e in range(2):
        select(W("CB", 384 * e, 384 * e + 128), "BY", [[0, 2], [-16, 8], [0, 8]], -8 * e, 1)
        cp(W("CB", 128 + 128 * e, 256 + 128 * e), W("CB", 384 * e, 384 * e + 128))
    quant("bq", "bs", "CB")
    act(W("CB3", 0, 512, 2), W("CB", 0, 512, 2))
    act(W("CB3", 1, 512, 2), W("CB", 1, 512, 2), 1280.0)
    quant("bq3", "bs3", "CB3")
    iota(W("NB8", 2560, 2576), [[0, 16]], 0, 0)
    iota("NBC", [[1, 8], [16, 20]], -320, 0)
    ts(pc(5), pc(0), 1, bw)
    ts(pc(6), pc(0), 1, shr, 7, bw)
    ts(pc(7), pc(0), 4, shr)
    cp(W("PCF", 28, 31), W("PCI", 5, 8))
    ts(pf(29), pf(29), 16.0, mul, pf(28), add)
    ts(pf(30), pf(30), 2.0, mul, pf(29), add)
    ts("LS", W("IOTA", ZERO, ZERO + 320, 128), pf(30), add, 319.0, mn_)
    fill(W("DT", 320, 512), 0.0)
    fill("K8", 0.0)
    fill(W("K8", 0, 320, 8), -FAR)
    cp("LB", "LBI")
    act(pf(9), pf(28), 8.0)
    tt(Q("NBF", 0, 2), Q("NBI", 0, 2), Q("NBC", 0, 2), sub)
    for k in range(2):
        ts(Q("NBL", 2 * k, 2), Q("NBF", 0, 2), Q(pf(9), 0, 2), sub)
    for k in range(8):
        (act if k < 5 else cp)(W("NB8", 320 * k, 320 * k + 320), I(W("IOTA", ZERO - 320, ZERO + 320), W("NBL", 20 * k, 20 * k + 20)))
        nodes[-1]["early"] = E5_
    ts(pf(5), c7, 320.0, mul, ch, add)
    ts("CIDX", W("IOTA", ZERO, ZERO + 320, 16), pf(5), add)
    iota(W("KT", 320, 640), [[0, 320]], 0, 0)
    iota(W("FM", 0, 256), [[0, 16], [1, 16]], 0, 0)
    ts("MASK", W("FM", 0, 256), cq, eq)
    fill("KEEP", 1.0)
    fill(W("KEEP", 0, 256, 16), 0.0)
    iota(W("ST", 640, 960), [[0, 320]], 0, 0)
    for k in ("DE", "DO", "DL", "D0E", "D0O", "D0L"):
        fill(k, 0.0)
    for k in ("D0E", "D0O"):
        fill(W(k, 2, 96, 6), -1.0)
        fill(W(k, 5, 96, 6), 1.0)
    ts(W("R", 0, 32), "PI", 0.0, add)
    fill("BK2", 0)
    fill("ON4", 0.25)
    fill("ON", 0.5)
    for n in nodes[-2:]:
        n["early"] = E0_
    for b in range(4):
        select("CT%d" % b, "ON", [[1, 512]], -b, -4)
        quant("eq%d" % b, "es%d" % b, "CT%d" % b)
        nodes[-1]["early"] = E1_
    mark = len(nodes)
    act(pf(6), cq, 1.0 / 512, -ZERO / 512 - 0.5)
    act(pf(6), ce, -0.5, pf(6))
    act(Q(W("N5", 0, 112, 7), 0), Q(W("IOTA", ZERO, ZERO + 256, 16), 0), 1.0 / 512, Q(pf(6), 0))
    for name, k in (("KEEP8", 4), ("KEEP5", 7), ("K3", 8), ("KEEP4", 4), ("KP", 16)):
        iota(name, [[0, width(name)]], 1, 0)
        iota(W(name, 0, width(name), k), [[0, width(name) // k]], 0, 0)
    iota(W("K3", 2, 128, 8), [[0, 16]], -1, 0)
    iota(W("KP", 1, 128, 17), [[0, 8]], 0, 0)
    iota("KEEPH", [[0, 512]], 1, 0)
    iota(W("KEEPH", 0, 512, 256), [[0, 2]], 0, 0)
    act("CE", W("IOTA", ZERO + 128, ZERO + 640, 16), bias=cq)
    ts(pc(7), pc(0), 5, shr)
    ts(pf(15), pc(7), 128.0, mul)
    act("ENT", W("IOTA", ZERO - 256, ZERO - 128), bias=pf(15))
    iota("SRT", [[0, 512]], 0, 0)
    RHO = W("IOTA", ZERO + 1, ZERO + 9)
    act(pf(13), cq, 16.0)
    act(pf(31), cq, 16.0, 15.0)
    act("T2", RHO, -2.0, 16.0)
    ts("NF", RHO, cq, le)
    tt("TF", "NF", RHO, mul)
    ts("LI", "TF", -16.0, mul, pf(31), add)
    tt("T3", "NF", "T2", mul)
    tt("T3", "T3", RHO, add)
    ts("LJ", "T3", 16.0, mul, 15.0, add)
    act(pf(7), cq, 17.0, -17.0)
    act(pf(8), cq, -16.0, 255.0)
    for e in range(2):
        ts(pf(9), pf(7), pf(8), mn_, 128.0 * e, add)
        ts(pf(14), cq, 0.0, eq, 273.0 - 128 * e, mul)
        ts(W("LE", e, e + 1), pf(14), pf(9), add)
    iota(W("EQS", 256, 272), [[0, 16]], 0, 0)
    iota("LOWC", [[16, 20], [0, 2], [1, 16]], 0, 0)
    lo = pf(28)
    two, rest = pf(19), pf(16)
    ts(two, cq, 2.0, eq)
    act(rest, two, -1.0, 1.0)
    act(pf(10), two, ce, 0.0)
    act(pf(11), ce, -1.0, 1.0)

    def split(k, out, src, scale, high, low):
        act(pf(k), lo, float(low - high), float(high))
        act(pf(k), pf(k), rest, 0.0)
        for a in range(0, width(out), 128):
            cut = lambda v: (v[0], v[1] + a, min(v[1] + a + 128, v[2])) + v[3:]
            act(cut(out), cut(src), scale, pf(k))
    for m in range(3):
        n_ = min(256, 640 - 256 * m)
        split(20 + m, W("YC", 256 * m, 256 * m + n_), W("IOTA", ZERO, ZERO + n_), lo, 256 * m, 0)
    act(pf(12), lo, pf(11), 0.0)
    for k, (a, b, high, low) in enumerate(((0, 256, 512, 128), (256, 640, 768, -128))):
        act(pf(26 + k), lo, float(low - high), float(high))
        act(pf(26 + k), pf(26 + k), rest, 0.0)
        act(pf(26 + k), pf(26 + k), pf(11), pf(10))
        for c in range(a, b, 128):
            act(W("LAI", c, c + 128), W("LOWC", c, c + 128), pf(12), pf(26 + k))
    act("LBI0", W("IOTA", ZERO, ZERO + 160), 0.0, two)
    for b in range(4):
        select("CU%d" % b, "ON4", [[1, 512]], -b, -4)
        quant("fq%d" % b, "fs%d" % b, "CU%d" % b)
    iota("REVF", [[-256, 2], [1, 16]], 256, 0)
    ts("REV", "REVF", pf(13), add)
    for n in nodes[mark:]:
        n["early"] = E2_
    quant("vq", "vs", "VT")

    MASK, KEEP = (lambda n: W("MASK", 0, n)), (lambda n: W("KEEP", 0, n))
    run = lambda name, k: W(name, k, 96, 6)
    slot = lambda name, k: W(name, k + 1, 48, 3)
    key = lambda k, name="N3": W(name, k, 128, 8)
    links = lambda k, name="N5": W(name, k, 112, 7)
    ends = lambda name, n=256: W(name, 15, n, 16)
    SE, SO = W("SI", 0, 512, 32), W("SI", 16, 512, 32)
    E, O, S30, DC = W("R", 0, 16), W("R", 16, 32), W("SD", 16, 32), W("SD", 0, 16)

    def lookup(g_, s_, win, off):
        tt(g_, I(win, off), MASK(16 * width(off)), mul)
        scan(s_, KEEP(16 * width(off)), g_)

    def shift(out, a, up):
        for q in range(3):
            act(Q(out, q + 1 if up else q), Q(a, q if up else q + 1))

    def eight(v, k):
        n, a, _b, st = N(v)[:4]
        return (n, a + 8 * k * st, a + (8 * k + 7) * st + 1, st, 0, 128, 1)

    def halfstep(h):
        even = h % 2 == 0
        kk, out, d0, d1 = "KK%d" % h, "OUT%d" % h, ("D0E", "D0O", "D0E", "D0L")[h], ("DE", "DO", "DE", "DL")[h]
        S = SE if even else SO
        if h == 0:
            y, n, s3, o, dc = E, O, S30, "NS", DC
        else:
            before = "OUT%d" % (h - 1)
            y, n, s3, o, dc = run(("DE", "DO", "DE")[h - 1], 2), run(before, 1), run(before, 2), run(before, 4), run(before, 5)
            tt(kk, o, s3, sub)
            if h == 1:
                act(Q(eight("KY", 1), 1), Q(eight(kk, 1), 0))
                act(Q(eight("KY", 0), 1), Q(eight(s3, 1), 0))
                for k in range(2):
                    tt(Q(eight(kk, k), 0), Q(ends("SK0", 128), k), Q(eight("KY" if k else kk, k), k), add)
                    act(Q(eight("BC", k), 0), Q(ends("SK0", 128), k))
                for k in range(2):
                    tt(Q(eight(s3, k), 0), Q(eight("KY" if k else s3, 0), k), Q(ends("SK0", 128), k), sub)
                tt(Q(n, 0), Q(n, 0), Q("BC", 0), add)
                ts(Q(links(1), 0), Q("BC", 0), 0.0, ne, -1.0, mul)
            cp("KU", kk)
        parts = 2 if h == 0 else 1
        for k in range(parts):
            w = 16 // parts
            lookup(W("GS", 16 * w * k, 16 * w * (k + 1)), W("SS", 16 * w * k, 16 * w * (k + 1)), W("ST", 0, 640) if even else W("ST", 320, 960), W("KU", w * k, w * (k + 1)))
        sl = run if h < 3 else slot
        tt("PR", dc, s3, mul)
        act(Q("NV", 0, 4 if h < 3 else 3), Q("PR", 0, 4 if h < 3 else 3), 1e24, func=ACT.Abs)
        if h == 3:
            ts(Q("NV", 3), Q(s3, 3), 0.0, eq, -BIG, mul)
            act(Q(sl(d0, 0), 3), Q("NV", 3), -1.0 / BIG)
        tt("SYV", S, "NV", add)
        tt(sl(d1, 0), kk, y, sub)
        for q, k in (((0, 4),), ((0, 3),), ((1, 1), (2, 2)), ((0, 4),))[h]:
            act(Q(sl(d1, 1), q, k), Q(y, q, k))
        end = 3 if even else 0
        now = 3 - end
        if h < 3:
            act(sl(d1, 2), n)
            act(run(d1, 5), n, -1.0)
            shift(run(d1, 3), run(d1, 0), not even)
            shift(run(d1, 4), y, not even)
            act(Q(run(d1, 4), end), Q(n, end))
        if h in (1, 2):
            ts(Q("Z1", now), Q(s3, now), 0.0, eq)
            tt(Q("BC", now), Q("B0", now), Q("Z1", now), mul)
            tt(Q(sl(d1, 1), now), Q("BC", now), Q(y, now), add)
            ts(Q(links(2) if h < 2 else key(6), 0), Q("BC", now), 0.0, ne, -1.0, mul)
            for q in range(4):
                far = 0.0 if q // 2 == end // 2 else 640.0
                act(Q(W("A7", 0, 8), q), Q(eight(n, q % 2), end), bias=far)
            cp("BKU", W("A7", 0, 8))
            lookup("GK1", "SK1", "KT", "BKU")
            for q in range(4):
                to = (SE if end == 0 else SO) if q // 2 != end // 2 else "B0" if h == 1 else slot("DL", -1)
                act(Q(eight(to, q % 2), end), Q(ends("SK1", 128), q))
        if h == 3:
            act(W("R", 48, 64), n)
            act(Q(W("R", 64, 80), 0, 3), Q(o, 0, 3))
            act(Q(W("R", 64, 80), 3), Q(n, 3))
            act(W("OUT3", 2, 48, 3), n)
        if h == 2:
            scan(Q("K5", 0), Q("KEEP5", 0), Q("N5", 0))
            act(Q(key(5), 0), Q(links(6, "K5"), 0))
            ts(Q("NE", 0), Q(s3, 3), 0.0, eq, -1.0, mul)
            act(Q(key(1, "K3"), 0), Q("NE", 0), 2.0, 1.0)
            for k in range(2):
                ts(Q("BK2", k), Q(eight(kk, k), 3), 319.0, mn_)
            lookup("GK0", "SK0", W("KT", 640, 960), "BK2")
            for k in range(2):
                ts(Q(eight(key(0), k), 0), Q(ends("SK1", 128), 2 + k), 0.0, ne)
                tt(Q(eight(key(2), k), 0), Q(ends("SK0", 128), k), Q(ends("SK1", 128), k), gt)
                tt(Q(key(1 + 2 * k), 0), Q("S6", 3), Q(SO, 3), gt)
            tt(Q(key(4), 0), Q(key(0), 0), Q("NE", 0), mul)
            tt(Q(key(3, "K3"), 0), Q(ends("SS"), 3), Q("SYV", 3), gt)
            tt(Q(key(7), 0), Q(ends("SS"), 0), Q("SYV", 0), gt)
        if h == 1:
            act(Q("S6", 3), Q(ends("SS"), 3))
        tt(sl(d0, 1), ends("SS"), "SYV", gt)
        if h < 3:
            for q in range(3):
                a, b = (q + 1, q) if even else (q, q + 1)
                tt(Q(run(d0, 4), b), Q(ends("SS"), a), Q("SYV", a), gt)
        if h < 2:
            act(Q(links(3 + h), 0), Q(run(d0, 1), now))
            tt("SG1", ends("SS"), "NV", sub)
            tt(S, S, "SG1", mx_)
        scan(out if h < 3 else W(out, 48, 96), d0, d1)
        if h == 3:
            act(W(out, 98, 144, 3), W(out, 50, 96, 3))

    for rd in range(ROUNDS):
        mq, ms, fw, al, pa = "mq%d" % rd, "ms%d" % rd, W("FW", 384, 1024), "ao%d" % rd, "po%d" % rd
        if rd == 0:
            for e in range(2):
                cp(W("OFFI", e, 32, 2), W("PL", 16 - 16 * e, 32 - 16 * e))
        act(Q("NS", 0), Q(E, 0))
        nodes[-1]["first"] = True
        shift("NS", O, True)
        tt("SD", W("NS", 0, 32), W("R", 0, 32), sub)
        tt("KK0", "NS", S30, sub)
        ts("SE0", "SD", 0.0, eq)
        for q in range(4):
            act(Q(W("NN", q, 128, 4), 0), Q("SE0", q))
        scan(Q("KS", 0), Q("KEEP8", 0), Q("NN", 0))
        for j in range(2):
            act(Q(links(5 + j), 0), Q(W("KS", 64 * j + 3, 64 * j + 64, 4), 0))
        cp("KU", "KK0")
        ts(Q("NZ", 0), Q(S30, 0), 0.0, ne, 320.0, mul)
        tt(Q("BL", 0), Q("NZ", 0), Q(E, 0), add)
        for k in range(2):
            act(Q(W("A7", 8, 16), k), Q(eight("BL", k), 0))
            act(Q(W("A7", 8, 16), 2 + k), Q(eight(O, k), 3))
        cp("BKU", W("A7", 8, 16))
        for k in range(2):
            mm(3 * k, W("ur", 0, 128), W("urs", 0, 128), W(mq, 160 * k, 160 * k + 160), W(ms, 160 * k, 160 * k + 160))
            (cp if k else act)(W("W07", 160 * k, 160 * k + 160), W("ps%d" % (3 * k), 0, 160))
        for k in (1, 2):
            mm(k, W("ur", 128 * k, 128 * k + 128), W("urs", 128 * k, 128 * k + 128), mq, ms)
        act(W("ST", 0, 320), W("ps1", 0, 320))
        act(W("ST", 320, 640), W("ps2", 0, 320))
        mm(0, W("ur", 384, 512), W("urs", 384, 512), mq, ms)
        act(W("KT", 640, 960), W("ps0", 0, 320))
        cp("GO", I("W07", "LS"))
        cp(W("GB", 0, 160), I("W07", W("LB", 0, 10)))
        act(W("GB", 160, 320), I("W07", W("LB", 10, 20)))
        scan("RM", "K8", "GB", add, mx_)
        for t in range(7):
            at = 80 * (t // 2) + t % 2
            tt(W("DT", at, at + 79, 2), W("RM", t, 320, 8), W("RM", 7, 320, 8), ne)
        tt(W("DT", 241, 320, 2), W("GO", 0, 40), W("RM", 7, 320, 8), ge)
        quant(W("dq", 0, 128), W("dsc", 0, 128), "DT")
        for k in range(4):
            mm(3, *(("bq", "bs") if k < 3 else ("bq3", "bs3")), W("dq", 20 * k, 20 * k + 128), W("dsc", 20 * k, 20 * k + 128), k == 0, k == 3)
        tt("BI", W("ps3", 0, 20), "CIDX", add)
        ts("BIU", "BI", 2560.0, mn_)
        cp(W("KT", 0, 160), I("NB8", W("BIU", 0, 10)))
        act(W("KT", 160, 320), I("NB8", W("BIU", 10, 20)))
        lookup("GK0", "SK0", W("KT", 0, 640), "BKU")
        for k in range(2):
            act(Q(eight("B0", k), 3), Q(ends("SK0", 128), 2 + k))
        mm(5, W("ur", 512, 640), W("urs", 512, 640), mq, ms)
        act("SN", W("ps5", 0, 320))
        for k in range(2):
            act(W("GI", 256 * k, 256 * k + 256), I("SN", W("OFFI", 16 * k, 16 * k + 16)))
            tr(W("SI", 256 * k, 256 * k + 256), W("GI", 256 * k, 256 * k + 256))
        for t in range(4):
            f = W("ps%d" % (4 + t), 0, 320)
            mm(4 + t, "eq%d" % t, "es%d" % t, mq, ms)
            act(W("YW%d" % t, 640, 960), f)
            if t < 2:
                act("FH%d" % t, f)
        dmas("y", "dla%d" % rd, [(W("LA", 0, 640), "LAI")])
        dmas("y", "dlb%d" % rd, [(W("LBW", a, a + 160), "LBI0") for a in range(0, 640, 160)])
        for h in range(4):
            halfstep(h)
        for k, src in enumerate((W("OUT3", 2, 96, 3), W("OUT3", 50, 144, 3), W("R", 48, 80))):
            tr(W("TA", 32 * k, 32 * k + 32), src)
            cp(W("AL", 32 * k, 32 * k + 32) if k else al, W("TA", 32 * k, 32 * k + 32))
            nodes[-1]["early"] = (E4_, 0.0, E3_)[k]
        send("ra%d" % rd, [("al%d" % rd, al, False)])
        for k in range(2):
            scan(Q(W("KD", 128 * k, 128 * k + 128), 0), Q("K3", 0), Q("N3", 0))
        tr(Q("KR", 0), Q(W("KD", 7, 256, 8), 0))
        for q in range(4):
            ts(Q("KL", q), Q("KR", 0), 512.0, mul, float(ZERO), add)
            act(Q("NK", q), Q(W("KD", 32 * q + 7, 32 * q + 32, 8), 0), 512.0)
        cp(W("RK", 0, 256), I("IOTA", W("KL", 0, 16)))
        act(W("RK", 256, 512), I("IOTA", W("KL", 16, 32)))
        for b in range(3):
            act(("SG0", "SG1B", "SG2")[b], "RK", -1.0, W("NK", b, b + 1), ACT.Sign, W("PS", b, b + 1))
        ts("CMP", "RK", W("NK", 3, 4), lt, 2.0, mul)
        scan("CNT", "KEEPH", "CMP")
        ts(W("PS", 3, 4), W("CNT", 255, 256), W("CNT", 511, 512), add, -511.0, add)
        for q in range(4):
            ts(Q(W("PP", 4 * q, 4 * q + 4), 0), Q(W("PS", 0, 4), q), -0.5, mul, 255.5, add)
            act(Q(W("PP", 16 + 4 * q, 20 + 4 * q), 0), Q(W("PS", 0, 4), q), -0.5, 255.5)
        tr(Q("PT", 0), Q("PP", 0))
        for q in range(4):
            cp(Q(pa, q), Q("PT", 0))
        send("rl%d" % rd, [("pa%d" % rd, pa, False)])
        nodes[-1]["early"] = E6_
        for q in range(4):
            cp(Q("PQ", q), Q(W("PT", 8 * q, 8 * q + 8), 0))
        act(W("SRT", 384, 512), "ENT", 0.0)
        cp(I("SRT", "PQ"), "ENT")
        cp(W("FWP", 0, 256), I(CELLM, W("al%d" % rd, 0, 16)))
        act(W("FWP", 256, 512), I(CELLM, W("al%d" % rd, 16, 32)))
        cp(I(W("FW", 0, 512), "pa%d" % rd), "FWP")
        act(W("FW", 512, 1024), I(CELLM, al))
        zq, zs = "zq%d" % rd, "zs%d" % rd
        for k in range(0, 32, VP):
            pick_codes(W(zq, 16 * k, 16 * (k + VP)), W(zs, 16 * k, 16 * (k + VP)), mq, ms, W("AL", 32 + k, 32 + k + VP))
        for t in range(4):
            for k in range(0, 32, SP):
                act(W("ZG%d" % t, 16 * k, 16 * (k + SP)), I(W("YW%d" % t, 640, 960), W("AL", 64 + k, 64 + k + SP)), 0.5)
            mm(t, "fq%d" % t, "fs%d" % t, zq, zs)
            for k in range(0, 32, VS):
                tt(W("YW%d" % t, 128 + 16 * k, 128 + 16 * (k + VS)), W("ps%d" % t, 16 * k, 16 * (k + VS)), W("ZG%d" % t, 16 * k, 16 * (k + VS)), add)
        tt("G8", W("SRT", 384, 512), MASK(128), mul)
        scan("S8", KEEP(128), "G8")
        for q in range(4):
            act(Q(W("E4", q, 32, 4), 0), Q(ends("S8", 128), q))
        scan(Q("ES", 0), Q("KEEP4", 0), Q("E4", 0))
        for q in range(4):
            ts(Q("EL2", q), Q(W("ES", 3, 32, 4), 0), 256.0, add)
        for t in range(4):
            act(W("HT", t, 512, 4), I(W("YW%d" % t, 128, 640), "EL2"), 2.0)
        aq, asc, lq, ls = "aq%d" % rd, "as%d" % rd, "lq%d" % rd, "ls%d" % rd
        quant(aq, asc, "HT")
        send("rq%d" % rd, [(lq, aq, True), (ls, asc, False)])
        for b in range(4):
            mm(b, W("wq", 128 * b, 128 * b + 128), W("wsc", 128 * b, 128 * b + 128), lq, ls)
            act(W("YW%d" % b, 0, 128), W("ps%d" % b, 0, 128), 2.0 ** -6)
        ts("PF", pa, 384.0, sub)
        ts("T1", pa, 384.0, lt, 1024.0, mul)
        tt("TM", "T1", "PF", mx_)
        tt("SELF", "TM", "CE", mn_)
        cp("SEL", "SELF")
        tr("VT_", "SELF")
        for par in range(2):
            cp(W("VL", par, 32, 2), W("VT_", 16 * par, 16 * par + 16))
        for w in range(2):
            act(W("SELX", 256 * w, 256 * w + 256), I("YC", W("VL", 16 * w, 16 * w + 16)))
        for e in range(2):
            half = lambda name, n: W(name, n * e, n * e + n)
            if e == 0:
                lookup(half("FM", 256), half("SCN", 256), fw, half("SEL", 16))
            else:
                act(W("FWP", 0, 256), I(fw, half("SEL", 16)))
                tt(half("FM", 256), W("FWP", 0, 256), MASK(256), mul)
                scan(half("SCN", 256), KEEP(256), half("FM", 256))
            act(half("PB_", 128), I(half("SCN", 256), "LJ"))
            tt(half("EQ", 128), I(half("SCN", 256), "LI"), half("PB_", 128), eq)
            scan(half("EQS", 128), "KP", half("EQ", 128))
        ts("FCI", ends("SCN", 512), 1.0 / 16, mul, (MID - 7.5) / 16, add)
        act("LZD", ends("SCN", 512), 1.0 / 640, MID / 640)
        ts("T1", "FCI", 16.0 / 640, mul)
        tt("PP_", "T1", "LZD", add)
        tt("OF", I("EQS", "LE"), "PP_", add)
        tr("OT", "OF")
        for par in range(2):
            ts(W("OFF", par, 32, 2), W("OT", 16 * par, 16 * par + 16), 640.0, mul, 16.0 * par + 0.25, add)
        if rd + 1 < ROUNDS:
            act("FCF", ends("SCN", 512), bias=float(MID))
            tr(W("R", 0, 32), "FCF")
            nodes[-1]["rd"].append(N("OFF"))
            for e in range(2):
                for par in range(2):
                    act(W("AB", 32 * e + 16 * par, 32 * e + 16 * par + 16), W("FCF", 16 * e, 16 * e + 16), ce if par else pf(11), 0.0)
            tr("AT", "AB")
            for e in range(2):
                tt(W("UF", e, 32, 2), W("AT", 32 * e, 32 * e + 16), W("AT", 32 * e + 16, 32 * e + 32), add)
            cp("OFFI", "UF")
        else:
            act("RK", I(fw, "SEL"), bias=float(MID))
            act("DP", I("RK", "REV"))
            dmas("y", "dad", [(T.ad[:, :], W("DP", 0, 512, 1, 0, 128, 16))])
        for y in range(7, -1, -1):
            for w in (1, 0):
                k = 8 * w + y
                cp(I("LA" if w else "LBW", W("OFF", 2 * k, 2 * k + 2)), W("SELX", 32 * k, 32 * k + 32))
        for j, win in enumerate(("LA", "LBW")):
            tr(W("TL", 640 * j, 640 * j + 640), W(win, 0, 640))
            row = lambda r: W("TL", 640 * j + r, 640 * j + 640, 16)
            tt(W("VA", j, 80, 2), row(0), row(1), add)
            act(W("XD", j, 80, 2), row(2))
        scan("XS", "XD", "VA")
        cp("EL", W("XS", 3, 80, 4))
        for k in range(2):
            half = lambda name, n: W(name, n * k, n * k + n)
            for t in range(2):
                tt(W("MT", 640 * k + t, 640 * k + 640, 4), I("YW%d" % t, half("EL", 10)), half("FH%d" % t, 160), add)
                act(half("G%d" % (2 + t), 160), I("YW%d" % (2 + t), half("EL", 10)))
                tt(W("MT", 640 * k + 2 + t, 640 * k + 640, 4), half("ps%d" % (6 + t), 160), half("G%d" % (2 + t), 160), add)
            quant(W("mq%d" % (rd + 1), 160 * k, 160 * k + 160), W("ms%d" % (rd + 1), 160 * k, 160 * k + 160), W("MT", 640 * k, 640 * k + 640))

    mq, ms = "mq%d" % ROUNDS, "ms%d" % ROUNDS
    for k in range(2):
        mm(k, "vq", "vs", W(mq, 160 * k, 160 * k + 160), W(ms, 160 * k, 160 * k + 160))
        (cp if k else act)(W("YO", 160 * k, 160 * k + 160), W("ps%d" % k, 0, 160))
        dmas("ys"[1 - k], ("dy", "dy1")[k], [(T.y[:, 160 * k:160 * k + 160], W("YO", 160 * k, 160 * k + 160))])
    dmas("y", "doc", [(T.oc[:, :], ("C", mq))] + [(T.osc[4 * k:4 * k + 4, :], W(ms, 0, 320, 1, 32 * k, 32 * k + 4)) for k in range(4)])

    seen = {}
    for i, n in enumerate(nodes):
        n["pre"], n["post"] = set(), []
        for v, w in [(v, False) for v in n["rd"]] + [(v, True) for v in n["wr"]]:
            if w:
                n.setdefault("src", set(n["pre"]))
            n["pre"].update(h["i"] for h in seen.get(v[0], ()) if clash(v, w, n["q"], h))
        n.setdefault("src", set(n["pre"]))
        for v, w in [(v, False) for v in n["rd"]] + [(v, True) for v in n["wr"]]:
            old = seen.setdefault(v[0], [])
            if w:
                old[:] = [h for h in old if not covers(v, h["v"])]
            old.append({"v": v, "w": w, "q": n["q"], "i": i})
        n["pre"].discard(i)
        for j in n["pre"]:
            nodes[j]["post"].append(i)

    def lay(way):
        left = [len(p) for p in pre]
        ready = sorted((way[i], -i) for i, k in enumerate(left) if k == 0)
        taken, start, done = {q: [] for q in queue}, [0.0] * len(nodes), [0.0] * len(nodes)
        while ready:
            i = -ready.pop()[1]
            at = 0.0
            for k, w in pre[i]:
                if done[k] + w * WAKE > at:
                    at = done[k] + w * WAKE
            line = taken[on[i]]
            k = len(line)
            while k > 0 and line[k - 1][1] > at:
                k -= 1
            while k < len(line) and line[k][0] < at + busy[i] - SLIP:
                if line[k][1] > at:
                    at = line[k][1]
                k += 1
            line.insert(k, (at, at + busy[i]))
            start[i], done[i] = at, at + busy[i] + after[i]
            for j in nodes[i]["post"]:
                left[j] -= 1
                if left[j] == 0:
                    ready.append((way[j], -j))
                    ready.sort()
        return sorted(range(len(nodes)), key=lambda i: (start[i], i))

    def span(order, wake, busy, after):
        last, done = {q: 0.0 for q in queue}, [0.0] * len(order)
        for i in order:
            at = last[on[i]]
            for k, w in pre[i]:
                if done[k] + w * wake > at:
                    at = done[k] + w * wake
            at += busy[i]
            last[on[i]] = at
            done[i] = at + after[i]
        return max(done)

    if not ORDER:
        lag = lambda i, j: 0.0 if nodes[j].get("chain") and nodes[i]["q"] == "t" else 1.0
        beside = lambda i, j: sum(nodes[k]["busy"] for k in nodes[j]["src"] if k > i and nodes[k]["q"] == nodes[i]["q"])
        busy, after, on = [n["busy"] for n in nodes], [n["after"] for n in nodes], [n["q"] for n in nodes]
        cases = [(wake, [(n["busy"] + ga * n["gathers"] + sc * n["scatters"]) * slow if n["kind"] == "op" else n["busy"] + issue * (n["kind"] == "send") for n in nodes],
                  [n["after"] + far * (n["kind"] == "send") for n in nodes]) for wake, slow, ga, sc, far, issue in CASES]
        pre = [[(k, lag(k, i)) for k in sorted(n["pre"])] for i, n in enumerate(nodes)]
        way = [0.0] * len(nodes)
        for i in reversed(range(len(nodes))):
            way[i] = busy[i] + after[i] + nodes[i].get("early", 0.0) + max([lag(i, j) * WAKE + beside(i, j) + way[j] for j in nodes[i]["post"]] or [0.0])
        alike, met = {}, {}
        for i, n in enumerate(nodes):
            if n.get("first"):
                met = {}
            v = (n["wr"] + n["rd"])[0]
            k = (n["q"], v[0][:2] if v[0][:2] in PER_ROUND else v[0]) + v[1:] + (n["rd"][0][1:] if n["rd"] else ())
            met[k] = met.get(k, 0) + 1
            alike.setdefault(k + (met[k],), []).append(i)
        alike = list(alike.values())
        seed = [SEED]

        def pick(n):
            seed[0] = (seed[0] * 1103515245 + 12345) % 2147483648
            return (seed[0] >> 8) % n
        best, now = None, 1e9
        for _pass in range(PASSES):
            trial = list(way)
            for _k in range(1 + pick(3) // 2 if best else 0):
                by = (100.0, 400.0, 1500.0)[pick(3)] * (0.3 + pick(100) / 100.0) * (2 * pick(2) - 1)
                for i in alike[pick(len(alike))]:
                    trial[i] += by
            order = lay(trial)
            worth = sum(span(order, *case) / sum(case[1]) for case in cases)
            if best is None or worth <= best[0]:
                best = (worth, order)
            if worth <= now * (1.0 + SLACK * (1.0 - _pass / PASSES) * pick(100) / 100.0):
                now, way = worth, trial
        ORDER.extend(best[1])
    order = ORDER

    count, know, totals, sent = {k: 0 for k in own}, {k: {} for k in queue}, {}, 0
    for i in order:
        n = nodes[i]
        q = n["q"]
        todo = {}
        for j in n["pre"]:
            m = nodes[j]
            if n.get("chain") and m["q"] == "t":
                continue
            if know[q].get(m["sig"], 0) < m["val"] and todo.get(m["sig"], {"val": 0})["val"] < m["val"]:
                todo[m["sig"]] = m
        for m in sorted(todo.values(), key=lambda m: -m["at"]):
            if know[q].get(m["sig"], 0) < m["val"]:
                queue[q].wait_ge(T.sem[m["sig"]], m["val"])
                for s, x in m["snap"].items():
                    know[q][s] = max(know[q].get(s, 0), x)
                know[q][m["sig"]] = m["val"]
        if n["kind"] == "op":
            count[q] += 1
            n["call"]().then_inc(T.sem[own[q]], 1)
            n["sig"], n["val"], n["snap"] = own[q], count[q], dict(know[q])
        else:
            n["call"]()
            totals[n["sem"]] = n["total"]
            sent += n.get("left", 0)
            n["sig"], n["val"], n["snap"] = n["sem"], n["total"], dict(know[q]) if n["kind"] == "dma" else {}
        n["at"] = len(totals) + sum(count.values())

    g.wait_ge(T.sem["rsend"], sent)
    for q in own:
        g.wait_ge(T.sem[own[q]], count[q])
    for s in sorted(totals):
        g.wait_ge(T.sem[s], totals[s])
